import numpy as np, ml_dtypes
CORES = [242,247,114,119]
N = 4
BF = ml_dtypes.bfloat16
V, HB, KB, S, SB, M, CL, RO = 3072, 10, 1024, 48, 16, 4, 12, 3
def hashes(v, a, t):
    u = np.matmul(a.transpose(0, 1, 3, 2), v)
    return np.add.reduce((u > t[..., None]) * (2 ** np.arange(HB))[:, None], axis=2)
def parts(rng):
    a = rng.integers(-8, 9, (1, 8, 16, HB))
    t = np.rint(127.5 * np.add.reduce(a, axis=2) + 700 * rng.standard_normal((1, 8, HB))).astype(np.int64)
    x = rng.integers(0, 256, (N, 8, 16, V)); s = rng.integers(0, 256, (N, 8, 16, S)); b = rng.integers(0, V, (N, 8, 16, KB))
    return x, s, b, a, t
def near(rng, x, s, b, a, t, d, share, twins):
    m = rng.integers(0, V, (N, 8, S)); p = np.take_along_axis(x, m[:, :, None, :], 3)
    v = np.where(rng.random((N, 8, 1, S)) < share, np.clip(p + d, 0, 255), s)
    for q in range(N):
        for g in range(8):
            o = rng.permutation(S); v[q, g][:, o[:twins]] = v[q, g][:, o[twins:2 * twins]]; m[q, g, o[:twins]] = m[q, g, o[twins:2 * twins]]
    b[np.arange(N)[:, None, None], np.arange(8)[None, :, None], rng.integers(0, 16, (N, 8, S)), hashes(v, a, t)] = m
    return v
def pack(x, s, b, a, t):
    w = np.zeros((N, 8, 16, 16), np.float32); w[..., :HB] = a
    z = np.zeros((N, 8, 16), np.int32); z[..., :HB] = t
    return {"nx": x.reshape(N, 128, V).astype(np.float32).astype(BF), "bk": np.ascontiguousarray(b.reshape(N, 128, KB)).astype(np.int32),
            "s0": s.reshape(N, 128, S).astype(np.float32).astype(BF), "pa": w.reshape(N, 128, 16).astype(BF), "th": z.reshape(N, 128, 1)}
def setup_inputs(rng):
    x, s, b, a, t = parts(rng)
    s = near(rng, x, s, b, a, t, rng.integers(-40, 41, s.shape), 0.5, S // 8)
    return pack(x, s, b, a, t)
def setup_inputs_ties(rng):
    x, s, b, a, t = parts(rng)
    pat = rng.integers(0, 256, (N, 8, 16, 24)); x = np.take_along_axis(pat, rng.integers(0, 24, (N, 8, 1, V)), 3)
    s = np.where(rng.random((N, 8, 1, S)) < 0.5, np.take_along_axis(pat, rng.integers(0, 24, (N, 8, 1, S)), 3), s)
    for i in range(HB): t[0, :, i] = np.add.reduce(a[0, :, :, i] * s[i % N, :, :, (7 * i) % S], axis=1)
    return pack(x, s, b, a, t)
def setup_inputs_alike(rng):
    x, s, b, a, t = parts(rng)
    s[:, 0] = s[:, 0, :, :1].copy(); s[:, 1] = np.repeat(s[:, 1, :, :S // 16], 16, axis=2)
    b[:, 2] = rng.choice(np.array([0, 1, V - 2, V - 1]), (N, 16, KB)); t[:, 3] = 32767; t[:, 4] = -32768
    b[:, 5] = b[:, 5, :1].copy(); b[:, 6, :, 1::2] = b[:, 6, :, 0::2]
    t[:, 7] = 32767
    for q in range(N):
        m = 16 * rng.integers(0, V // 16, 2); lo, hi = int(m[0]), int(m[1]) + 8
        x[q, 7][:, lo] = rng.integers(0, 4, 16); x[q, 7][:, hi] = rng.integers(252, 256, 16)
        b[q, 7, :, :M] = hi; b[q, 7, 0, :M] = lo
    s[:, 7] = rng.integers(0, 4, (N, 16, S)); s[:, 7, :, :2] = 255 - s[:, 7, :, :2]
    return pack(x, s, b, a, t)
def setup_inputs_ends(rng):
    x, s, b, a, t = parts(rng)
    x = rng.integers(CL + 1, 255 - CL, x.shape); d = rng.choice(np.array([-CL - 1, -CL, 1 - CL, -1, 0, 1, CL - 1, CL, CL + 1]), s.shape)
    s = near(rng, x, s, b, a, t, d, 0.9, 2)
    x[:, 5] = 255 * rng.integers(0, 2, (N, 16, V)); s[:, 5] = 255 * rng.integers(0, 2, (N, 16, S)); x[:, 6] = 255; s[:, 6] = 0
    e = HB - 1; a[0, 3] = np.eye(16, HB, dtype=np.int64)
    t[0, 3] = CL // 2; t[0, 3, 1::2] = 0; t[0, 3, e] = 2 * CL + CL // 2
    pat = rng.permutation(2 ** e)[:S] + 2 ** e
    on = np.ones((16, S), bool); on[:HB] = ((pat[None, :] >> np.arange(HB)[:, None]) & 1) == 1
    s[:, 3] = np.where(on, rng.integers(128, 161, (N, 16, S)), 0); x[:, 3] = 0
    for q in range(N): b[q, 3, 0, pat] = rng.permutation(V)[:S]
    a[0, 4] = np.where(np.arange(HB) % 2 == 1, -1, 1) * (8 - (rng.random((16, HB)) < 0.125).astype(np.int64))
    a[0, 4, :, 0] = 8; a[0, 4, :, 1] = -8
    t[0, 4] = np.clip(240 * np.add.reduce(a[0, 4], axis=0) + np.rint(250 * rng.standard_normal(HB)).astype(np.int64), -32768, 32767)
    t[0, 4, 0] = 32639; t[0, 4, 1] = -32640
    x[:, 4] = rng.integers(225, 256, (N, 16, V)); s[:, 4] = rng.integers(225, 256, (N, 16, S)); s[:, 4, :, ::8] = 255
    x[:, 7] = rng.integers(253, 256, (N, 16, V)); s[:, 7] = rng.integers(0, 41, (N, 16, S))
    t[0, 7] = np.rint(20 * np.add.reduce(a[0, 7], axis=0) + 100 * rng.standard_normal(HB)).astype(np.int64)
    return pack(x, s, b, a, t)
def setup_inputs_few(rng):
    x, s, b, a, t = parts(rng)
    t[:, :, 5:] = np.where(rng.random((1, 8, HB - 5)) < 0.5, 32767, -32768)
    a[:, 1, :, 6] = 0; t[:, 1, 6] = -1; a[:, 2, :, 7] = 0; t[:, 2, 7] = 0
    s = near(rng, x, s, b, a, t, rng.integers(-60, 61, s.shape), 0.7, S // 8)
    return pack(x, s, b, a, t)
def setup_inputs_spread(rng):
    x, s, b, a, t = parts(rng)
    a = np.where(rng.random(a.shape) < 0.5, 0, a)
    t = np.rint(40 * np.add.reduce(a, axis=2) + 400 * rng.standard_normal((1, 8, HB))).astype(np.int64)
    x = np.minimum((np.exp2(8 * rng.random((N, 8, 1, V))) * rng.random(x.shape)).astype(np.int64), 255)
    s = np.minimum((np.exp2(8 * rng.random((N, 8, 1, S))) * rng.random(s.shape)).astype(np.int64), 255)
    b = np.minimum((V * rng.random(b.shape) ** 3).astype(np.int64), V - 1)
    return pack(x, s, b, a, t)
def check_inputs(d):
    bad = []
    for k, lo, hi in (("nx", 0, 255), ("bk", 0, V - 1), ("s0", 0, 255), ("pa", -8, 8), ("th", -32768, 32767)):
        v = np.asarray(d[k]).astype(np.float64)
        if not np.all((v >= lo) & (v <= hi) & (v == np.floor(v))): bad.append("range of " + k)
    p = np.asarray(d["pa"]).astype(np.float64); z = np.asarray(d["th"]).astype(np.float64)
    if np.any(p != p[:1]): bad.append("pa alike on all ranks")
    if np.any(z != z[:1]): bad.append("th alike on all ranks")
    if np.any(p[:, :, HB:] != 0): bad.append("zeros of pa")
    if np.any(z.reshape(-1, 8, 16)[:, :, HB:] != 0): bad.append("zeros of th")
    return bad
def reference(nx, bk, s0, pa, th):
    x = nx.astype(np.float32).astype(np.int64).reshape(N, 8, 16, V); b = bk.astype(np.int64).reshape(N, 8, 16, KB)
    s = s0.astype(np.float32).astype(np.int64).reshape(N, 8, 16, S)
    a = pa.astype(np.float32).astype(np.int64).reshape(N, 8, 16, 16)[..., :HB]; t = th.astype(np.int64).reshape(N, 8, 16)[..., :HB]
    lower = np.tri(S, S, -1) > 0
    src = (np.arange(N)[:, None] - 1 - np.arange(S)[None, :] // SB) % N
    for rnd in range(RO):
        h = hashes(s, a, t)
        cols = h[..., None] ^ np.arange(M)
        cand = np.take_along_axis(b, cols.reshape(N, 8, 1, S * M), 3).reshape(N, 8, 16, S, M)
        cand = np.ascontiguousarray(cand.transpose(0, 1, 3, 4, 2)).reshape(N, 8, S, 16 * M)
        w = np.take_along_axis(x, cand.reshape(N, 8, 1, S * 16 * M), 3).reshape(N, 8, 16, S, 16 * M)
        dist = np.add.reduce(np.abs(w - s[..., None]), axis=2)
        c = np.take_along_axis(cand, np.argmin(dist, axis=3)[..., None], 3)[..., 0]
        xc = np.take_along_axis(x, c[:, :, None, :], 3)
        x1 = xc + np.clip(s - xc, -CL, CL); h1 = hashes(x1, a, t)
        same = (c[..., :, None] == c[..., None, :]) | (h1[..., :, None] == h1[..., None, :])
        stand = ~np.any(same & lower, axis=3)
        s1 = (s + xc) & 255
        for r in range(N):
            for g in range(8):
                k = np.flatnonzero(stand[r, g]); ck = c[r, g, k]
                x[r, g][:, ck] = x1[r, g][:, k]
                b[r, g, (ck + k) & 15, h1[r, g, k]] = ck
        s = np.take_along_axis(s1, src[:, None, None, :], 0)
    return {"ys": s.reshape(N, 128, S).astype(np.float32), "yb": b.reshape(N, 128, KB).astype(np.float32)}

@@ -1,0 +1,578 @@
+import math
+from concourse.mybir import AluOpType, AxisListType, ActivationFunctionType
+
+ALU, ACT = AluOpType, ActivationFunctionType
+V, KB, S, RO = 3072, 1024, 48, 3
+PAD = 64
+BIG = 8192.0
+C2048 = 1.5 * 2.0 ** 34
+C256 = 1.5 * 2.0 ** 31
+C16 = 1.5 * 2.0 ** 27
+
+PLAN = {
+    "chunks": "v2a4v5v5 a3v5a3v5 a4v5v4v3",
+    "updates": [(0, 2), (2, 3)], "scan": [True, True, False],
+    "steps": [("cu", 0, 1), ("cf", 0, 1), ("search", 0, 1), ("cu", 1, 2), ("cf", 1, 2), ("search", 1, 2), ("winner", 0, 1), ("hash", 2, 3),
+              ("cu", 2, 3), ("cf", 2, 3), ("search", 2, 3), ("winner", 1, 2), ("update", 0, 2), ("move", 0, 1), ("move", 1, 2),
+              ("next", 0, 1), ("winner", 2, 3), ("next", 1, 2), ("update", 2, 3), ("move", 2, 3)],
+    "starts": [(40.0, 1000.0), (40.0, 2500.0), (40.0, 5000.0), (70.0, 2500.0)], "passes": 5, "moves": 14000,
+}
+EST = [{"cyc": 1.04, "pe": 0.55, "hop": 70.0, "gather": 1.56, "scatter": 3.8, "remote": 3000.0, "weight": 2},
+       {"cyc": 1.04, "pe": 0.8, "hop": 120.0, "gather": 1.9, "scatter": 5.0, "remote": 3600.0, "weight": 1},
+       {"cyc": 1.04, "pe": 0.45, "hop": 60.0, "gather": 1.2, "scatter": 2.5, "remote": 2200.0, "weight": 1}]
+
+SCRATCH = {}
+for _names, _cols, _dt in (
+        ("NX", PAD + V, "bfloat16"), ("BI", KB, "int32"), ("BF", PAD + KB, "float32"), ("ST", RO * S, "bfloat16"),
+        ("SX", (RO - 1) * 2 * S, "bfloat16"), ("SOF SLF CS RY M2 NM CM GO", S, "float32"), ("PA I16", 16, "bfloat16"), ("TH", 4, "int32"),
+        ("NTH AC", 1, "float32"), ("TS WC", 4, "float32"), ("XG AB", V, "bfloat16"),
+        ("ONE BM0 BM ID ID2 NID N128 AM NAM WR QI LOW", 128, "bfloat16"), ("BMH", 128, "float16"), ("GM VC", 8, "float32"),
+        ("W4", 512, "bfloat16"), ("ZA", 144, "bfloat16"), ("PI PJ", 1, "int32"), ("JR", 64, "float32"), ("J16 QT", 128, "float32"),
+        ("PW TWO ZER PWM J1 J2", 16, "float32"), ("SG", 2, "float32"), ("CK", 112, "bfloat16"), ("TK", 64, "bfloat16"), ("TC CN", 3, "float32"),
+        ("BS DD EE", S, "bfloat16"), ("BW", 2 * S, "bfloat16"), ("OF", 12, "uint16"), ("CU", 192, "uint16"), ("CF AD", 192, "float32"),
+        ("MM", 12, "float32"), ("OQ FO", 16, "uint16"), ("EQ", 384, "bfloat16"), ("SEL", S, "float16"), ("J3 DG", 96, "float32"),
+        ("SEG", 32, "float32")):
+    for _n in _names.split():
+        SCRATCH[_n] = ("sbuf", [128, _cols], _dt)
+for _n in "K0 K1 MB CA HA PP PQ HS".split():
+    SCRATCH[_n] = ("psum", [128, 512], "float32")
+SEMAPHORES = (["e_t", "e_v", "e_a", "e_g", "sent", "l_pa", "l_th", "l_s", "l_nx", "l_bk", "o_ys", "o_yb"]
+              + ["arr%d" % i for i in range(RO * 3)])
+
+
+def vw(name, c0=0, c1=None, step=1):
+    return (name, c0, SCRATCH[name][1][1] if c1 is None else c1, step)
+
+
+def width(v):
+    return (v[2] - v[1] + v[3] - 1) // v[3]
+
+
+def trace(T, send, est):
+    ops, cur, cyc = [], ["setup"], est["cyc"]
+
+    def ap(v):
+        if v[0] == "ind":
+            return ap(v[1]).indirect(ap(v[2]))
+        return T[v[0]][:, v[1]:v[2]:v[3]] if v[3] != 1 else T[v[0]][:, v[1]:v[2]]
+
+    def sc(x):
+        return ap(x) if isinstance(x, tuple) else x
+
+    def add(eng, fn, out, ins, cost, sem=None, lat=0.0):
+        rd, wr = [], []
+        for v in ins:
+            if isinstance(v, tuple):
+                rd.extend([v[1], v[2]] if v[0] == "ind" else [v])
+        for v in out:
+            if v[0] == "ind":
+                wr.append(v[1]); rd.append(v[2])
+            else:
+                wr.append(v)
+        ops.append({"eng": eng, "fn": fn, "rd": rd, "wr": wr, "cost": cost, "sem": sem, "lat": lat, "cls": cur[0]})
+
+    def ind(win, off):
+        return ("ind", win, off)
+
+    def vcost(out, a, per=None):
+        if out[0] == "ind":
+            return (60 + 16 * width(out[2]) * est["scatter"]) * cyc
+        if a[0] == "ind":
+            return (60 + 16 * width(a[2]) * est["gather"]) * cyc
+        if per is None:
+            per = 0.5 if all(SCRATCH[v[0]][2] in ("bfloat16", "float16", "uint16") for v in (out, a)) else 1.0
+        return max(64, width(a) * per) * cyc
+
+    def ts(out, a, s1, s2, op0, op1=None):
+        if op1 is None:
+            fn = lambda q: q.vector.tensor_scalar(ap(out), ap(a), sc(s1), None, op0)
+        else:
+            fn = lambda q: q.vector.tensor_scalar(ap(out), ap(a), sc(s1), sc(s2), op0, op1)
+        add("v", fn, [out], [a, s1, s2], vcost(out, a))
+
+    def tt(out, a, b, op):
+        add("v", lambda q: q.vector.tensor_tensor(ap(out), ap(a), ap(b), op), [out], [a, b], vcost(out, a, 2.0))
+
+    def cp(out, a):
+        add("v", lambda q: q.vector.tensor_copy(ap(out), ap(a)), [out], [a], vcost(out, a))
+
+    def ms(out, val):
+        add("v", lambda q: q.vector.memset(ap(out), val), [out], [], vcost(out, out))
+
+    def red(out, a, op):
+        add("v", lambda q: q.vector.tensor_reduce(ap(out), ap(a), AxisListType.X, op), [out], [a], vcost(out, a, 1.0))
+
+    def scan(out, d0, d1, init, op0, op1):
+        add("v", lambda q: q.vector.tensor_tensor_scan(ap(out), ap(d0), ap(d1), init, op0, op1), [out], [d0, d1], vcost(out, d0, 1.0))
+
+    def act(out, a, func, bias=0.0, scale=1.0, acc=None):
+        if acc is None:
+            fn = lambda q: q.scalar.activation(ap(out), ap(a), func, bias=sc(bias), scale=sc(scale))
+        else:
+            fn = lambda q: q.scalar.activation(ap(out), ap(a), func, bias=sc(bias), scale=sc(scale), accum_out=ap(acc))
+        cost = (78 + 16 * width(a[2]) * est["gather"]) * cyc if a[0] == "ind" else max(70, width(a)) * cyc
+        add("a", fn, [out] + ([acc] if acc else []), [a, bias, scale], cost + (20 if acc else 0))
+
+    def mm(out, lhs, rhs, start, stop):
+        add("t", lambda q: q.tensor.matmul(ap(out), ap(lhs), ap(rhs), start, stop), [out], [lhs, rhs], 64 * est["pe"])
+
+    def bank(terms):
+        for i, (out, lhs, rhs) in enumerate(terms):
+            mm(out, lhs, rhs, i == 0, i == len(terms) - 1)
+
+    def iota(out, pattern, base, mult, small=True):
+        if small:
+            fn = lambda q: q.iota(ap(out), pattern, base, mult, allow_small_or_imprecise_dtypes=True)
+        else:
+            fn = lambda q: q.iota(ap(out), pattern, base, mult)
+        add("g", fn, [out], [], 160 + 2 * width(out) * cyc)
+
+    def sel(out, a, pattern, cmp, base, mult):
+        add("g", lambda q: q.affine_select(ap(out), ap(a), pattern, cmp, 0.0, base, mult), [out], [a], 210 + 2 * width(out) * cyc)
+
+    add("s", lambda q: q.sync.dma_start(ap(vw("PA")), T.pa[:]), [vw("PA")], [], 60, "l_pa", 2000)
+    add("s", lambda q: q.sync.dma_start(ap(vw("TH", 0, 1)), T.th[:]), [vw("TH")], [], 60, "l_th", 2000)
+    add("s", lambda q: q.sync.dma_start(ap(vw("ST", 0, S)), T.s0[:]), [vw("ST", 0, S)], [], 60, "l_s", 2000)
+    add("a", lambda q: q.scalar.dma_start(ap(vw("BI")), T.bk[:]), [vw("BI")], [], 60, "l_bk", 3800)
+    add("s", lambda q: q.sync.dma_start(ap(vw("NX", PAD)), T.nx[:]), [vw("NX", PAD)], [], 60, "l_nx", 5500)
+
+    ms(vw("ONE"), 1.0)
+    iota(vw("PI"), [[0, 1]], 0, 1, small=False)
+    iota(vw("JR"), [[1, 64]], 0, 0)
+    sel(vw("BM0"), vw("ONE"), [[-16, 8], [0, 16]], ALU.is_ge, 0, 1)
+    sel(vw("BM"), vw("BM0"), [[16, 8], [0, 16]], ALU.is_ge, 15, -1)
+    sel(vw("ID"), vw("ONE"), [[-1, 128]], ALU.is_equal, 0, 1)
+    iota(vw("J16"), [[0, 8], [1, 16]], 0, 0)
+    ts(vw("PJ"), vw("PI"), 15, None, ALU.bitwise_and)
+    cp(vw("AC"), vw("PJ"))
+    ts(vw("I16"), vw("JR", 0, 16), vw("AC"), None, ALU.is_equal)
+    ms(vw("TWO"), 2.0); ms(vw("ZER"), 0.0)
+    scan(vw("PW"), vw("TWO"), vw("ZER"), 0.25, ALU.mult, ALU.add)
+    ms(vw("PW", 10, 11), -(512.0 + PAD)); ms(vw("PW", 11, 12), 0.5); ms(vw("PW", 12, 16), 0.0)
+    tt(vw("PWM"), vw("PW"), vw("I16"), ALU.mult)
+    red(vw("WC", 0, 1), vw("PWM"), ALU.add)
+    ts(vw("SG"), vw("I16", 0, 2), -2.0, 1.0, ALU.mult, ALU.add)
+    ts(vw("WC", 1, 3), vw("SG"), vw("WC", 0, 1), None, ALU.mult)
+    ts(vw("WC", 3, 4), vw("WC", 1, 2), vw("SG", 1, 2), None, ALU.mult)
+    ms(vw("W4"), 0.0)
+    cp(vw("GM"), vw("BM", 0, 128, 16))
+    for gg in range(8):
+        act(vw("AM", 16 * gg, 16 * gg + 16), vw("PA"), ACT.Copy, scale=vw("GM", gg, gg + 1))
+    ts(vw("NTH"), vw("TH", 0, 1), -1.0, -0.5, ALU.mult, ALU.add)
+    for aa in range(4):
+        for k in range(4):
+            o = vw("W4", 128 * aa + 4 * aa + k, 128 * (aa + 1), 16)
+            if k % 2:
+                act(o, vw("GM"), ACT.Copy, scale=vw("WC", k, k + 1))
+            else:
+                ts(o, vw("GM"), vw("WC", k, k + 1), None, ALU.mult)
+    ms(vw("ZA"), 0.0)
+    ts(vw("ZA", 15, 143, 16), vw("GM"), 2048.0, None, ALU.mult)
+    ts(vw("LOW", 0, 64), vw("JR"), -7.5, None, ALU.add)
+    ts(vw("LOW", 64, 128), vw("ONE", 0, 64), vw("AC"), 64.0, ALU.mult, ALU.mult)
+    act(vw("NAM"), vw("AM"), ACT.Copy, scale=-1.0)
+    act(vw("NID"), vw("ID"), ACT.Copy, scale=-1.0)
+    act(vw("ID2"), vw("ID"), ACT.Copy, scale=2.0)
+    act(vw("N128"), vw("ID"), ACT.Copy, scale=-128.0)
+    act(vw("WR"), vw("BM"), ACT.Copy, scale=vw("WC", 0, 1))
+    cp(vw("BMH"), vw("BM"))
+    ts(vw("QT"), vw("J16"), -107.5, None, ALU.add)
+    tt(vw("QT"), vw("QT"), vw("BM"), ALU.mult)
+    ts(vw("QI"), vw("QT"), 100.0, None, ALU.add)
+    j16 = vw("JR", 0, 16)
+    CKH_M, CKH_D, CKC_M, CKC_D, CK_U, CK_Y, CK_C = [vw("CK", 16 * i, 16 * i + 16) for i in range(7)]
+    ts(CKH_M, j16, vw("AC"), BIG, ALU.is_ge, ALU.mult)
+    ts(CKH_D, vw("I16"), BIG, -BIG, ALU.mult, ALU.add)
+    ts(CKC_M, CKH_M, 1536.0 + PAD, None, ALU.max)
+    ts(CKC_D, vw("I16"), BIG + 1536.0 + PAD, -BIG, ALU.mult, ALU.add)
+    ms(CK_U, 1536.0 + PAD); ms(CK_C, 1536.0)
+    ts(CK_Y, j16, vw("AC"), None, ALU.subtract)
+    ts(vw("TC"), vw("JR", 0, 48, 16), vw("AC"), None, ALU.add)
+    ms(vw("BF", 0, PAD), 0.0)
+    ts(vw("TS", 0, 1), vw("TH", 0, 1), C256, C256, ALU.add, ALU.subtract)
+    ts(vw("TS", 1, 2), vw("TH", 0, 1), vw("TS", 0, 1), None, ALU.subtract)
+    act(vw("TK", 0, 16), vw("ONE", 0, 16), ACT.Copy, scale=vw("TS", 0, 1))
+    act(vw("TK", 16, 32), vw("ONE", 0, 16), ACT.Copy, scale=vw("TS", 1, 2))
+    ms(vw("TK", 32, 48), 255.0); ms(vw("TK", 48, 64), -128.0)
+    ms(vw("SEG"), 1.0); ms(vw("SEG", 0, 32, 16), 0.0)
+
+    def hash_state(r, b0, b1):
+        n = 16 * (b1 - b0)
+        bank([(vw("HS", 0, n), vw("AM"), vw("ST", S * r + 16 * b0, S * r + 16 * b1))])
+        act(vw("BS", 16 * b0, 16 * b1), vw("HS", 0, n), ACT.Sign, bias=vw("NTH"))
+        ho = vw("HS", 64 + 4 * b0, 64 + 4 * b1)
+        bank([(ho, vw("W4", 128 * aa, 128 * aa + 128), vw("BS", 16 * b0 + aa, 16 * b1, 4)) for aa in range(4)])
+        ts(vw("OF", 4 * b0, 4 * b1), ho, -float(PAD) if r == 0 else 0.0, None, ALU.add)
+
+    def search(r, b):
+        key = vw("K%d" % ((3 * r + b) % 2), 0, 64)
+        mm(key, vw("ID"), vw("LOW", 0, 64), True, False)
+        mm(key, vw("ID"), vw("LOW", 64, 128), False, False)
+        spec, a0 = PLAN["chunks"].split()[b], 0
+        for eng, n in zip(spec[0::2], map(int, spec[1::2])):
+            t0 = 16 * b + a0
+            src = ind(vw("NX", PAD), vw("CU", 4 * t0, 4 * (t0 + n)))
+            if eng == "v":
+                cp(vw("XG", 64 * t0, 64 * (t0 + n)), src)
+            else:
+                act(vw("XG", 64 * t0, 64 * (t0 + n)), src, ACT.Copy)
+            for a in range(a0, a0 + n):
+                t = 16 * b + a
+                d = vw("AB", 64 * t, 64 * t + 64)
+                act(d, vw("XG", 64 * t, 64 * t + 64), ACT.Abs, bias=vw("ST", S * r + t, S * r + t + 1), scale=-1.0)
+                mm(key, vw("ZA", 15 - a, 143 - a), d, False, a == 15)
+            a0 += n
+        red(vw("MM", b, b + 1), key, ALU.min)
+
+    def winner(r, b):
+        last, c0, c1 = r == RO - 1, 16 * b, 16 * b + 16
+        s = vw("ST", S * r + c0, S * r + c1)
+        d, e, sb, cs, eq = vw("DD", c0, c1), vw("EE", c0, c1), vw("SEL", c0, c1), vw("CS", c0, c1), vw("EQ", 128 * b, 128 * b + 128)
+        m, r1, r2 = vw("MM", b, b + 1), vw("MM", 4 + b, 5 + b), vw("MM", 8 + b, 9 + b)
+        o1, oq = vw("OQ", 2 * b, 2 * b + 1), vw("OQ", 8 + 2 * b, 9 + 2 * b)
+        ts(r1, m, C2048, C2048, ALU.add, ALU.subtract)
+        ts(o1, m, r1, 7.5, ALU.subtract, ALU.add)
+        ts(r2, m, C16, C16, ALU.add, ALU.subtract)
+        tt(d, ind(vw("XG", 1024 * b, 1024 * b + 1024), o1), s, ALU.subtract)
+        ts(e, d, -12.0, 12.0, ALU.max, ALU.min)
+        ts(oq, r2, r1, 1.0 / 16, ALU.subtract, ALU.mult)
+        ts(eq, vw("QI"), r2, m, ALU.add, ALU.is_equal)
+        act(cs, ind(vw("CF", 64 * b, 64 * b + 64), oq), ACT.Copy)
+        mk = vw("K%d" % ((3 * r + b) % 2), 64, 80)
+        bank([(mk, eq, vw("I16"))])
+        tt(sb, mk, cs, ALU.mult)
+        pr, y, s1, x1 = vw("PP", 0, 16), vw("PP", 16, 32), vw("PQ", 0, 16), vw("PQ", 16, 32)
+        bank([(pr, vw("NID"), vw("TK", 0, 16)), (pr, vw("NID"), vw("TK", 16, 32)), (y, vw("NID"), vw("TK", 32, 48)),
+              (pr, vw("AM"), s), (y, vw("ID2"), s), (y, vw("ID"), d), (pr, vw("AM"), d), (pr, vw("NAM"), e)])
+        act(vw("BW", 2 * c0, 2 * c1), vw("PP", 0, 32), ACT.Sign, bias=-0.5)
+        bx = vw("BW", 2 * c0, 2 * c0 + 16)
+        scanned = PLAN["scan"][b]
+        terms = {"HA": ([], []), "CA": ([], []), "MB": ([], [])}
+
+        def part(out, const, lhs, rhs):
+            if const is not None:
+                terms[out[0]][0].append((out, vw("ID"), const))
+            terms[out[0]][1].append((out, lhs, rhs))
+
+        mpos, upos = (0, 16, 64)[b], (32, 48, None)[b]
+        part(vw("MB", 64 + c0, 64 + c1), CK_Y, vw("BMH"), sb)
+        part(vw("MB", 128 + c0, 128 + c1), CK_C, vw("BMH"), sb)
+        part(vw("MB", 208, 224) if scanned else vw("CA", 80, 96), CKC_D, vw("BMH"), sb)
+        part(vw("MB", 192, 208) if scanned else vw("HA", 80, 96), CKH_D, vw("WR"), bx)
+        part(vw("CA", mpos, mpos + 16), CKC_M, vw("BMH"), sb)
+        part(vw("HA", mpos, mpos + 16), CKH_M, vw("WR"), bx)
+        if upos is not None:
+            part(vw("CA", upos, upos + 16), CK_U, vw("BMH"), sb)
+            part(vw("HA", upos, upos + 16), None, vw("WR"), bx)
+        for name in ("HA", "CA", "MB"):
+            bank(terms[name][0] + terms[name][1])
+        bank(([] if last else [(x1, vw("NID"), vw("TK", 48, 64)), (x1, vw("ID"), s)]) + [(s1, vw("ID2"), s), (s1, vw("ID"), d)]
+             + ([] if last else [(x1, vw("ID"), d), (x1, vw("NID"), e)]) + [(s1, vw("N128"), vw("BW", 2 * c0 + 16, 2 * c1))])
+        base = 2 * S * r + 2 * c0
+        if last:
+            so, land = vw("SOF", c0, c1), vw("SLF", c0, c1)
+            act(so, s1, ACT.Identity, bias=-128.0)
+        else:
+            so, land = vw("SX", base, base + 16), vw("ST", S * (r + 1) + c0, S * (r + 1) + c1)
+            act(vw("SX", base, base + 32), vw("PQ", 0, 32), ACT.Identity, bias=-128.0)
+        add("g", lambda q: send(q, r, b, ap(land), ap(so)), [land], [so], 300, "arr%d" % (3 * r + b), est["remote"])
+        span, ad = ((0, 16), (16, 48), (32, 80))[b], (0, 32, 96)[b]
+        w = span[1] - span[0]
+        if scanned:
+            scan(vw("DG", 2 * c0, 2 * c1), vw("SEG"), vw("MB", 192, 224), 0.0, ALU.mult, ALU.max)
+            hc, cc, both = vw("DG", 32 * b + 15, 32 * b + 16), vw("DG", 32 * b + 31, 32 * b + 32), vw("DG", 32 * b + 15, 32 * b + 32, 16)
+        else:
+            hc, cc, both = vw("VC", b, b + 1), vw("VC", 4 + b, 5 + b), vw("VC", b, b + 5, 4)
+            act(vw("J2"), vw("CA", 80, 96), ACT.Relu, acc=cc)
+        act(vw("AD", ad + w, ad + 2 * w), vw("CA", span[0], span[1]), ACT.Abs, bias=cc, scale=-1.0)
+        if not scanned:
+            act(vw("J1"), vw("HA", 80, 96), ACT.Relu, acc=hc)
+        act(vw("AD", ad, ad + w), vw("HA", span[0], span[1]), ACT.Abs, bias=hc, scale=-1.0)
+        cn = vw("CN", b, b + 1)
+        act(vw("J3", 0, 2 * w), vw("AD", ad, ad + 2 * w), ACT.Relu, bias=BIG, scale=-BIG, acc=cn)
+        ph, pc = b + [x for x, z in PLAN["updates"] if x <= b < z][0], 8 + 2 * b
+        ts(vw("FO", ph, pc + 1, pc - ph), both, cn, vw("TC", b, b + 1), ALU.subtract, ALU.max)
+
+    def update(r, b0, b1):
+        c0, c1 = 16 * b0, 16 * b1
+        y, cc = vw("MB", 64 + c0, 64 + c1), vw("MB", 128 + c0, 128 + c1)
+        ry, m2, nm, cm, go = [vw(n, c0, c1) for n in ("RY", "M2", "NM", "CM", "GO")]
+        off = vw("FO", 2 * b0, b0 + b1)
+        ts(ry, y, C16, C16, ALU.add, ALU.subtract)
+        tt(m2, ry, y, ALU.is_equal)
+        act(nm, m2, ACT.Identity, bias=1.0, scale=-1.0)
+        tt(cm, m2, cc, ALU.mult)
+        tt(go, ind(vw("BF"), off), nm, ALU.mult)
+        tt(ind(vw("BF"), off), go, cm, ALU.add)
+
+    hash_state(0, 0, 3)
+    cp(vw("CU"), ind(vw("BI"), vw("OF")))
+    ts(vw("CF"), vw("CU"), -1536.0, None, ALU.add)
+    cp(vw("BF", PAD), vw("BI"))
+    for r in range(RO):
+        for name, b0, b1 in PLAN["steps"]:
+            cur[0] = name + str(b0)
+            if name == "cu" and r > 0:
+                cp(vw("CU", 64 * b0, 64 * b1), ind(vw("BF"), vw("OF", 4 * b0, 4 * b1)))
+            elif name == "cf" and r > 0:
+                ts(vw("CF", 64 * b0, 64 * b1), vw("CU", 64 * b0, 64 * b1), -1536.0, None, ALU.add)
+            elif name == "search":
+                search(r, b0)
+            elif name == "winner":
+                winner(r, b0)
+            elif name == "update":
+                update(r, b0, b1)
+            elif name == "hash" and r > 0:
+                hash_state(r, b0, b1)
+            elif name == "next" and r < RO - 1:
+                hash_state(r + 1, b0, b1)
+            elif name == "move" and r < RO - 1:
+                base = 2 * S * r + 32 * b0 + 16
+                cp(ind(vw("NX"), vw("FO", 8 + 2 * b0, 9 + 2 * b0)), vw("SX", base, base + 16))
+    add("s", lambda q: q.sync.dma_start(T.yb[:], ap(vw("BF", PAD))), [], [vw("BF", PAD)], 60, "o_yb", 3800)
+    add("a", lambda q: q.scalar.dma_start(T.ys[:], ap(vw("SLF"))), [], [vw("SLF")], 60, "o_ys", 2000)
+    return ops
+
+
+def edges(ops):
+    seen, reach = {}, []
+    for i, o in enumerate(ops):
+        dep = set()
+        for vs, writes in ((o["rd"], False), (o["wr"], True)):
+            for v in vs:
+                psum = SCRATCH[v[0]][0] == "psum"
+                for j, u, w in seen.get(v[0], []):
+                    if (psum and (ops[j]["eng"] != o["eng"] or o["eng"] == "t")) or ((w or writes) and u[1] < v[2] and v[1] < u[2]):
+                        dep.add(j)
+        for vs, writes in ((o["rd"], False), (o["wr"], True)):
+            for v in vs:
+                seen.setdefault(v[0], []).append((i, v, writes))
+        cover = 0
+        for j in dep:
+            cover |= reach[j]
+        o["dep"] = sorted(dep)
+        o["near"] = [j for j in o["dep"] if not cover >> j & 1]
+        for j in dep:
+            cover |= 1 << j
+        reach.append(cover)
+    return reach
+
+
+def times(order, eng, fig):
+    cost, lat, gp = fig
+    end, why = [0.0] * len(cost), [-1] * len(cost)
+    free, last, m, mi = dict.fromkeys("tvags", 0.0), dict.fromkeys("tvags", -1), 0.0, -1
+    for i in order:
+        e = eng[i]
+        t, w = free[e], last[e]
+        for j, gap in gp[i]:
+            if end[j] + gap > t:
+                t, w = end[j] + gap, j
+        end[i] = free[e] = t + cost[i]
+        why[i], last[e] = w, i
+        if end[i] + lat[i] > m:
+            m, mi = end[i] + lat[i], i
+    return m, mi, why, end
+
+
+def greedy(eng, cost, pred, prio, slack, at):
+    n = len(eng)
+    left, succ = [len(p) for p in pred], [[] for i in range(n)]
+    for i in range(n):
+        for j, gap in pred[i]:
+            succ[j].append((i, gap))
+    at, end, free = list(at), [0.0] * n, dict.fromkeys("tvags", 0.0)
+    ready, order = [i for i in range(n) if left[i] == 0], []
+    while ready:
+        first = min(ready, key=lambda i: (max(at[i], free[eng[i]]), -prio[i], i))
+        e = eng[first]
+        t0 = max(at[first], free[e]) + min(slack, cost[first])
+        i = max((k for k in ready if eng[k] == e and at[k] <= t0), key=lambda k: (prio[k], -k))
+        ready.remove(i)
+        end[i] = free[e] = max(at[i], free[e]) + cost[i]
+        order.append(i)
+        for k, gap in succ[i]:
+            at[k] = max(at[k], end[i] + gap)
+            left[k] -= 1
+            if left[k] == 0:
+                ready.append(k)
+    return order, end
+
+
+def plan(T):
+    ops = trace(T, None, EST[0])
+    reach, n, eng = edges(ops), len(ops), [o["eng"] for o in ops]
+    figs = []
+    for est in EST:
+        alt = trace(T, None, est)
+        figs.append(([o["cost"] for o in alt], [o["lat"] for o in alt],
+                     [[(j, 0.0 if eng[j] == "t" and eng[i] == "t" else alt[j]["lat"] + est["hop"]) for j in ops[i]["near"]] for i in range(n)]))
+
+    def full(o):
+        res = [times(o, eng, f) for f in figs]
+        return sum(est["weight"] * x[0] for est, x in zip(EST, res)) / sum(est["weight"] for est in EST), res
+
+    cost, lat, gp = figs[0]
+    back = [[] for i in range(n)]
+    for i in range(n):
+        for j, gap in gp[i]:
+            back[j].append((i, gap))
+    tail = [cost[i] + lat[i] for i in range(n)]
+    for i in range(n - 1, -1, -1):
+        for j, gap in gp[i]:
+            tail[j] = max(tail[j], cost[j] + gap + tail[i])
+    early = [not (o["cls"][:2] == "se" or o["cls"] in ("winner2", "update2")) for o in ops]
+    best = None
+    for slack, bonus in PLAN["starts"]:
+        prio = [tail[i] + bonus * early[i] for i in range(n)]
+        for it in range(PLAN["passes"]):
+            order, end = greedy(eng, cost, gp, prio, slack, [0.0] * n)
+            score = full(order)[0]
+            if best is None or score < best[0]:
+                best = (score, order)
+            prio = greedy(eng, cost, back, end, slack, [0.0 if back[i] else lat[i] for i in range(n)])[1]
+    state = [1]
+
+    def rnd(k):
+        state[0] = (state[0] * 6364136223846793005 + 1442695040888963407) % (1 << 64)
+        return (state[0] >> 33) % k
+
+    order = best[1]
+    now, res = full(order)
+    for it in range(PLAN["moves"]):
+        m, i, why, end = res[rnd(len(figs))]
+        arcs = []
+        while why[i] >= 0:
+            j = why[i]
+            if eng[j] == eng[i] and not reach[i] >> j & 1:
+                arcs.append((j, i))
+            i = j
+        if not arcs:
+            continue
+        u, v = arcs[rnd(len(arcs))]
+        pu, pv, far, moved, queues = order.index(u), order.index(v), rnd(4) if rnd(2) else 0, set(), set()
+        if rnd(2):
+            for k in range(far):
+                q = pu - 1
+                while q >= 0 and eng[order[q]] != eng[v]:
+                    q -= 1
+                if q < 0 or reach[v] >> order[q] & 1:
+                    break
+                pu = q
+            mid, bits = order[pu:pv], reach[v]
+            for x in reversed(mid):
+                if bits >> x & 1 or eng[x] in queues:
+                    moved.add(x); queues.add(eng[x]); bits |= reach[x]
+            if eng[v] in queues:
+                continue
+            new = order[:pu] + [x for x in mid if x in moved] + [v] + [x for x in mid if x not in moved] + order[pv + 1:]
+        else:
+            for k in range(far):
+                q = pv + 1
+                while q < n and eng[order[q]] != eng[u]:
+                    q += 1
+                if q >= n or reach[order[q]] >> u & 1:
+                    break
+                pv = q
+            mid, bits = order[pu + 1:pv + 1], 1 << u
+            for x in mid:
+                if reach[x] & bits or eng[x] in queues:
+                    moved.add(x); queues.add(eng[x]); bits |= 1 << x
+            if eng[u] in queues:
+                continue
+            new = order[:pu] + [x for x in mid if x not in moved] + [u] + [x for x in mid if x in moved] + order[pv + 1:]
+        score, nres = full(new)
+        if score <= now or rnd(1 << 20) / (1 << 20) < math.exp((now - score) / (20.0 * (1 - it / PLAN["moves"]) + 1)):
+            order, now, res = new, score, nres
+            if now < best[0]:
+                best = (now, order)
+    return best[1], full(best[1])[1]
+
+
+PLANNED = {}
+
+
+def engines_for(topo, cores, src, r, b):
+    common = None
+    for k in range(1, len(cores)):
+        es = topo.engines(cores[src], cores[(src + k) % len(cores)])
+        common = es if common is None else [e for e in common if e in es]
+    h = len(common) // 2
+    if r == 0 and b < 2:
+        return common[h * b:h * b + h]
+    return common
+
+
+def rank_program(g, core, T, topo):
+    rank = T.rank_of(core)
+    if rank is None:
+        return
+    cores = list(T.cores)
+    nr = len(cores)
+    sent = [0]
+
+    def send(q, r, b, land, so):
+        dst = cores[(rank + 1 + b) % nr]
+        rid, pid = topo.addr(dst, core)
+        es = engines_for(topo, cores, rank, r, b)
+        sent[0] += len(es)
+        q.remote_dma(land, so, T.sem["arr%d" % (3 * r + b)], T.sem.sent, pid, rid, sum(1 << e for e in es))
+
+    if "order" not in PLANNED:
+        PLANNED["order"], PLANNED["times"] = plan(T)
+    order, end = PLANNED["order"], PLANNED["times"][0][3]
+    ops = trace(T, send, EST[0])
+    edges(ops)
+    queue = {"t": g.tensor, "v": g.vector, "a": g.scalar, "g": g, "s": g.sync}
+    pos, count = {}, {e: 0 for e in queue}
+    for i in order:
+        count[ops[i]["eng"]] += 1
+        pos[i] = count[ops[i]["eng"]]
+    known, after, waits = {e: {} for e in queue}, {}, {}
+    for i in order:
+        o = ops[i]
+        kn = known[o["eng"]]
+        want = {}
+        for j in o["dep"]:
+            if not (ops[j]["eng"] == "t" and o["eng"] == "t"):
+                key = ops[j]["sem"] or ops[j]["eng"]
+                if key not in want or pos[want[key]] < pos[j]:
+                    want[key] = j
+        mine = []
+        for j in sorted(want.values(), key=lambda j: -end[j]):
+            key = ops[j]["sem"] or ops[j]["eng"]
+            if kn.get(key, 0) >= pos[j]:
+                continue
+            mine.append(j)
+            kn[key] = pos[j]
+            if not (ops[j]["sem"] or "").startswith("arr"):
+                for k2, v2 in after[j].items():
+                    kn[k2] = max(kn.get(k2, 0), v2)
+        waits[i] = mine
+        after[i] = dict(kn)
+    raised = set(j for i in order for j in waits[i])
+    value, count = {}, {e: 0 for e in queue}
+    for i in order:
+        o = ops[i]
+        if o["sem"] is None:
+            if i in raised:
+                count[o["eng"]] += 1
+                value[i] = count[o["eng"]]
+        elif o["sem"].startswith("arr"):
+            k = int(o["sem"][3:])
+            value[i] = len(engines_for(topo, cores, (rank - 1 - k % 3) % nr, k // 3, k % 3))
+        else:
+            value[i] = 16
+    for i in order:
+        o = ops[i]
+        for j in waits[i]:
+            queue[o["eng"]].wait_ge(T.sem[ops[j]["sem"] or "e_" + ops[j]["eng"]], value[j])
+        ins = o["fn"](g)
+        if o["sem"] is None:
+            if i in raised:
+                ins.then_inc(T.sem["e_" + o["eng"]], 1)
+        elif not o["sem"].startswith("arr"):
+            ins.then_inc(T.sem[o["sem"]], 16)
+    g.wait_ge(T.sem.sent, sent[0])
+    g.sync.wait_ge(T.sem.o_yb, 16)
+    g.scalar.wait_ge(T.sem.o_ys, 16)

@@ -6,30 +6,30 @@ V, KB, S, RO = 3072, 1024, 48, 3
 PAD = 64
 BIG = 8192.0
 C2048 = 1.5 * 2.0 ** 34
-C256 = 1.5 * 2.0 ** 31
 C16 = 1.5 * 2.0 ** 27
 
 PLAN = {
-    "chunks": "v2a4v5v5 a3v5a3v5 a4v5v4v3",
+    "chunks": "v2a3v3v3a2v3 a3v3v3a3v2v2 a3v3v3a3v2v2",
     "updates": [(0, 2), (2, 3)], "scan": [True, True, False],
     "steps": [("cu", 0, 1), ("cf", 0, 1), ("search", 0, 1), ("cu", 1, 2), ("cf", 1, 2), ("search", 1, 2), ("winner", 0, 1), ("hash", 2, 3),
               ("cu", 2, 3), ("cf", 2, 3), ("search", 2, 3), ("winner", 1, 2), ("update", 0, 2), ("move", 0, 1), ("move", 1, 2),
               ("next", 0, 1), ("winner", 2, 3), ("next", 1, 2), ("update", 2, 3), ("move", 2, 3)],
-    "starts": [(40.0, 1000.0), (40.0, 2500.0), (40.0, 5000.0), (70.0, 2500.0)], "passes": 5, "moves": 14000,
+    "starts": [(40.0, 2500.0), (100.0, 5000.0), (60.0, 1000.0)], "passes": 5, "moves": 14000,
 }
-EST = [{"cyc": 1.04, "pe": 0.55, "hop": 70.0, "gather": 1.56, "scatter": 3.8, "remote": 3000.0, "weight": 2},
-       {"cyc": 1.04, "pe": 0.8, "hop": 120.0, "gather": 1.9, "scatter": 5.0, "remote": 3600.0, "weight": 1},
-       {"cyc": 1.04, "pe": 0.45, "hop": 60.0, "gather": 1.2, "scatter": 2.5, "remote": 2200.0, "weight": 1}]
+EST = [{"cyc": 0.9, "pe": 0.46, "hop": 150.0, "gather": 1.56, "scatter": 3.8, "remote": 4300.0, "first": 2000.0, "weight": 1},
+       {"cyc": 0.87, "pe": 0.44, "hop": 200.0, "gather": 1.56, "scatter": 3.8, "remote": 3000.0, "first": 0.0, "weight": 1},
+       {"cyc": 0.87, "pe": 0.44, "hop": 100.0, "gather": 1.8, "scatter": 3.8, "remote": 5300.0, "first": 1500.0, "weight": 1},
+       {"cyc": 1.15, "pe": 0.6, "hop": 120.0, "gather": 1.8, "scatter": 4.5, "remote": 3500.0, "first": 2000.0, "weight": 1}]
 
 SCRATCH = {}
 for _names, _cols, _dt in (
         ("NX", PAD + V, "bfloat16"), ("BI", KB, "int32"), ("BF", PAD + KB, "float32"), ("ST", RO * S, "bfloat16"),
-        ("SX", (RO - 1) * 2 * S, "bfloat16"), ("SOF SLF CS RY M2 NM CM GO", S, "float32"), ("PA I16", 16, "bfloat16"), ("TH", 4, "int32"),
-        ("NTH AC", 1, "float32"), ("TS WC", 4, "float32"), ("XG AB", V, "bfloat16"),
-        ("ONE BM0 BM ID ID2 NID N128 AM NAM WR QI LOW", 128, "bfloat16"), ("BMH", 128, "float16"), ("GM VC", 8, "float32"),
+        ("SO", (RO - 1) * S, "bfloat16"), ("SOF SLF YY YW CS RY M2 NM CM GO", S, "float32"), ("PA I16", 16, "bfloat16"), ("TH", 4, "int32"),
+        ("NTH AC", 1, "float32"), ("WC", 4, "float32"), ("XG AB", V, "bfloat16"),
+        ("ONE BM0 BM ID NID AM NAM WR QI LOW", 128, "bfloat16"), ("BMH", 128, "float16"), ("GM VC", 8, "float32"),
         ("W4", 512, "bfloat16"), ("ZA", 144, "bfloat16"), ("PI PJ", 1, "int32"), ("JR", 64, "float32"), ("J16 QT", 128, "float32"),
-        ("PW TWO ZER PWM J1 J2", 16, "float32"), ("SG", 2, "float32"), ("CK", 112, "bfloat16"), ("TK", 64, "bfloat16"), ("TC CN", 3, "float32"),
-        ("BS DD EE", S, "bfloat16"), ("BW", 2 * S, "bfloat16"), ("OF", 12, "uint16"), ("CU", 192, "uint16"), ("CF AD", 192, "float32"),
+        ("PW TWO ZER PWM J1 J2", 16, "float32"), ("SG", 2, "float32"), ("CK", 112, "bfloat16"), ("TC CN", 3, "float32"),
+        ("BS DD EE BX XN", S, "bfloat16"), ("OF", 12, "uint16"), ("CU", 192, "uint16"), ("CF AD", 192, "float32"),
         ("MM", 12, "float32"), ("OQ FO", 16, "uint16"), ("EQ", 384, "bfloat16"), ("SEL", S, "float16"), ("J3 DG", 96, "float32"),
         ("SEG", 32, "float32")):
     for _n in _names.split():
@@ -110,7 +110,7 @@ def trace(T, send, est):
             fn = lambda q: q.scalar.activation(ap(out), ap(a), func, bias=sc(bias), scale=sc(scale))
         else:
             fn = lambda q: q.scalar.activation(ap(out), ap(a), func, bias=sc(bias), scale=sc(scale), accum_out=ap(acc))
-        cost = (78 + 16 * width(a[2]) * est["gather"]) * cyc if a[0] == "ind" else max(70, width(a)) * cyc
+        cost = (78 + 16 * width(a[2]) * est["gather"] if a[0] == "ind" else max(66, width(a))) * cyc
         add("a", fn, [out] + ([acc] if acc else []), [a, bias, scale], cost + (20 if acc else 0))
 
     def mm(out, lhs, rhs, start, stop):
@@ -134,7 +134,7 @@ def trace(T, send, est):
     add("s", lambda q: q.sync.dma_start(ap(vw("TH", 0, 1)), T.th[:]), [vw("TH")], [], 60, "l_th", 2000)
     add("s", lambda q: q.sync.dma_start(ap(vw("ST", 0, S)), T.s0[:]), [vw("ST", 0, S)], [], 60, "l_s", 2000)
     add("a", lambda q: q.scalar.dma_start(ap(vw("BI")), T.bk[:]), [vw("BI")], [], 60, "l_bk", 3800)
-    add("s", lambda q: q.sync.dma_start(ap(vw("NX", PAD)), T.nx[:]), [vw("NX", PAD)], [], 60, "l_nx", 5500)
+    add("s", lambda q: q.sync.dma_start(ap(vw("NX", PAD)), T.nx[:]), [vw("NX", PAD)], [], 60, "l_nx", 6500)
 
     ms(vw("ONE"), 1.0)
     iota(vw("PI"), [[0, 1]], 0, 1, small=False)
@@ -172,8 +172,6 @@ def trace(T, send, est):
     ts(vw("LOW", 64, 128), vw("ONE", 0, 64), vw("AC"), 64.0, ALU.mult, ALU.mult)
     act(vw("NAM"), vw("AM"), ACT.Copy, scale=-1.0)
     act(vw("NID"), vw("ID"), ACT.Copy, scale=-1.0)
-    act(vw("ID2"), vw("ID"), ACT.Copy, scale=2.0)
-    act(vw("N128"), vw("ID"), ACT.Copy, scale=-128.0)
     act(vw("WR"), vw("BM"), ACT.Copy, scale=vw("WC", 0, 1))
     cp(vw("BMH"), vw("BM"))
     ts(vw("QT"), vw("J16"), -107.5, None, ALU.add)
@@ -189,11 +187,6 @@ def trace(T, send, est):
     ts(CK_Y, j16, vw("AC"), None, ALU.subtract)
     ts(vw("TC"), vw("JR", 0, 48, 16), vw("AC"), None, ALU.add)
     ms(vw("BF", 0, PAD), 0.0)
-    ts(vw("TS", 0, 1), vw("TH", 0, 1), C256, C256, ALU.add, ALU.subtract)
-    ts(vw("TS", 1, 2), vw("TH", 0, 1), vw("TS", 0, 1), None, ALU.subtract)
-    act(vw("TK", 0, 16), vw("ONE", 0, 16), ACT.Copy, scale=vw("TS", 0, 1))
-    act(vw("TK", 16, 32), vw("ONE", 0, 16), ACT.Copy, scale=vw("TS", 1, 2))
-    ms(vw("TK", 32, 48), 255.0); ms(vw("TK", 48, 64), -128.0)
     ms(vw("SEG"), 1.0); ms(vw("SEG", 0, 32, 16), 0.0)
 
     def hash_state(r, b0, b1):
@@ -227,13 +220,21 @@ def trace(T, send, est):
     def winner(r, b):
         last, c0, c1 = r == RO - 1, 16 * b, 16 * b + 16
         s = vw("ST", S * r + c0, S * r + c1)
-        d, e, sb, cs, eq = vw("DD", c0, c1), vw("EE", c0, c1), vw("SEL", c0, c1), vw("CS", c0, c1), vw("EQ", 128 * b, 128 * b + 128)
-        m, r1, r2 = vw("MM", b, b + 1), vw("MM", 4 + b, 5 + b), vw("MM", 8 + b, 9 + b)
+        d, e, sb, cs, yy, ww, bx = [vw(n, c0, c1) for n in ("DD", "EE", "SEL", "CS", "YY", "YW", "BX")]
+        eq, m, r1, r2 = vw("EQ", 128 * b, 128 * b + 128), vw("MM", b, b + 1), vw("MM", 4 + b, 5 + b), vw("MM", 8 + b, 9 + b)
         o1, oq = vw("OQ", 2 * b, 2 * b + 1), vw("OQ", 8 + 2 * b, 9 + 2 * b)
         ts(r1, m, C2048, C2048, ALU.add, ALU.subtract)
         ts(o1, m, r1, 7.5, ALU.subtract, ALU.add)
         ts(r2, m, C16, C16, ALU.add, ALU.subtract)
-        tt(d, ind(vw("XG", 1024 * b, 1024 * b + 1024), o1), s, ALU.subtract)
+        win = ind(vw("XG", 1024 * b, 1024 * b + 1024), o1)
+        so = vw("SOF", c0, c1) if last else vw("SO", S * r + c0, S * r + c1)
+        land = vw("SLF", c0, c1) if last else vw("ST", S * (r + 1) + c0, S * (r + 1) + c1)
+        tt(yy, win, s, ALU.add)
+        ts(ww, yy, 256.0, -256.0, ALU.is_ge, ALU.mult)
+        tt(so, yy, ww, ALU.add)
+        add("g", lambda q: send(q, r, b, ap(land), ap(so)), [land], [so], 300, "arr%d" % (3 * r + b),
+            est["remote"] + (est["first"] if r == 0 and b < 2 else 0.0))
+        tt(d, win, s, ALU.subtract)
         ts(e, d, -12.0, 12.0, ALU.max, ALU.min)
         ts(oq, r2, r1, 1.0 / 16, ALU.subtract, ALU.mult)
         ts(eq, vw("QI"), r2, m, ALU.add, ALU.is_equal)
@@ -241,11 +242,9 @@ def trace(T, send, est):
         mk = vw("K%d" % ((3 * r + b) % 2), 64, 80)
         bank([(mk, eq, vw("I16"))])
         tt(sb, mk, cs, ALU.mult)
-        pr, y, s1, x1 = vw("PP", 0, 16), vw("PP", 16, 32), vw("PQ", 0, 16), vw("PQ", 16, 32)
-        bank([(pr, vw("NID"), vw("TK", 0, 16)), (pr, vw("NID"), vw("TK", 16, 32)), (y, vw("NID"), vw("TK", 32, 48)),
-              (pr, vw("AM"), s), (y, vw("ID2"), s), (y, vw("ID"), d), (pr, vw("AM"), d), (pr, vw("NAM"), e)])
-        act(vw("BW", 2 * c0, 2 * c1), vw("PP", 0, 32), ACT.Sign, bias=-0.5)
-        bx = vw("BW", 2 * c0, 2 * c0 + 16)
+        pr, x1 = vw("PP", 0, 16), vw("PQ", 0, 16)
+        bank([(pr, vw("AM"), s), (pr, vw("AM"), d), (pr, vw("NAM"), e)])
+        act(bx, pr, ACT.Sign, bias=vw("NTH"))
         scanned = PLAN["scan"][b]
         terms = {"HA": ([], []), "CA": ([], []), "MB": ([], [])}
 
@@ -266,16 +265,9 @@ def trace(T, send, est):
             part(vw("HA", upos, upos + 16), None, vw("WR"), bx)
         for name in ("HA", "CA", "MB"):
             bank(terms[name][0] + terms[name][1])
-        bank(([] if last else [(x1, vw("NID"), vw("TK", 48, 64)), (x1, vw("ID"), s)]) + [(s1, vw("ID2"), s), (s1, vw("ID"), d)]
-             + ([] if last else [(x1, vw("ID"), d), (x1, vw("NID"), e)]) + [(s1, vw("N128"), vw("BW", 2 * c0 + 16, 2 * c1))])
-        base = 2 * S * r + 2 * c0
-        if last:
-            so, land = vw("SOF", c0, c1), vw("SLF", c0, c1)
-            act(so, s1, ACT.Identity, bias=-128.0)
-        else:
-            so, land = vw("SX", base, base + 16), vw("ST", S * (r + 1) + c0, S * (r + 1) + c1)
-            act(vw("SX", base, base + 32), vw("PQ", 0, 32), ACT.Identity, bias=-128.0)
-        add("g", lambda q: send(q, r, b, ap(land), ap(so)), [land], [so], 300, "arr%d" % (3 * r + b), est["remote"])
+        if not last:
+            bank([(x1, vw("ID"), s), (x1, vw("ID"), d), (x1, vw("NID"), e)])
+            act(vw("XN", c0, c1), x1, ACT.Copy)
         span, ad = ((0, 16), (16, 48), (32, 80))[b], (0, 32, 96)[b]
         w = span[1] - span[0]
         if scanned:
@@ -290,8 +282,8 @@ def trace(T, send, est):
         act(vw("AD", ad, ad + w), vw("HA", span[0], span[1]), ACT.Abs, bias=hc, scale=-1.0)
         cn = vw("CN", b, b + 1)
         act(vw("J3", 0, 2 * w), vw("AD", ad, ad + 2 * w), ACT.Relu, bias=BIG, scale=-BIG, acc=cn)
-        ph, pc = b + [x for x, z in PLAN["updates"] if x <= b < z][0], 8 + 2 * b
-        ts(vw("FO", ph, pc + 1, pc - ph), both, cn, vw("TC", b, b + 1), ALU.subtract, ALU.max)
+        slot = b + [x for x, z in PLAN["updates"] if x <= b < z][0]
+        ts(vw("FO", slot, slot + 9, 8), both, cn, vw("TC", b, b + 1), ALU.subtract, ALU.max)
 
     def update(r, b0, b1):
         c0, c1 = 16 * b0, 16 * b1
@@ -304,6 +296,8 @@ def trace(T, send, est):
         tt(cm, m2, cc, ALU.mult)
         tt(go, ind(vw("BF"), off), nm, ALU.mult)
         tt(ind(vw("BF"), off), go, cm, ALU.add)
+        if r < RO - 1:
+            cp(ind(vw("NX"), vw("FO", 8 + 2 * b0, 8 + b0 + b1)), vw("XN", c0, c1))
 
     hash_state(0, 0, 3)
     cp(vw("CU"), ind(vw("BI"), vw("OF")))
@@ -326,10 +320,7 @@ def trace(T, send, est):
                 hash_state(r, b0, b1)
             elif name == "next" and r < RO - 1:
                 hash_state(r + 1, b0, b1)
-            elif name == "move" and r < RO - 1:
-                base = 2 * S * r + 32 * b0 + 16
-                cp(ind(vw("NX"), vw("FO", 8 + 2 * b0, 9 + 2 * b0)), vw("SX", base, base + 16))
-    add("s", lambda q: q.sync.dma_start(T.yb[:], ap(vw("BF", PAD))), [], [vw("BF", PAD)], 60, "o_yb", 3800)
+    add("s", lambda q: q.sync.dma_start(T.yb[:], ap(vw("BF", PAD))), [], [vw("BF", PAD)], 60, "o_yb", 4500)
     add("a", lambda q: q.scalar.dma_start(T.ys[:], ap(vw("SLF"))), [], [vw("SLF")], 60, "o_ys", 2000)
     return ops
 

@@ -10,16 +10,14 @@ C16 = 1.5 * 2.0 ** 27
 
 PLAN = {
     "chunks": "v2a3v3v3a2v3 a3v3v3a3v2v2 a3v3v3a3v2v2",
-    "updates": [(0, 2), (2, 3)], "scan": [True, True, False],
-    "steps": [("cu", 0, 1), ("cf", 0, 1), ("search", 0, 1), ("cu", 1, 2), ("cf", 1, 2), ("search", 1, 2), ("winner", 0, 1), ("hash", 2, 3),
-              ("cu", 2, 3), ("cf", 2, 3), ("search", 2, 3), ("winner", 1, 2), ("update", 0, 2), ("move", 0, 1), ("move", 1, 2),
-              ("next", 0, 1), ("winner", 2, 3), ("next", 1, 2), ("update", 2, 3), ("move", 2, 3)],
-    "starts": [(40.0, 2500.0), (100.0, 5000.0), (60.0, 1000.0)], "passes": 5, "moves": 14000,
+    "steps": [("cu", 0, 1), ("search", 0, 1), ("cu", 1, 2), ("search", 1, 2), ("winner", 0, 1), ("hash", 2, 3), ("cu", 2, 3),
+              ("search", 2, 3), ("winner", 1, 2), ("update", 0, 2), ("next", 0, 1), ("winner", 2, 3), ("next", 1, 2), ("update", 2, 3)],
+    "starts": [(40.0, 2500.0), (100.0, 5000.0), (60.0, 1000.0), (150.0, 2500.0)], "passes": 5, "moves": 14000,
 }
-EST = [{"cyc": 0.9, "pe": 0.46, "hop": 150.0, "gather": 1.56, "scatter": 3.8, "remote": 4300.0, "first": 2000.0, "weight": 1},
-       {"cyc": 0.87, "pe": 0.44, "hop": 200.0, "gather": 1.56, "scatter": 3.8, "remote": 3000.0, "first": 0.0, "weight": 1},
-       {"cyc": 0.87, "pe": 0.44, "hop": 100.0, "gather": 1.8, "scatter": 3.8, "remote": 5300.0, "first": 1500.0, "weight": 1},
-       {"cyc": 1.15, "pe": 0.6, "hop": 120.0, "gather": 1.8, "scatter": 4.5, "remote": 3500.0, "first": 2000.0, "weight": 1}]
+_E = {"cyc": 0.87, "pe": 0.44, "hop": 190.0, "gather": 1.56, "scatter": 3.8, "remote": 3200.0, "first": 500.0, "nx": 6500, "bk": 3800, "weight": 1}
+EST = [dict(_E, nx=5500, bk=3300, weight=2), dict(_E, hop=150.0, remote=4300.0, first=2000.0),
+       dict(_E, cyc=1.2, pe=0.62, gather=1.9, scatter=5.0, hop=220.0, remote=4000.0, first=1500.0),
+       dict(_E, gather=1.15, scatter=2.2, hop=170.0, remote=2600.0, nx=4300, bk=2800)]
 
 SCRATCH = {}
 for _names, _cols, _dt in (
@@ -30,8 +28,8 @@ for _names, _cols, _dt in (
         ("W4", 512, "bfloat16"), ("ZA", 144, "bfloat16"), ("PI PJ", 1, "int32"), ("JR", 64, "float32"), ("J16 QT", 128, "float32"),
         ("PW TWO ZER PWM J1 J2", 16, "float32"), ("SG", 2, "float32"), ("CK", 112, "bfloat16"), ("TC CN", 3, "float32"),
         ("BS DD EE BX XN", S, "bfloat16"), ("OF", 12, "uint16"), ("CU", 192, "uint16"), ("CF AD", 192, "float32"),
-        ("MM", 12, "float32"), ("OQ FO", 16, "uint16"), ("EQ", 384, "bfloat16"), ("SEL", S, "float16"), ("J3 DG", 96, "float32"),
-        ("SEG", 32, "float32")):
+        ("MM", 12, "float32"), ("OQ FO", 16, "uint16"), ("HU", 8, "uint16"), ("EQ", 384, "bfloat16"), ("SEL", S, "float16"),
+        ("J3 DG", 96, "float32"), ("SEG", 32, "float32")):
     for _n in _names.split():
         SCRATCH[_n] = ("sbuf", [128, _cols], _dt)
 for _n in "K0 K1 MB CA HA PP PQ HS".split():
@@ -133,8 +131,8 @@ def trace(T, send, est):
     add("s", lambda q: q.sync.dma_start(ap(vw("PA")), T.pa[:]), [vw("PA")], [], 60, "l_pa", 2000)
     add("s", lambda q: q.sync.dma_start(ap(vw("TH", 0, 1)), T.th[:]), [vw("TH")], [], 60, "l_th", 2000)
     add("s", lambda q: q.sync.dma_start(ap(vw("ST", 0, S)), T.s0[:]), [vw("ST", 0, S)], [], 60, "l_s", 2000)
-    add("a", lambda q: q.scalar.dma_start(ap(vw("BI")), T.bk[:]), [vw("BI")], [], 60, "l_bk", 3800)
-    add("s", lambda q: q.sync.dma_start(ap(vw("NX", PAD)), T.nx[:]), [vw("NX", PAD)], [], 60, "l_nx", 6500)
+    add("a", lambda q: q.scalar.dma_start(ap(vw("BI")), T.bk[:]), [vw("BI")], [], 60, "l_bk", est["bk"])
+    add("s", lambda q: q.sync.dma_start(ap(vw("NX", PAD)), T.nx[:]), [vw("NX", PAD)], [], 60, "l_nx", est["nx"])
 
     ms(vw("ONE"), 1.0)
     iota(vw("PI"), [[0, 1]], 0, 1, small=False)
@@ -239,13 +237,13 @@ def trace(T, send, est):
         ts(oq, r2, r1, 1.0 / 16, ALU.subtract, ALU.mult)
         ts(eq, vw("QI"), r2, m, ALU.add, ALU.is_equal)
         act(cs, ind(vw("CF", 64 * b, 64 * b + 64), oq), ACT.Copy)
-        mk = vw("K%d" % ((3 * r + b) % 2), 64, 80)
+        mk = vw("PQ", 0, 16)
         bank([(mk, eq, vw("I16"))])
         tt(sb, mk, cs, ALU.mult)
-        pr, x1 = vw("PP", 0, 16), vw("PQ", 0, 16)
+        pr, x1 = vw("PP", 0, 16), vw("PP", 16, 32)
         bank([(pr, vw("AM"), s), (pr, vw("AM"), d), (pr, vw("NAM"), e)])
         act(bx, pr, ACT.Sign, bias=vw("NTH"))
-        scanned = PLAN["scan"][b]
+        scanned = b < 2
         terms = {"HA": ([], []), "CA": ([], []), "MB": ([], [])}
 
         def part(out, const, lhs, rhs):
@@ -282,19 +280,24 @@ def trace(T, send, est):
         act(vw("AD", ad, ad + w), vw("HA", span[0], span[1]), ACT.Abs, bias=hc, scale=-1.0)
         cn = vw("CN", b, b + 1)
         act(vw("J3", 0, 2 * w), vw("AD", ad, ad + 2 * w), ACT.Relu, bias=BIG, scale=-BIG, acc=cn)
-        slot = b + [x for x, z in PLAN["updates"] if x <= b < z][0]
+        slot = (0, 1, 4)[b]
         ts(vw("FO", slot, slot + 9, 8), both, cn, vw("TC", b, b + 1), ALU.subtract, ALU.max)
 
     def update(r, b0, b1):
         c0, c1 = 16 * b0, 16 * b1
         y, cc = vw("MB", 64 + c0, 64 + c1), vw("MB", 128 + c0, 128 + c1)
         ry, m2, nm, cm, go = [vw(n, c0, c1) for n in ("RY", "M2", "NM", "CM", "GO")]
-        off = vw("FO", 2 * b0, b0 + b1)
+        off = old = vw("FO", 2 * b0, b0 + b1)
         ts(ry, y, C16, C16, ALU.add, ALU.subtract)
         tt(m2, ry, y, ALU.is_equal)
-        act(nm, m2, ACT.Identity, bias=1.0, scale=-1.0)
+        if b0 == 2:
+            old = vw("HU", 0, 1)
+            tt(nm, ry, y, ALU.not_equal)
+            cp(old, vw("VC", 2, 3))
+        else:
+            act(nm, m2, ACT.Identity, bias=1.0, scale=-1.0)
         tt(cm, m2, cc, ALU.mult)
-        tt(go, ind(vw("BF"), off), nm, ALU.mult)
+        tt(go, ind(vw("BF"), old), nm, ALU.mult)
         tt(ind(vw("BF"), off), go, cm, ALU.add)
         if r < RO - 1:
             cp(ind(vw("NX"), vw("FO", 8 + 2 * b0, 8 + b0 + b1)), vw("XN", c0, c1))
@@ -308,7 +311,6 @@ def trace(T, send, est):
             cur[0] = name + str(b0)
             if name == "cu" and r > 0:
                 cp(vw("CU", 64 * b0, 64 * b1), ind(vw("BF"), vw("OF", 4 * b0, 4 * b1)))
-            elif name == "cf" and r > 0:
                 ts(vw("CF", 64 * b0, 64 * b1), vw("CU", 64 * b0, 64 * b1), -1536.0, None, ALU.add)
             elif name == "search":
                 search(r, b0)
@@ -422,7 +424,7 @@ def plan(T):
             if best is None or score < best[0]:
                 best = (score, order)
             prio = greedy(eng, cost, back, end, slack, [0.0 if back[i] else lat[i] for i in range(n)])[1]
-    state = [1]
+    state = [2]
 
     def rnd(k):
         state[0] = (state[0] * 6364136223846793005 + 1442695040888963407) % (1 << 64)

@@ -4,42 +4,58 @@ from concourse.mybir import AluOpType, AxisListType, ActivationFunctionType
 ALU, ACT = AluOpType, ActivationFunctionType
 V, KB, S, RO = 3072, 1024, 48, 3
 PAD = 64
-BIG = 8192.0
-C2048 = 1.5 * 2.0 ** 34
-C16 = 1.5 * 2.0 ** 27
+MID = 1536.0
+B = 4096.0
+C16B = 1.5 * 2.0 ** 39
+C256 = 1.5 * 2.0 ** 31
+PARTS = {0: (0, 1, 2, 3, 4), 2: (0, 1, 3, 4, 2)}
+SLOT = 24
 
 PLAN = {
-    "chunks": "v2a3v3v3a2v3 a3v3v3a3v2v2 a3v3v3a3v2v2",
-    "steps": [("cu", 0, 1), ("search", 0, 1), ("cu", 1, 2), ("search", 1, 2), ("winner", 0, 1), ("hash", 2, 3), ("cu", 2, 3),
-              ("search", 2, 3), ("winner", 1, 2), ("update", 0, 2), ("next", 0, 1), ("winner", 2, 3), ("next", 1, 2), ("update", 2, 3)],
-    "starts": [(40.0, 2500.0), (100.0, 5000.0), (60.0, 1000.0), (150.0, 2500.0)], "passes": 5, "moves": 14000,
+    "chunks": "a2v2a3v3v3v3 a6v3v3v2v2 a5v3v2v2v2v2",
+    "steps": [("recv", 0), ("cu", 0), ("search", 0), ("recv", 1), ("cu", 1), ("search", 1), ("winner", 0), ("move", 0), ("name", 0),
+              ("stand", 0), ("recv", 2), ("cu", 2), ("search", 2), ("winner", 1), ("move", 1), ("name", 1), ("place", 0), ("stand", 1),
+              ("update", 0), ("winner", 2), ("move", 2), ("name", 2), ("place", 2), ("stand", 2), ("update", 2)],
+    "countv": 0, "roundv": True, "joint": False,
+    "v": "CU0 ST0 XG0.1 XG0.3-5 CU1 ST1 XG1.1 R10 UU0 XG1.2 OO0 XG1.3 GG0 GE0 XG1.4 CU2 ST2 CF0 OQ0 XG2.1 SO0 XG2.2 R11 UU1 XG2.3 OO1 "
+         "XG2.4 GG1 GE1 XG2.5 SB0 OQ1 CF1 CF2 ZZ0 SO1 R12 UU2 SB1 OO2 OQ2 FO0 GG2 GE2 ZZ1 RC20 SB2 FO1 SO2 GO0 RB2 BF0 HU2 ZZ2 UL2 NX0 "
+         "FO2 GO2 BF2 NX2",
+    "a": "XG0.0 XG0.2 AB0.0-3 SC0 AB0.4-15 XG1.0 AB1.6-8 SC1 AB1.0-5 AB1.9-11 BS0 SOF0 AB1.12-15 XG2.0 LB0.0-1 AB2.5-7 AB2.0-2 CS0 "
+         "AB2.3-4 SC2 AB2.8-13 BS1 SOF1 AB2.14-15 CS1 LB1.0-1 CS2 LB2.0-1 BS2 SOF2 UL0",
+    "slacks": (0.0, 20.0, 60.0), "passes": 3, "moves": 50000, "heat": 25.0, "seed": 2,
 }
 _E = {"cyc": 0.87, "pe": 0.44, "hop": 190.0, "gather": 1.56, "scatter": 3.8, "remote": 3200.0, "first": 500.0, "nx": 6500, "bk": 3800, "weight": 1}
-EST = [dict(_E, nx=5500, bk=3300, weight=2), dict(_E, hop=150.0, remote=4300.0, first=2000.0),
-       dict(_E, cyc=1.2, pe=0.62, gather=1.9, scatter=5.0, hop=220.0, remote=4000.0, first=1500.0),
-       dict(_E, gather=1.15, scatter=2.2, hop=170.0, remote=2600.0, nx=4300, bk=2800)]
+EST = [dict(_E, nx=4500, bk=3000, weight=2), dict(_E, hop=150.0, remote=4300.0, first=2000.0, nx=5500),
+       dict(_E, cyc=1.2, pe=0.62, gather=1.9, scatter=5.0, hop=220.0, remote=4000.0, first=1500.0, nx=5000),
+       dict(_E, gather=1.15, scatter=2.2, hop=170.0, remote=2600.0, nx=4000, bk=2800)]
 
 SCRATCH = {}
 for _names, _cols, _dt in (
         ("NX", PAD + V, "bfloat16"), ("BI", KB, "int32"), ("BF", PAD + KB, "float32"), ("ST", RO * S, "bfloat16"),
-        ("SO", (RO - 1) * S, "bfloat16"), ("SOF SLF YY YW CS RY M2 NM CM GO", S, "float32"), ("PA I16", 16, "bfloat16"), ("TH", 4, "int32"),
-        ("NTH AC", 1, "float32"), ("WC", 4, "float32"), ("XG AB", V, "bfloat16"),
-        ("ONE BM0 BM ID NID AM NAM WR QI LOW", 128, "bfloat16"), ("BMH", 128, "float16"), ("GM VC", 8, "float32"),
-        ("W4", 512, "bfloat16"), ("ZA", 144, "bfloat16"), ("PI PJ", 1, "int32"), ("JR", 64, "float32"), ("J16 QT", 128, "float32"),
-        ("PW TWO ZER PWM J1 J2", 16, "float32"), ("SG", 2, "float32"), ("CK", 112, "bfloat16"), ("TC CN", 3, "float32"),
-        ("BS DD EE BX XN", S, "bfloat16"), ("OF", 12, "uint16"), ("CU", 192, "uint16"), ("CF AD", 192, "float32"),
-        ("MM", 12, "float32"), ("OQ FO", 16, "uint16"), ("HU", 8, "uint16"), ("EQ", 384, "bfloat16"), ("SEL", S, "float16"),
-        ("J3 DG", 96, "float32"), ("SEG", 32, "float32")):
+        ("SO LD", (RO - 1) * 3 * SLOT, "uint16"), ("SOF SLF ORD", S, "float32"), ("PA I16", 16, "bfloat16"), ("TH", 4, "int32"),
+        ("AC", 1, "float32"), ("WC EV OCT", 4, "float32"), ("XG AB", V, "bfloat16"),
+        ("ONE BM0 BM ID NID NID256 AM NAM NAM256 BMB NBMB", 128, "bfloat16"), ("GM NN OC ZZ TC", 8, "float32"),
+        ("W4", 140, "bfloat16"), ("ZA LB2", 144, "bfloat16"), ("PI PJ", 1, "int32"), ("JR J16", 64, "float32"),
+        ("PW TWO ZER PWM", 16, "float32"), ("SG", 2, "float32"), ("CKS BS GE", S, "bfloat16"),
+        ("IDT", 192, "bfloat16"), ("DL", 67, "float32"), ("MK", 297, "bfloat16"), ("CKA", 160, "bfloat16"), ("CKB", 80, "bfloat16"),
+        ("RC", 50, "bfloat16"), ("LB", 146, "bfloat16"), ("SB GG", 144, "float16"), ("KK", 32, "float32"),
+        ("OF", 12, "uint16"), ("CU", 192, "uint16"), ("CF SC", 192, "float32"), ("CS", 144, "float32"),
+        ("R1", 3, "float32"), ("UU", 3 * 68, "float32"), ("OO", 24, "uint16"), ("OQ FO", 16, "uint16"), ("HU", 2, "uint16"),
+        ("RA", 64, "float32"), ("RC2", 64, "bfloat16"), ("UL", 144, "float32"), ("AD", 192, "float32"), ("RB GO", S, "float32")):
     for _n in _names.split():
         SCRATCH[_n] = ("sbuf", [128, _cols], _dt)
-for _n in "K0 K1 MB CA HA PP PQ HS".split():
+for _n in "K0 K1 PR SD PS GA GB UA".split():
     SCRATCH[_n] = ("psum", [128, 512], "float32")
 SEMAPHORES = (["e_t", "e_v", "e_a", "e_g", "sent", "l_pa", "l_th", "l_s", "l_nx", "l_bk", "o_ys", "o_yb"]
               + ["arr%d" % i for i in range(RO * 3)])
 
 
 def vw(name, c0=0, c1=None, step=1):
-    return (name, c0, SCRATCH[name][1][1] if c1 is None else c1, step)
+    return (name, c0, SCRATCH[name][1][1] if c1 is None else c1, step, 0, 128)
+
+
+def rows(v, q):
+    return v[:4] + (32 * q, 32 * q + 32)
 
 
 def width(v):
@@ -47,12 +63,12 @@ def width(v):
 
 
 def trace(T, send, est):
-    ops, cur, cyc = [], ["setup"], est["cyc"]
+    ops, cur, cyc, groups = [], ["setup", 0], est["cyc"], {}
 
     def ap(v):
         if v[0] == "ind":
             return ap(v[1]).indirect(ap(v[2]))
-        return T[v[0]][:, v[1]:v[2]:v[3]] if v[3] != 1 else T[v[0]][:, v[1]:v[2]]
+        return T[v[0]][v[4]:v[5], v[1]:v[2]:v[3]] if v[3] != 1 else T[v[0]][v[4]:v[5], v[1]:v[2]]
 
     def sc(x):
         return ap(x) if isinstance(x, tuple) else x
@@ -67,7 +83,7 @@ def trace(T, send, est):
                 wr.append(v[1]); rd.append(v[2])
             else:
                 wr.append(v)
-        ops.append({"eng": eng, "fn": fn, "rd": rd, "wr": wr, "cost": cost, "sem": sem, "lat": lat, "cls": cur[0]})
+        ops.append({"eng": eng, "fn": fn, "rd": rd, "wr": wr, "cost": cost, "sem": sem, "lat": lat, "cls": cur[0], "round": cur[1]})
 
     def ind(win, off):
         return ("ind", win, off)
@@ -89,7 +105,8 @@ def trace(T, send, est):
         add("v", fn, [out], [a, s1, s2], vcost(out, a))
 
     def tt(out, a, b, op):
-        add("v", lambda q: q.vector.tensor_tensor(ap(out), ap(a), ap(b), op), [out], [a, b], vcost(out, a, 2.0))
+        per = 1.0 if a[0] != "ind" and SCRATCH[a[0]][0] == "psum" else 2.0
+        add("v", lambda q: q.vector.tensor_tensor(ap(out), ap(a), ap(b), op), [out], [a, b], vcost(out, a, per))
 
     def cp(out, a):
         add("v", lambda q: q.vector.tensor_copy(ap(out), ap(a)), [out], [a], vcost(out, a))
@@ -97,8 +114,12 @@ def trace(T, send, est):
     def ms(out, val):
         add("v", lambda q: q.vector.memset(ap(out), val), [out], [], vcost(out, out))
 
-    def red(out, a, op):
-        add("v", lambda q: q.vector.tensor_reduce(ap(out), ap(a), AxisListType.X, op), [out], [a], vcost(out, a, 1.0))
+    def red(out, a, op, absolute=False):
+        if absolute:
+            fn = lambda q: q.vector.tensor_reduce(ap(out), ap(a), AxisListType.X, op, apply_absolute_value=True)
+        else:
+            fn = lambda q: q.vector.tensor_reduce(ap(out), ap(a), AxisListType.X, op)
+        add("v", fn, [out], [a], vcost(out, a, 1.0))
 
     def scan(out, d0, d1, init, op0, op1):
         add("v", lambda q: q.vector.tensor_tensor_scan(ap(out), ap(d0), ap(d1), init, op0, op1), [out], [d0, d1], vcost(out, d0, 1.0))
@@ -111,12 +132,16 @@ def trace(T, send, est):
         cost = (78 + 16 * width(a[2]) * est["gather"] if a[0] == "ind" else max(66, width(a))) * cyc
         add("a", fn, [out] + ([acc] if acc else []), [a, bias, scale], cost + (20 if acc else 0))
 
-    def mm(out, lhs, rhs, start, stop):
-        add("t", lambda q: q.tensor.matmul(ap(out), ap(lhs), ap(rhs), start, stop), [out], [lhs, rhs], 64 * est["pe"])
+    def mm(out, lhs, rhs, start=False, stop=False, pin=False):
+        ends = [start, stop]
+        add("t", lambda q: q.tensor.matmul(ap(out), ap(lhs), ap(rhs), ends[0], ends[1]), [out], [lhs, rhs],
+            max(min(64, width(lhs)), width(rhs)) * est["pe"])
+        groups[out[0]] = groups.get(out[0], 0) + start
+        ops[-1].update(group=(out[0], groups[out[0]]), ends=ends, first=pin and start, last=pin and stop, wide=rhs[0][:2] == "CK")
 
-    def bank(terms):
+    def bank(terms, start=True, stop=True):
         for i, (out, lhs, rhs) in enumerate(terms):
-            mm(out, lhs, rhs, i == 0, i == len(terms) - 1)
+            mm(out, lhs, rhs, start and i == 0, stop and i == len(terms) - 1)
 
     def iota(out, pattern, base, mult, small=True):
         if small:
@@ -134,71 +159,106 @@ def trace(T, send, est):
     add("a", lambda q: q.scalar.dma_start(ap(vw("BI")), T.bk[:]), [vw("BI")], [], 60, "l_bk", est["bk"])
     add("s", lambda q: q.sync.dma_start(ap(vw("NX", PAD)), T.nx[:]), [vw("NX", PAD)], [], 60, "l_nx", est["nx"])
 
+    ID, BM, AM, AC = vw("ID"), vw("BM"), vw("AM"), vw("AC")
     ms(vw("ONE"), 1.0)
     iota(vw("PI"), [[0, 1]], 0, 1, small=False)
-    iota(vw("JR"), [[1, 64]], 0, 0)
+    iota(vw("J16"), [[0, 4], [1, 16]], 0, 0)
     sel(vw("BM0"), vw("ONE"), [[-16, 8], [0, 16]], ALU.is_ge, 0, 1)
-    sel(vw("BM"), vw("BM0"), [[16, 8], [0, 16]], ALU.is_ge, 15, -1)
-    sel(vw("ID"), vw("ONE"), [[-1, 128]], ALU.is_equal, 0, 1)
-    iota(vw("J16"), [[0, 8], [1, 16]], 0, 0)
+    sel(BM, vw("BM0"), [[16, 8], [0, 16]], ALU.is_ge, 15, -1)
+    sel(ID, vw("ONE"), [[-1, 128]], ALU.is_equal, 0, 1)
+    iota(vw("JR"), [[16, 64]], 0, 0)
+    iota(vw("ORD"), [[128, 16], [2048, 3]], 64, 0)
+    iota(vw("CKS", 0, 32), [[-24, 2], [0, 16]], 12, 0)
+    iota(vw("CKS", 32, 48), [[0, 16]], 256, 0)
     ts(vw("PJ"), vw("PI"), 15, None, ALU.bitwise_and)
-    cp(vw("AC"), vw("PJ"))
-    ts(vw("I16"), vw("JR", 0, 16), vw("AC"), None, ALU.is_equal)
+    cp(AC, vw("PJ"))
+    ts(vw("IDT", 128, 192), vw("J16"), AC, None, ALU.is_equal)
+    i16 = vw("IDT", 128, 144)
     ms(vw("TWO"), 2.0); ms(vw("ZER"), 0.0)
     scan(vw("PW"), vw("TWO"), vw("ZER"), 0.25, ALU.mult, ALU.add)
     ms(vw("PW", 10, 11), -(512.0 + PAD)); ms(vw("PW", 11, 12), 0.5); ms(vw("PW", 12, 16), 0.0)
-    tt(vw("PWM"), vw("PW"), vw("I16"), ALU.mult)
+    tt(vw("PWM"), vw("PW"), i16, ALU.mult)
     red(vw("WC", 0, 1), vw("PWM"), ALU.add)
-    ts(vw("SG"), vw("I16", 0, 2), -2.0, 1.0, ALU.mult, ALU.add)
+    ts(vw("SG"), vw("IDT", 128, 130), -2.0, 1.0, ALU.mult, ALU.add)
     ts(vw("WC", 1, 3), vw("SG"), vw("WC", 0, 1), None, ALU.mult)
     ts(vw("WC", 3, 4), vw("WC", 1, 2), vw("SG", 1, 2), None, ALU.mult)
     ms(vw("W4"), 0.0)
     cp(vw("GM"), vw("BM", 0, 128, 16))
     for gg in range(8):
-        act(vw("AM", 16 * gg, 16 * gg + 16), vw("PA"), ACT.Copy, scale=vw("GM", gg, gg + 1))
-    ts(vw("NTH"), vw("TH", 0, 1), -1.0, -0.5, ALU.mult, ALU.add)
-    for aa in range(4):
-        for k in range(4):
-            o = vw("W4", 128 * aa + 4 * aa + k, 128 * (aa + 1), 16)
-            if k % 2:
-                act(o, vw("GM"), ACT.Copy, scale=vw("WC", k, k + 1))
-            else:
-                ts(o, vw("GM"), vw("WC", k, k + 1), None, ALU.mult)
+        if gg % 2:
+            act(vw("AM", 16 * gg, 16 * gg + 16), vw("PA"), ACT.Copy, scale=vw("GM", gg, gg + 1))
+        else:
+            ts(vw("AM", 16 * gg, 16 * gg + 16), vw("PA"), vw("GM", gg, gg + 1), None, ALU.mult)
+    nth = vw("NN", 1, 2)
+    ts(nth, vw("TH", 0, 1), -1.0, -0.5, ALU.mult, ALU.add)
+    for k in range(4):
+        if k % 2:
+            act(vw("W4", 12 + k, 140, 16), vw("GM"), ACT.Copy, scale=vw("WC", k, k + 1))
+        else:
+            ts(vw("W4", 12 + k, 140, 16), vw("GM"), vw("WC", k, k + 1), None, ALU.mult)
     ms(vw("ZA"), 0.0)
-    ts(vw("ZA", 15, 143, 16), vw("GM"), 2048.0, None, ALU.mult)
-    ts(vw("LOW", 0, 64), vw("JR"), -7.5, None, ALU.add)
-    ts(vw("LOW", 64, 128), vw("ONE", 0, 64), vw("AC"), 64.0, ALU.mult, ALU.mult)
-    act(vw("NAM"), vw("AM"), ACT.Copy, scale=-1.0)
-    act(vw("NID"), vw("ID"), ACT.Copy, scale=-1.0)
-    act(vw("WR"), vw("BM"), ACT.Copy, scale=vw("WC", 0, 1))
-    cp(vw("BMH"), vw("BM"))
-    ts(vw("QT"), vw("J16"), -107.5, None, ALU.add)
-    tt(vw("QT"), vw("QT"), vw("BM"), ALU.mult)
-    ts(vw("QI"), vw("QT"), 100.0, None, ALU.add)
-    j16 = vw("JR", 0, 16)
-    CKH_M, CKH_D, CKC_M, CKC_D, CK_U, CK_Y, CK_C = [vw("CK", 16 * i, 16 * i + 16) for i in range(7)]
-    ts(CKH_M, j16, vw("AC"), BIG, ALU.is_ge, ALU.mult)
-    ts(CKH_D, vw("I16"), BIG, -BIG, ALU.mult, ALU.add)
-    ts(CKC_M, CKH_M, 1536.0 + PAD, None, ALU.max)
-    ts(CKC_D, vw("I16"), BIG + 1536.0 + PAD, -BIG, ALU.mult, ALU.add)
-    ms(CK_U, 1536.0 + PAD); ms(CK_C, 1536.0)
-    ts(CK_Y, j16, vw("AC"), None, ALU.subtract)
-    ts(vw("TC"), vw("JR", 0, 48, 16), vw("AC"), None, ALU.add)
-    ms(vw("BF", 0, PAD), 0.0)
-    ms(vw("SEG"), 1.0); ms(vw("SEG", 0, 32, 16), 0.0)
+    act(vw("ZA", 15, 143, 16), vw("GM"), ACT.Copy, scale=64.0)
+    red(vw("EV", 0, 1), vw("GM", 0, 8, 2), ALU.add)
+    red(vw("EV", 1, 2), vw("GM", 1, 8, 2), ALU.add)
+    for name, src, f in (("NAM", AM, -1.0), ("NAM256", AM, -256.0), ("NID", ID, -1.0), ("NID256", ID, -256.0), ("BMB", BM, B), ("NBMB", BM, -B)):
+        act(vw(name), src, ACT.Copy, scale=f)
+    for k in range(2):
+        act(vw("IDT", 64 * k, 64 * k + 64), vw("IDT", 128, 192), ACT.Copy, scale=vw("EV", k, k + 1))
 
-    def hash_state(r, b0, b1):
-        n = 16 * (b1 - b0)
-        bank([(vw("HS", 0, n), vw("AM"), vw("ST", S * r + 16 * b0, S * r + 16 * b1))])
-        act(vw("BS", 16 * b0, 16 * b1), vw("HS", 0, n), ACT.Sign, bias=vw("NTH"))
-        ho = vw("HS", 64 + 4 * b0, 64 + 4 * b1)
-        bank([(ho, vw("W4", 128 * aa, 128 * aa + 128), vw("BS", 16 * b0 + aa, 16 * b1, 4)) for aa in range(4)])
-        ts(vw("OF", 4 * b0, 4 * b1), ho, -float(PAD) if r == 0 else 0.0, None, ALU.add)
+    def first_hash():
+        bank([(vw("PR", 0, S), AM, vw("ST", 0, S))])
+        act(vw("BS"), vw("PR", 0, S), ACT.Sign, bias=nth)
+        bank([(vw("SD", 0, 12), vw("W4", 12 - 4 * aa, 140 - 4 * aa), vw("BS", aa, S, 4)) for aa in range(4)])
+        ts(vw("OF"), vw("SD", 0, 12), -float(PAD), None, ALU.add)
+        cp(vw("CU", 0, 64), ind(vw("BI"), vw("OF", 0, 4)))
+        cp(vw("CU", 64, 192), ind(vw("BI"), vw("OF", 4, 12)))
+        ts(vw("CF"), vw("CU"), -MID, None, ALU.add)
+
+    first_hash()
+    sel(vw("BF", PAD), vw("BI"), [[0, KB]], ALU.is_ge, 0, 0)
+    bank([(vw("UA", 0, 1), AM, vw("ONE", 0, 1))])
+    ts(vw("NN", 0, 1), vw("UA", 0, 1), -12.0, nth, ALU.mult, ALU.add)
+    act(vw("EV", 2, 4), vw("EV", 0, 2), ACT.Copy, scale=vw("NN", 0, 1))
+    ms(vw("DL", 0, 64), -1.0); ms(vw("DL", 65, 67), 0.0)
+    ts(vw("DL", 64, 65), AC, 64.0, 55.5, ALU.mult, ALU.add)
+    ts(vw("OC", 0, 4), vw("ONE", 0, 4), vw("DL", 64, 65), 7.5, ALU.mult, ALU.add)
+    act(vw("OC", 4, 7), vw("JR", 0, 12, 4), ACT.Identity, bias=63.0)
+    ms(vw("K0", 64, 67), 2.0 ** 20); ms(vw("K1", 64, 67), 2.0 ** 20)
+    act(vw("TC", 0, 3), vw("JR", 0, 3), ACT.Identity, bias=AC)
+    act(vw("TC", 3, 6), vw("TC", 0, 3), ACT.Copy, scale=128.0)
+    act(vw("OCT", 0, 3), vw("TC", 0, 3), ACT.Copy, scale=-128.0 * 64)
+    ms(vw("MK", 0, 297, 99), 0.0); ms(vw("MK", 97, 297, 99), 1.0); ms(vw("MK", 98, 297, 99), MID + PAD)
+    for b in range(3):
+        ts(vw("MK", 99 * b + 1, 99 * b + 49), vw("ORD"), vw("TC", 3 + b, 4 + b), -16.0, ALU.subtract, ALU.max)
+        act(vw("MK", 99 * b + 49, 99 * b + 97), vw("ORD"), ACT.Relu, bias=vw("OCT", b, b + 1), scale=64.0)
+    ms(vw("RC", 0, 48), -1.0)
+    act(vw("RC", 48, 50), vw("J16", 0, 2), ACT.Copy)
+    ts(vw("KK"), vw("J16", 0, 32), AC, None, ALU.subtract)
+    for name, w, places in (("CKA", 32, PARTS[0]), ("CKB", 16, PARTS[2])):
+        for k, (f, c) in zip(places, ((B, -7.5 * B), (-B, 7.5 * B), (B, 0.0), (-B, MID), (0.0, -12.0))):
+            act(vw(name, k * w, k * w + w), vw("KK", 0, w), ACT.Identity, bias=c, scale=f)
+    ms(vw("LB", 1, 97), 0.0)
+    act(vw("LB", 0, 1), vw("WC", 0, 1), ACT.Copy)
+    ms(vw("RB", 0, 16), 0.0)
+    for b in range(3):
+        act(vw("SC", 64 * b, 64 * b + 16), vw("ZER"), ACT.Copy)
+    ms(vw("BF", 0, PAD), 0.0)
+
+    def state(r, b):
+        return vw("ST", S * r + 16 * b, S * r + 16 * b + 16)
+
+    def slot(name, r, b, c0, c1):
+        return vw(name, SLOT * (3 * r + b) + c0, SLOT * (3 * r + b) + c1)
+
+    def recv(r, b):
+        s = state(r, b)
+        if r > 0:
+            cp(s, slot("LD", r - 1, b, 0, 16))
+        bank([(vw("PR", 0, 48), ID, vw("CKS")), (vw("PR", 0, 16), ID, s), (vw("PR", 16, 32), ID, s), (vw("PR", 32, 48), vw("NID"), s)])
+        act(vw("SC", 64 * b + 16, 64 * b + 64), vw("PR", 0, 48), ACT.Copy)
 
     def search(r, b):
         key = vw("K%d" % ((3 * r + b) % 2), 0, 64)
-        mm(key, vw("ID"), vw("LOW", 0, 64), True, False)
-        mm(key, vw("ID"), vw("LOW", 64, 128), False, False)
         spec, a0 = PLAN["chunks"].split()[b], 0
         for eng, n in zip(spec[0::2], map(int, spec[1::2])):
             t0 = 16 * b + a0
@@ -211,135 +271,163 @@ def trace(T, send, est):
                 t = 16 * b + a
                 d = vw("AB", 64 * t, 64 * t + 64)
                 act(d, vw("XG", 64 * t, 64 * t + 64), ACT.Abs, bias=vw("ST", S * r + t, S * r + t + 1), scale=-1.0)
-                mm(key, vw("ZA", 15 - a, 143 - a), d, False, a == 15)
+                mm(key, vw("ZA", 15 - a, 143 - a), d, a == 0, a == 15)
             a0 += n
-        red(vw("MM", b, b + 1), key, ALU.min)
+
+    def conflict_bank(b):
+        return ("GB" if b == 1 else "GA", 0)
+
+    def part(r, b, k):
+        if b == 2:
+            c0, ub = 128 + 16 * PARTS[2][k], "K%d" % ((r + 1) % 2)
+        else:
+            c0, ub = (256 + 32 * k + 16 * b, "GB") if k < 2 else (32 * (k - 2) + 16 * b, "UA")
+        return vw(ub, c0, c0 + 16)
 
     def winner(r, b):
-        last, c0, c1 = r == RO - 1, 16 * b, 16 * b + 16
-        s = vw("ST", S * r + c0, S * r + c1)
-        d, e, sb, cs, yy, ww, bx = [vw(n, c0, c1) for n in ("DD", "EE", "SEL", "CS", "YY", "YW", "BX")]
-        eq, m, r1, r2 = vw("EQ", 128 * b, 128 * b + 128), vw("MM", b, b + 1), vw("MM", 4 + b, 5 + b), vw("MM", 8 + b, 9 + b)
-        o1, oq = vw("OQ", 2 * b, 2 * b + 1), vw("OQ", 8 + 2 * b, 9 + 2 * b)
-        ts(r1, m, C2048, C2048, ALU.add, ALU.subtract)
-        ts(o1, m, r1, 7.5, ALU.subtract, ALU.add)
-        ts(r2, m, C16, C16, ALU.add, ALU.subtract)
-        win = ind(vw("XG", 1024 * b, 1024 * b + 1024), o1)
-        so = vw("SOF", c0, c1) if last else vw("SO", S * r + c0, S * r + c1)
-        land = vw("SLF", c0, c1) if last else vw("ST", S * (r + 1) + c0, S * (r + 1) + c1)
-        tt(yy, win, s, ALU.add)
-        ts(ww, yy, 256.0, -256.0, ALU.is_ge, ALU.mult)
-        tt(so, yy, ww, ALU.add)
+        last, kb = r == RO - 1, "K%d" % ((3 * r + b) % 2)
+        s, r1, u = state(r, b), vw("R1", b, b + 1), 68 * b
+        red(r1, vw(kb, 0, 64), ALU.min)
+        scan(vw("UU", u, u + 67), vw("DL"), vw(kb, 0, 67), 2.0 ** 21, ALU.add, ALU.min)
+        ts(vw("OO", 8 * b, 8 * b + 7), vw("OC", 0, 7), vw("UU", u + 63, u + 64), r1, ALU.add, ALU.subtract)
+        xg = vw("XG", 1024 * b, 1024 * b + 1024)
+        tt(vw("GG", 48 * b, 48 * b + 48), ind(xg, vw("OO", 8 * b, 8 * b + 3)), vw("SC", 64 * b, 64 * b + 48), ALU.max)
+        m0, m1, m2 = [vw("GG", 48 * b + 16 * k, 48 * b + 16 * k + 16) for k in range(3)]
+        ge = vw("GE", 16 * b, 16 * b + 16)
+        tt(ge, ind(xg, vw("OO", 8 * b, 8 * b + 1)), vw("SC", 64 * b + 48, 64 * b + 64), ALU.is_ge)
+        sv, ps = vw("SD", 0, 16), vw("PS", 0, 16)
+        bank([(sv, ID, s), (sv, ID, m0), (sv, vw("NID256"), ge)], stop=last)
+        if last:
+            so, land = vw("SOF", 16 * b, 16 * b + 16), vw("SLF", 16 * b, 16 * b + 16)
+            act(so, sv, ACT.Copy)
+        else:
+            bank([(ps, AM, s), (ps, AM, m0), (ps, vw("NAM256"), ge)])
+            act(vw("BS", 16 * b, 16 * b + 16), ps, ACT.Sign, bias=nth)
+            bank([(vw("SD", 16, 20), vw("W4", 12 - 4 * aa, 140 - 4 * aa), vw("BS", 16 * b + aa, 16 * b + 16, 4)) for aa in range(4)], start=False)
+            so, land = slot("SO", r, b, 0, 20), slot("LD", r, b, 0, 20)
+            cp(so, vw("SD", 0, 20))
         add("g", lambda q: send(q, r, b, ap(land), ap(so)), [land], [so], 300, "arr%d" % (3 * r + b),
             est["remote"] + (est["first"] if r == 0 and b < 2 else 0.0))
-        tt(d, win, s, ALU.subtract)
-        ts(e, d, -12.0, 12.0, ALU.max, ALU.min)
-        ts(oq, r2, r1, 1.0 / 16, ALU.subtract, ALU.mult)
-        ts(eq, vw("QI"), r2, m, ALU.add, ALU.is_equal)
-        act(cs, ind(vw("CF", 64 * b, 64 * b + 64), oq), ACT.Copy)
-        mk = vw("PQ", 0, 16)
-        bank([(mk, eq, vw("I16"))])
-        tt(sb, mk, cs, ALU.mult)
-        pr, x1 = vw("PP", 0, 16), vw("PP", 16, 32)
-        bank([(pr, vw("AM"), s), (pr, vw("AM"), d), (pr, vw("NAM"), e)])
-        act(bx, pr, ACT.Sign, bias=vw("NTH"))
-        scanned = b < 2
-        terms = {"HA": ([], []), "CA": ([], []), "MB": ([], [])}
 
-        def part(out, const, lhs, rhs):
-            if const is not None:
-                terms[out[0]][0].append((out, vw("ID"), const))
-            terms[out[0]][1].append((out, lhs, rhs))
-
-        mpos, upos = (0, 16, 64)[b], (32, 48, None)[b]
-        part(vw("MB", 64 + c0, 64 + c1), CK_Y, vw("BMH"), sb)
-        part(vw("MB", 128 + c0, 128 + c1), CK_C, vw("BMH"), sb)
-        part(vw("MB", 208, 224) if scanned else vw("CA", 80, 96), CKC_D, vw("BMH"), sb)
-        part(vw("MB", 192, 208) if scanned else vw("HA", 80, 96), CKH_D, vw("WR"), bx)
-        part(vw("CA", mpos, mpos + 16), CKC_M, vw("BMH"), sb)
-        part(vw("HA", mpos, mpos + 16), CKH_M, vw("WR"), bx)
-        if upos is not None:
-            part(vw("CA", upos, upos + 16), CK_U, vw("BMH"), sb)
-            part(vw("HA", upos, upos + 16), None, vw("WR"), bx)
-        for name in ("HA", "CA", "MB"):
-            bank(terms[name][0] + terms[name][1])
+    def move(r, b):
+        last = r == RO - 1
+        m0, m1, m2 = [vw("GG", 48 * b + 16 * k, 48 * b + 16 * k + 16) for k in range(3)]
+        pr = vw("PR", 0, 16)
+        bank([(pr, AM, m0), (pr, AM, m1), (pr, vw("NAM"), m2)])
+        for k in range(2):
+            act(vw("LB", 1 + 48 * k + b, 49 + 48 * k, 3), pr, ACT.Sign, bias=vw("EV", 2 + k, 3 + k), scale=vw("EV", k, k + 1))
+        gb, g0 = conflict_bank(b)
+        if b != 1:
+            mm(vw(gb, 0, 99), ID, vw("MK", 99 * b, 99 * b + 99), True, pin=True)
+        if b == 0:
+            mm(vw("GB", 0, 99), ID, vw("MK", 99, 198), True, pin=True)
+        for q in range(4):
+            lhs = rows(vw("LB", 1 + b, 97, 3), q)
+            mm(rows(vw(gb, g0, g0 + 49), q), lhs, rows(vw("LB", 0, 49), q))
+            mm(rows(vw(gb, g0 + 1, g0 + 49), q), lhs, rows(vw("LB", 49, 97), q))
+        if b == 0:
+            mm(vw("GB", 256, 320), ID, vw("CKA", 0, 64))
+            mm(vw("UA", 0, 96), ID, vw("CKA", 64, 160), True)
+        if b == 2:
+            mm(vw(part(r, b, 0)[0], 128, 208), ID, vw("CKB"), True)
         if not last:
-            bank([(x1, vw("ID"), s), (x1, vw("ID"), d), (x1, vw("NID"), e)])
-            act(vw("XN", c0, c1), x1, ACT.Copy)
-        span, ad = ((0, 16), (16, 48), (32, 80))[b], (0, 32, 96)[b]
-        w = span[1] - span[0]
-        if scanned:
-            scan(vw("DG", 2 * c0, 2 * c1), vw("SEG"), vw("MB", 192, 224), 0.0, ALU.mult, ALU.max)
-            hc, cc, both = vw("DG", 32 * b + 15, 32 * b + 16), vw("DG", 32 * b + 31, 32 * b + 32), vw("DG", 32 * b + 15, 32 * b + 32, 16)
-        else:
-            hc, cc, both = vw("VC", b, b + 1), vw("VC", 4 + b, 5 + b), vw("VC", b, b + 5, 4)
-            act(vw("J2"), vw("CA", 80, 96), ACT.Relu, acc=cc)
-        act(vw("AD", ad + w, ad + 2 * w), vw("CA", span[0], span[1]), ACT.Abs, bias=cc, scale=-1.0)
-        if not scanned:
-            act(vw("J1"), vw("HA", 80, 96), ACT.Relu, acc=hc)
-        act(vw("AD", ad, ad + w), vw("HA", span[0], span[1]), ACT.Abs, bias=hc, scale=-1.0)
-        cn = vw("CN", b, b + 1)
-        act(vw("J3", 0, 2 * w), vw("AD", ad, ad + 2 * w), ACT.Relu, bias=BIG, scale=-BIG, acc=cn)
-        slot = (0, 1, 4)[b]
-        ts(vw("FO", slot, slot + 9, 8), both, cn, vw("TC", b, b + 1), ALU.subtract, ALU.max)
+            bank([(part(r, b, 4), ID, m0), (part(r, b, 4), ID, m1), (part(r, b, 4), vw("NID"), m2)], False, False)
 
-    def update(r, b0, b1):
-        c0, c1 = 16 * b0, 16 * b1
-        y, cc = vw("MB", 64 + c0, 64 + c1), vw("MB", 128 + c0, 128 + c1)
-        ry, m2, nm, cm, go = [vw(n, c0, c1) for n in ("RY", "M2", "NM", "CM", "GO")]
-        off = old = vw("FO", 2 * b0, b0 + b1)
-        ts(ry, y, C16, C16, ALU.add, ALU.subtract)
-        tt(m2, ry, y, ALU.is_equal)
-        if b0 == 2:
-            old = vw("HU", 0, 1)
-            tt(nm, ry, y, ALU.not_equal)
-            cp(old, vw("VC", 2, 3))
+    def name(r, b):
+        oq, cs = vw("OQ", 4 * b, 4 * b + 3), vw("CS", 48 * b, 48 * b + 48)
+        ts(oq, vw("UU", 68 * b + 64, 68 * b + 67), vw("R1", b, b + 1), 1.0 / 16, ALU.subtract, ALU.mult)
+        act(cs, ind(vw("CF", 64 * b, 64 * b + 64), oq), ACT.Copy)
+        tt(vw("SB", b, 144, 3), ind(vw("IDT"), vw("OO", 8 * b + 4, 8 * b + 7)), cs, ALU.mult)
+        sb = vw("SB", 96 + b, 144, 3)
+        for k, lhs in ((0, "BMB"), (1, "NBMB"), (2, "BMB"), (3, "NBMB"), (3, "BM")):
+            mm(part(r, b, k), vw(lhs), sb)
+        gb, g0 = conflict_bank(b)
+        for q in range(4):
+            mm(rows(vw(gb, g0 + 49, g0 + 99), q), rows(vw("SB", b, 96, 3), q), rows(vw("RC"), q))
+        if b < 2:
+            for u in range(b + 1):
+                mm(vw(gb, g0 + 49 + u, g0 + 97, 3), BM, vw("SB", 96 + u, 144, 3), False, u == b, pin=True)
         else:
-            act(nm, m2, ACT.Identity, bias=1.0, scale=-1.0)
-        tt(cm, m2, cc, ALU.mult)
-        tt(go, ind(vw("BF"), old), nm, ALU.mult)
-        tt(ind(vw("BF"), off), go, cm, ALU.add)
+            mm(vw(gb, g0 + 49, g0 + 97), BM, vw("SB", 96, 144), False, True, pin=True)
+
+    def stand(r, b):
+        gb, g0 = conflict_bank(b)
+        z, fo, both, tc = vw("ZZ", b, b + 1), vw("FO", b, b + 9, 8), vw(gb, g0, g0 + 99, 98), vw("TC", b, b + 1)
+        if b >= PLAN["countv"]:
+            red(z, vw(gb, g0 + 1, g0 + 98), ALU.min, True)
+            if b == 2:
+                cp(vw("HU", 0, 1), vw(gb, 0, 1))
+            ts(fo, both, z, tc, ALU.mult, ALU.max)
+        else:
+            ad = vw("AD", 96 * b, 96 * b + 96)
+            act(ad, vw(gb, g0 + 1, g0 + 97), ACT.Abs)
+            act(ad, ad, ACT.Relu, bias=2 * B, scale=-2 * B, acc=z)
+            ts(fo, both, z, tc, ALU.subtract, ALU.max)
+
+    def place(r, b):
+        last = r == RO - 1
+        if b == 0:
+            if PLAN["roundv"]:
+                ts(vw("RC2"), vw("GB", 256, 320), C16B, C16B, ALU.add, ALU.subtract)
+            else:
+                act(vw("RA"), vw("GB", 256, 320), ACT.Identity, bias=C16B)
+                act(vw("RC2"), vw("RA"), ACT.Identity, bias=-C16B)
+            mm(vw("UA", 0, 64), vw("NID"), vw("RC2"))
+            act(vw("UL", 0, 64 if last else 96), vw("UA", 0, 64 if last else 96), ACT.Copy)
+        else:
+            ub, skip = part(r, b, 0)[0], 16 if last else 0
+            ts(vw("RB", 16, 48), vw(ub, 128, 160), C16B, C16B, ALU.add, ALU.subtract)
+            tt(vw("UL", 96 + skip, 144), vw(ub, 160 + skip, 208), vw("RB", skip, 48), ALU.subtract)
+
+    def update(r, b):
+        n, u = (2, 0) if b == 0 else (1, 112)
+        go = vw("GO", 16 * b, 16 * (b + n))
+        tt(go, ind(vw("BF"), vw("HU", 0, 1) if b == 2 else vw("FO", b, b + n)), vw("UL", u, u + 16 * n), ALU.min)
+        tt(ind(vw("BF"), vw("FO", b, b + n)), go, vw("UL", u + 16 * n, u + 32 * n), ALU.max)
         if r < RO - 1:
-            cp(ind(vw("NX"), vw("FO", 8 + 2 * b0, 8 + b0 + b1)), vw("XN", c0, c1))
+            if not PLAN["joint"]:
+                cp(ind(vw("NX"), vw("FO", 8 + b, 8 + b + n)), vw("UL", 64 + 16 * b, 64 + 16 * (b + n)))
+            elif b == 2:
+                cp(ind(vw("NX"), vw("FO", 8, 11)), vw("UL", 64, 112))
 
-    hash_state(0, 0, 3)
-    cp(vw("CU"), ind(vw("BI"), vw("OF")))
-    ts(vw("CF"), vw("CU"), -1536.0, None, ALU.add)
-    cp(vw("BF", PAD), vw("BI"))
     for r in range(RO):
-        for name, b0, b1 in PLAN["steps"]:
-            cur[0] = name + str(b0)
-            if name == "cu" and r > 0:
-                cp(vw("CU", 64 * b0, 64 * b1), ind(vw("BF"), vw("OF", 4 * b0, 4 * b1)))
-                ts(vw("CF", 64 * b0, 64 * b1), vw("CU", 64 * b0, 64 * b1), -1536.0, None, ALU.add)
-            elif name == "search":
-                search(r, b0)
-            elif name == "winner":
-                winner(r, b0)
-            elif name == "update":
-                update(r, b0, b1)
-            elif name == "hash" and r > 0:
-                hash_state(r, b0, b1)
-            elif name == "next" and r < RO - 1:
-                hash_state(r + 1, b0, b1)
+        for step, b in PLAN["steps"]:
+            cur[:] = [step + str(b), r]
+            if step == "cu" and r > 0:
+                cp(vw("CU", 64 * b, 64 * b + 64), ind(vw("BF"), slot("LD", r - 1, b, 16, 20)))
+                ts(vw("CF", 64 * b, 64 * b + 64), vw("CU", 64 * b, 64 * b + 64), -MID, None, ALU.add)
+            elif step == "next" and r < RO - 1:
+                recv(r + 1, b)
+            elif step in ("recv", "search", "winner", "move", "name", "stand", "update", "place"):
+                {"recv": recv, "place": place, "search": search, "winner": winner, "move": move, "name": name, "stand": stand, "update": update}[step](r, b)
     add("s", lambda q: q.sync.dma_start(T.yb[:], ap(vw("BF", PAD))), [], [vw("BF", PAD)], 60, "o_yb", 4500)
     add("a", lambda q: q.scalar.dma_start(T.ys[:], ap(vw("SLF"))), [], [vw("SLF")], 60, "o_ys", 2000)
     return ops
 
 
 def edges(ops):
-    seen, reach = {}, []
+    seen, reach, bits = {}, [], {}
+
+    def cols(v):
+        if v[1:4] not in bits:
+            bits[v[1:4]] = sum(1 << c for c in range(v[1], v[2], v[3]))
+        return bits[v[1:4]]
+
     for i, o in enumerate(ops):
         dep = set()
         for vs, writes in ((o["rd"], False), (o["wr"], True)):
             for v in vs:
                 psum = SCRATCH[v[0]][0] == "psum"
                 for j, u, w in seen.get(v[0], []):
-                    if (psum and (ops[j]["eng"] != o["eng"] or o["eng"] == "t")) or ((w or writes) and u[1] < v[2] and v[1] < u[2]):
+                    p = ops[j]
+                    if psum and p["eng"] == "t" and o["eng"] == "t":
+                        if p["group"] != o["group"] or p["first"] or o["last"] or (u & cols(v) == cols(v) != u and p["wide"]):
+                            dep.add(j)
+                    elif (psum and p["eng"] != o["eng"]) or ((w or writes) and u & cols(v)):
                         dep.add(j)
         for vs, writes in ((o["rd"], False), (o["wr"], True)):
             for v in vs:
-                seen.setdefault(v[0], []).append((i, v, writes))
+                seen.setdefault(v[0], []).append((i, cols(v), writes))
         cover = 0
         for j in dep:
             cover |= reach[j]
@@ -351,21 +439,36 @@ def edges(ops):
     return reach
 
 
-def times(order, eng, fig):
-    cost, lat, gp = fig
-    end, why = [0.0] * len(cost), [-1] * len(cost)
-    free, last, m, mi = dict.fromkeys("tvags", 0.0), dict.fromkeys("tvags", -1), 0.0, -1
+def close_groups(ops, order):
+    last = {}
     for i in order:
+        o = ops[i]
+        if o["eng"] == "t":
+            o["ends"][:] = [o["group"] not in last, False]
+            last[o["group"]] = o
+    for o in last.values():
+        o["ends"][1] = True
+
+
+def times(order, eng, fig, p0=0, old=None):
+    cost, lat, gp = fig
+    n = len(cost)
+    why, end = (old[2][:], old[3][:]) if old else ([-1] * n, [0.0] * n)
+    last = dict.fromkeys("tvags", -1)
+    for i in order[max(0, p0 - 300):p0]:
+        last[eng[i]] = i
+    free = {e: end[i] if i >= 0 else 0.0 for e, i in last.items()}
+    for i in order[p0:]:
         e = eng[i]
         t, w = free[e], last[e]
         for j, gap in gp[i]:
-            if end[j] + gap > t:
-                t, w = end[j] + gap, j
+            gap += end[j]
+            if gap > t:
+                t, w = gap, j
         end[i] = free[e] = t + cost[i]
         why[i], last[e] = w, i
-        if end[i] + lat[i] > m:
-            m, mi = end[i] + lat[i], i
-    return m, mi, why, end
+    mi = max(n - 2, n - 1, key=lambda i: end[i] + lat[i])
+    return end[mi] + lat[mi], mi, why, end
 
 
 def greedy(eng, cost, pred, prio, slack, at):
@@ -401,30 +504,39 @@ def plan(T):
         figs.append(([o["cost"] for o in alt], [o["lat"] for o in alt],
                      [[(j, 0.0 if eng[j] == "t" and eng[i] == "t" else alt[j]["lat"] + est["hop"]) for j in ops[i]["near"]] for i in range(n)]))
 
-    def full(o):
-        res = [times(o, eng, f) for f in figs]
+    def full(o, p0=0, old=None):
+        res = [times(o, eng, f, p0, old and old[k]) for k, f in enumerate(figs)]
         return sum(est["weight"] * x[0] for est, x in zip(EST, res)) / sum(est["weight"] for est in EST), res
 
     cost, lat, gp = figs[0]
+    pred, named = [list(p) for p in gp], {}
+    for i, o in enumerate(ops):
+        if o["eng"] in "va" and o["wr"] and o["cls"] != "setup":
+            named.setdefault((o["round"], o["wr"][0][0] + o["cls"][-1]), []).append(i)
+    for e in "va":
+        chain = []
+        for r in range(RO):
+            for word in PLAN[e].split():
+                name, dot, span = word.partition(".")
+                a, dash, b = span.partition("-")
+                chain += [i for i in named.get((r, name), [])[int(a or 0):int(b or a or 0) + 1] if eng[i] == e]
+        for u, v in zip(chain, chain[1:]):
+            pred[v].append((u, 0.0))
     back = [[] for i in range(n)]
     for i in range(n):
-        for j, gap in gp[i]:
+        for j, gap in pred[i]:
             back[j].append((i, gap))
-    tail = [cost[i] + lat[i] for i in range(n)]
-    for i in range(n - 1, -1, -1):
-        for j, gap in gp[i]:
-            tail[j] = max(tail[j], cost[j] + gap + tail[i])
-    early = [not (o["cls"][:2] == "se" or o["cls"] in ("winner2", "update2")) for o in ops]
+    start = [0.0 if back[i] else lat[i] for i in range(n)]
     best = None
-    for slack, bonus in PLAN["starts"]:
-        prio = [tail[i] + bonus * early[i] for i in range(n)]
+    for slack in PLAN["slacks"]:
+        prio = greedy(eng, cost, back, [0.0] * n, slack, start)[1]
         for it in range(PLAN["passes"]):
-            order, end = greedy(eng, cost, gp, prio, slack, [0.0] * n)
+            order, end = greedy(eng, cost, pred, prio, slack, [0.0] * n)
             score = full(order)[0]
             if best is None or score < best[0]:
                 best = (score, order)
-            prio = greedy(eng, cost, back, end, slack, [0.0 if back[i] else lat[i] for i in range(n)])[1]
-    state = [2]
+            prio = greedy(eng, cost, back, end, slack, start)[1]
+    state = [PLAN["seed"]]
 
     def rnd(k):
         state[0] = (state[0] * 6364136223846793005 + 1442695040888963407) % (1 << 64)
@@ -474,8 +586,8 @@ def plan(T):
             if eng[u] in queues:
                 continue
             new = order[:pu] + [x for x in mid if x not in moved] + [u] + [x for x in mid if x in moved] + order[pv + 1:]
-        score, nres = full(new)
-        if score <= now or rnd(1 << 20) / (1 << 20) < math.exp((now - score) / (20.0 * (1 - it / PLAN["moves"]) + 1)):
+        score, nres = full(new, pu, res)
+        if score <= now or rnd(1 << 20) / (1 << 20) < math.exp((now - score) / (PLAN["heat"] * (1 - it / PLAN["moves"]) + 1)):
             order, now, res = new, score, nres
             if now < best[0]:
                 best = (now, order)
@@ -514,8 +626,10 @@ def rank_program(g, core, T, topo):
     if "order" not in PLANNED:
         PLANNED["order"], PLANNED["times"] = plan(T)
     order, end = PLANNED["order"], PLANNED["times"][0][3]
+    order = list(range(5)) + [i for i in order if i >= 5]
     ops = trace(T, send, EST[0])
     edges(ops)
+    close_groups(ops, order)
     queue = {"t": g.tensor, "v": g.vector, "a": g.scalar, "g": g, "s": g.sync}
     pos, count = {}, {e: 0 for e in queue}
     for i in order:

@@ -12,33 +12,46 @@ PARTS = {0: (0, 1, 2, 3, 4), 2: (0, 1, 3, 4, 2)}
 SLOT = 24
 
 PLAN = {
-    "chunks": "a2v2a3v3v3v3 a6v3v3v2v2 a5v3v2v2v2v2",
-    "steps": [("recv", 0), ("cu", 0), ("search", 0), ("recv", 1), ("cu", 1), ("search", 1), ("winner", 0), ("move", 0), ("name", 0),
-              ("stand", 0), ("recv", 2), ("cu", 2), ("search", 2), ("winner", 1), ("move", 1), ("name", 1), ("place", 0), ("stand", 1),
-              ("update", 0), ("winner", 2), ("move", 2), ("name", 2), ("place", 2), ("stand", 2), ("update", 2)],
-    "countv": 0, "roundv": True, "joint": False,
-    "v": "CU0 ST0 XG0.1 XG0.3-5 CU1 ST1 XG1.1 R10 UU0 XG1.2 OO0 XG1.3 GG0 GE0 XG1.4 CU2 ST2 CF0 OQ0 XG2.1 SO0 XG2.2 R11 UU1 XG2.3 OO1 "
-         "XG2.4 GG1 GE1 XG2.5 SB0 OQ1 CF1 CF2 ZZ0 SO1 R12 UU2 SB1 OO2 OQ2 FO0 GG2 GE2 ZZ1 RC20 SB2 FO1 SO2 GO0 RB2 BF0 HU2 ZZ2 UL2 NX0 "
-         "FO2 GO2 BF2 NX2",
-    "a": "XG0.0 XG0.2 AB0.0-3 SC0 AB0.4-15 XG1.0 AB1.6-8 SC1 AB1.0-5 AB1.9-11 BS0 SOF0 AB1.12-15 XG2.0 LB0.0-1 AB2.5-7 AB2.0-2 CS0 "
-         "AB2.3-4 SC2 AB2.8-13 BS1 SOF1 AB2.14-15 CS1 LB1.0-1 CS2 LB2.0-1 BS2 SOF2 UL0",
-    "slacks": (0.0, 20.0, 60.0), "passes": 3, "moves": 50000, "heat": 25.0, "seed": 2,
+    "chunks": "a2v2a3v3v3v3 a6v5v2v3 a2a4v5v2v3",
+    "steps": [("recv", 0), ("cu", 0), ("search", 0), ("recv", 1), ("cu", 1), ("search", 1), ("winner", 0), ("proj", 0), ("recv", 2),
+              ("cu", 2), ("search", 2), ("winner", 1), ("proj", 1), ("bits", 0), ("bits", 1), ("move", 0), ("name", 0), ("meet", 0),
+              ("move", 1), ("name", 1), ("meet", 1), ("place", 0), ("stand", 0), ("stand", 1), ("update", 0), ("winner", 2), ("proj", 2),
+              ("bits", 2), ("move", 2), ("name", 2), ("meet", 2), ("place", 2), ("stand", 2), ("update", 2)],
+    "gst": False, "gcf": True, "soa": (), "foa": (), "csv": (0, 1), "maxv": (), "lastv": (2,), "countv": 0, "roundv": True, "joint": False,
+    "v": "CU0 ST0 XG0.1 XG0.3-5 CU1 ST1 XG1.1 R10 UU0 XG1.2 OO0 XG1.3 GG0 CU2 GE0 ST2 OQ0 XG2.2 R11 UU1 XG2.3 OO1 OQ1 SO0 XG2.4 GG1 "
+         "GE1 CS0 CS1 SB0 SB1 R12 UU2 OO2 OQ2 SO1 RC20 GG2 YY2 GE2 ZZ0 ZZ1 YW2 SB2 FO0 FO1 SOF2 GO0 NX0 RB2 BF0 UL2 HU2 ZZ2 SO2 GO2 FO2 "
+         "BF2 NX2",
+    "a": "XG0.0 XG0.2 AB0.0-15 SC0 XG1.0 AB1.6-10 AB1.0-5 AB1.11-15 XG2.0 SC1 BS0 SOF0 XG2.1 AB2.0-1 AB2.6-10 AB2.2-5 AB2.11-15 "
+         "SC2 BS1 SOF1 LB1.0-1 LB0.0-1 CS2 UL0 LB2.0-1 BS2 SOF2",
+    "chunks0": "a3v2a3v3v3v2 a7v4v2v3 a2a4v4v2v2v2", "maxv0": (8, 9, 10, 11),
+    "v0": "XG0.1 XG0.3-5 AB0.8-11 XG1.1 R10 UU0 XG1.2 OO0 XG1.3 GE0 GG0 XG2.3 XG2.2 R11 UU1 OQ0 SO0 OO1 OQ1 CS0 GE1 GG1 XG2.4-5 CS1 "
+          "SB0 SB1 SO1 R12 UU2 OO2 OQ2 RC20 GG2 ZZ0 GE2 ZZ1 SB2 FO0 FO1 GO0 NX0 RB2 BF0 UL2 ZZ2 HU2 SO2 FO2 GO2 BF2 NX2",
+    "a0": "SC0 XG0.0 XG0.2 AB0.0-7 AB0.12-15 XG1.0 AB1.7-10 AB1.0-6 AB1.11-15 SC1 BS0 XG2.0-1 AB2.10-11 AB2.0-1 AB2.6-9 AB2.2-5 SC2 "
+          "BS1 AB2.12-15 LB0.0-1 LB1.0-1 CS2 UL0 LB2.0-1 BS2",
+    "v2": "CU0 ST0 XG0.1 XG0.3-5 CU1 ST1 XG1.1 R10 UU0 XG1.2 OO0 XG1.3 GG0 GE0 CU2 ST2 OQ0 XG2.2 R11 UU1 XG2.3 OO1 OQ1 XG2.4 GG1 CS0 "
+          "CS1 GE1 SB0 SB1 R12 UU2 OO2 OQ2 YY2 GG2 RC20 YW2 ZZ0 SB2 ZZ1 SOF2 FO0 FO1 GO0 RB2 BF0 UL2 HU2 ZZ2 GO2 FO2 BF2",
+    "a2": "XG0.0 XG0.2 AB0.0-15 SC0 XG1.0 AB1.6-10 AB1.0-5 AB1.11-15 SC1 XG2.0-1 SOF0 AB2.0-1 AB2.6-10 AB2.2-5 AB2.11-15 SC2 "
+          "LB1.0-1 LB0.0-1 SOF1 CS2 UL0 LB2.0-1",
+    "t": "Pproj2.0-2 Pwinner2.1-2 Swinner2.1-2 Kmove2.1-3 Kname2.0-4 Gname2.0-5 Gmeet2.0-5 Swinner2.3-6",
+    "g": "PI J16 JG JR JP ORD CKS BF CF",
+    "slacks": (0.0, 15.0, 40.0, 60.0), "moves": 70000, "heat": 8.0, "seed": 3,
 }
-_E = {"cyc": 0.87, "pe": 0.44, "hop": 190.0, "gather": 1.56, "scatter": 3.8, "remote": 3200.0, "first": 500.0, "nx": 6500, "bk": 3800, "weight": 1}
-EST = [dict(_E, nx=4500, bk=3000, weight=2), dict(_E, hop=150.0, remote=4300.0, first=2000.0, nx=5500),
-       dict(_E, cyc=1.2, pe=0.62, gather=1.9, scatter=5.0, hop=220.0, remote=4000.0, first=1500.0, nx=5000),
-       dict(_E, gather=1.15, scatter=2.2, hop=170.0, remote=2600.0, nx=4000, bk=2800)]
+_E = {"cyc": 0.87, "pe": 0.44, "hop": 190.0, "gather": 1.56, "scatter": 3.8, "remote": 3200.0, "first": 500.0, "nx": 6500, "bk": 3000, "short": 1500,
+      "yb": 4500, "ys": 2300, "weight": 1}
+EST = [dict(_E, nx=3550, bk=2400, short=1400, pe=0.47, remote=3300.0, first=700.0, weight=2),
+       dict(_E, cyc=1.15, pe=0.62, gather=1.8, scatter=5.0, hop=210.0, remote=3800.0, first=1500.0, nx=3800, short=1800),
+       dict(_E, hop=170.0, remote=3900.0, first=1300.0, nx=3600, short=1600)]
 
 SCRATCH = {}
 for _names, _cols, _dt in (
         ("NX", PAD + V, "bfloat16"), ("BI", KB, "int32"), ("BF", PAD + KB, "float32"), ("ST", RO * S, "bfloat16"),
-        ("SO LD", (RO - 1) * 3 * SLOT, "uint16"), ("SOF SLF ORD", S, "float32"), ("PA I16", 16, "bfloat16"), ("TH", 4, "int32"),
-        ("AC", 1, "float32"), ("WC EV OCT", 4, "float32"), ("XG AB", V, "bfloat16"),
-        ("ONE BM0 BM ID NID NID256 AM NAM NAM256 BMB NBMB", 128, "bfloat16"), ("GM NN OC ZZ TC", 8, "float32"),
-        ("W4", 140, "bfloat16"), ("ZA LB2", 144, "bfloat16"), ("PI PJ", 1, "int32"), ("JR J16", 64, "float32"),
-        ("PW TWO ZER PWM", 16, "float32"), ("SG", 2, "float32"), ("CKS BS GE", S, "bfloat16"),
-        ("IDT", 192, "bfloat16"), ("DL", 67, "float32"), ("MK", 297, "bfloat16"), ("CKA", 160, "bfloat16"), ("CKB", 80, "bfloat16"),
-        ("RC", 50, "bfloat16"), ("LB", 146, "bfloat16"), ("SB GG", 144, "float16"), ("KK", 32, "float32"),
+        ("SO LD", (RO - 1) * 3 * SLOT, "uint16"), ("SOF SLF YY YW", S, "float32"), ("PA I16", 16, "bfloat16"), ("THR", 128, "int32"), ("THF", 128, "float32"),
+        ("AC GC", 1, "float32"), ("WC EV OCT", 4, "float32"), ("XG AB", V, "bfloat16"),
+        ("ONE JG JP BM ID NID NID256 AM NAM NAM256 BMB NBMB", 128, "bfloat16"), ("GM0 GM NN OC ZZ TC", 8, "float32"),
+        ("W4", 140, "bfloat16"), ("AM2", 32, "bfloat16"), ("ZA NZA", 144, "bfloat16"), ("PI PJ", 1, "int32"), ("J16", 64, "float32"), ("JR", 12, "float32"),
+        ("PW ZER PWM", 16, "float32"), ("TWO", 17, "float32"), ("SG", 2, "float32"), ("CKS BS GE", S, "bfloat16"),
+        ("IDT", 256, "bfloat16"), ("ORD", 99, "float32"), ("RH", 49, "bfloat16"), ("WR", 128, "bfloat16"), ("DL", 67, "float32"), ("MK", 297, "float16"), ("CKA", 160, "bfloat16"), ("CKB", 80, "bfloat16"),
+        ("RC", 50, "bfloat16"), ("LB", 96, "bfloat16"), ("SB GG", 144, "float16"), ("KK", 32, "float32"),
         ("OF", 12, "uint16"), ("CU", 192, "uint16"), ("CF SC", 192, "float32"), ("CS", 144, "float32"),
         ("R1", 3, "float32"), ("UU", 3 * 68, "float32"), ("OO", 24, "uint16"), ("OQ FO", 16, "uint16"), ("HU", 2, "uint16"),
         ("RA", 64, "float32"), ("RC2", 64, "bfloat16"), ("UL", 144, "float32"), ("AD", 192, "float32"), ("RB GO", S, "float32")):
@@ -132,12 +145,12 @@ def trace(T, send, est):
         cost = (78 + 16 * width(a[2]) * est["gather"] if a[0] == "ind" else max(66, width(a))) * cyc
         add("a", fn, [out] + ([acc] if acc else []), [a, bias, scale], cost + (20 if acc else 0))
 
-    def mm(out, lhs, rhs, start=False, stop=False, pin=False):
+    def mm(out, lhs, rhs, start=False, stop=False, pin=False, alone=False):
         ends = [start, stop]
         add("t", lambda q: q.tensor.matmul(ap(out), ap(lhs), ap(rhs), ends[0], ends[1]), [out], [lhs, rhs],
             max(min(64, width(lhs)), width(rhs)) * est["pe"])
         groups[out[0]] = groups.get(out[0], 0) + start
-        ops[-1].update(group=(out[0], groups[out[0]]), ends=ends, first=pin and start, last=pin and stop, wide=rhs[0][:2] == "CK")
+        ops[-1].update(group=(out[0], groups[out[0]]), ends=ends, first=pin and start, last=pin and stop, wide=rhs[0][:2] in ("CK", "MK"))
 
     def bank(terms, start=True, stop=True):
         for i, (out, lhs, rhs) in enumerate(terms):
@@ -153,44 +166,52 @@ def trace(T, send, est):
     def sel(out, a, pattern, cmp, base, mult):
         add("g", lambda q: q.affine_select(ap(out), ap(a), pattern, cmp, 0.0, base, mult), [out], [a], 210 + 2 * width(out) * cyc)
 
-    add("s", lambda q: q.sync.dma_start(ap(vw("PA")), T.pa[:]), [vw("PA")], [], 60, "l_pa", 2000)
-    add("s", lambda q: q.sync.dma_start(ap(vw("TH", 0, 1)), T.th[:]), [vw("TH")], [], 60, "l_th", 2000)
-    add("s", lambda q: q.sync.dma_start(ap(vw("ST", 0, S)), T.s0[:]), [vw("ST", 0, S)], [], 60, "l_s", 2000)
-    add("a", lambda q: q.scalar.dma_start(ap(vw("BI")), T.bk[:]), [vw("BI")], [], 60, "l_bk", est["bk"])
+    add("s", lambda q: q.sync.dma_start(ap(vw("PA")), T.pa[:]), [vw("PA")], [], 60, "l_pa", est["short"])
+    thr, thf = ("THR", 0, 128, 1, 0, 1), ("THF", 0, 128, 1, 0, 1)
+    add("s", lambda q: q.sync.dma_start(ap(thr), T.th[:]), [thr], [], 60, "l_th", est["short"])
+    add("s", lambda q: q.sync.dma_start(ap(vw("ST", 0, S)), T.s0[:]), [vw("ST", 0, S)], [], 60, "l_s", est["short"])
+    add("s", lambda q: q.sync.dma_start(ap(vw("BI")), T.bk[:]), [vw("BI")], [], 60, "l_bk", est["bk"])
     add("s", lambda q: q.sync.dma_start(ap(vw("NX", PAD)), T.nx[:]), [vw("NX", PAD)], [], 60, "l_nx", est["nx"])
 
     ID, BM, AM, AC = vw("ID"), vw("BM"), vw("AM"), vw("AC")
     ms(vw("ONE"), 1.0)
     iota(vw("PI"), [[0, 1]], 0, 1, small=False)
     iota(vw("J16"), [[0, 4], [1, 16]], 0, 0)
-    sel(vw("BM0"), vw("ONE"), [[-16, 8], [0, 16]], ALU.is_ge, 0, 1)
-    sel(BM, vw("BM0"), [[16, 8], [0, 16]], ALU.is_ge, 15, -1)
-    sel(ID, vw("ONE"), [[-1, 128]], ALU.is_equal, 0, 1)
-    iota(vw("JR"), [[16, 64]], 0, 0)
-    iota(vw("ORD"), [[128, 16], [2048, 3]], 64, 0)
+    iota(vw("JG"), [[16, 8], [0, 16]], 0, 0)
+    iota(vw("JP"), [[-1, 128]], 0, 1)
+    iota(vw("JR"), [[16, 12]], 0, 0)
+    iota(vw("ORD", 0, 48), [[1, 16], [16, 3]], 0, 0)
+    iota(vw("ORD", 48, 99), [[1, 51]], -3, 0)
     iota(vw("CKS", 0, 32), [[-24, 2], [0, 16]], 12, 0)
     iota(vw("CKS", 32, 48), [[0, 16]], 256, 0)
     ts(vw("PJ"), vw("PI"), 15, None, ALU.bitwise_and)
     cp(AC, vw("PJ"))
-    ts(vw("IDT", 128, 192), vw("J16"), AC, None, ALU.is_equal)
-    i16 = vw("IDT", 128, 144)
-    ms(vw("TWO"), 2.0); ms(vw("ZER"), 0.0)
-    scan(vw("PW"), vw("TWO"), vw("ZER"), 0.25, ALU.mult, ALU.add)
+    ts(vw("GC"), vw("PI"), AC, None, ALU.subtract)
+    ts(vw("GM"), vw("JG", 0, 128, 16), vw("GC"), None, ALU.is_equal)
+    for name, f in (("BM", 1.0), ("BMB", B), ("NBMB", -B)):
+        ts(vw(name), vw("JG"), vw("GC"), f, ALU.is_equal, ALU.mult)
+    for name, f in (("ID", 1.0), ("NID", -1.0), ("NID256", -256.0)):
+        ts(vw(name), vw("JP"), 0.0, f, ALU.is_equal, ALU.mult)
+    ts(vw("IDT", 0, 64), vw("J16"), AC, None, ALU.is_equal)
+    i16 = vw("IDT", 0, 16)
+    ms(vw("TWO", 0, 16), 2.0); ms(vw("ZER"), 0.0)
+    scan(vw("PW"), vw("TWO", 0, 16), vw("ZER"), 0.25, ALU.mult, ALU.add)
     ms(vw("PW", 10, 11), -(512.0 + PAD)); ms(vw("PW", 11, 12), 0.5); ms(vw("PW", 12, 16), 0.0)
     tt(vw("PWM"), vw("PW"), i16, ALU.mult)
     red(vw("WC", 0, 1), vw("PWM"), ALU.add)
-    ts(vw("SG"), vw("IDT", 128, 130), -2.0, 1.0, ALU.mult, ALU.add)
+    ts(vw("SG"), vw("IDT", 0, 2), -2.0, 1.0, ALU.mult, ALU.add)
     ts(vw("WC", 1, 3), vw("SG"), vw("WC", 0, 1), None, ALU.mult)
     ts(vw("WC", 3, 4), vw("WC", 1, 2), vw("SG", 1, 2), None, ALU.mult)
     ms(vw("W4"), 0.0)
-    cp(vw("GM"), vw("BM", 0, 128, 16))
     for gg in range(8):
-        if gg % 2:
-            act(vw("AM", 16 * gg, 16 * gg + 16), vw("PA"), ACT.Copy, scale=vw("GM", gg, gg + 1))
-        else:
-            ts(vw("AM", 16 * gg, 16 * gg + 16), vw("PA"), vw("GM", gg, gg + 1), None, ALU.mult)
+        act(vw("AM", 16 * gg, 16 * gg + 16), vw("PA"), ACT.Copy, scale=vw("GM", gg, gg + 1))
     nth = vw("NN", 1, 2)
-    ts(nth, vw("TH", 0, 1), -1.0, -0.5, ALU.mult, ALU.add)
+    one, tht = ("TWO", 16, 17, 1, 0, 1), vw("PS", 0, 1)
+    ms(one, 1.0)
+    cp(thf, thr)
+    add("t", lambda q: q.tensor.transpose(ap(tht), ap(thf), ap(one)), [tht], [thf, one], 256 * est["pe"])
+    ops[-1].update(group=("PS", 0), ends=[True, True], first=False, last=False, wide=False)
+    ts(nth, tht, -1.0, -0.5, ALU.mult, ALU.add)
     for k in range(4):
         if k % 2:
             act(vw("W4", 12 + k, 140, 16), vw("GM"), ACT.Copy, scale=vw("WC", k, k + 1))
@@ -198,21 +219,26 @@ def trace(T, send, est):
             ts(vw("W4", 12 + k, 140, 16), vw("GM"), vw("WC", k, k + 1), None, ALU.mult)
     ms(vw("ZA"), 0.0)
     act(vw("ZA", 15, 143, 16), vw("GM"), ACT.Copy, scale=64.0)
+    act(vw("NZA"), vw("ZA"), ACT.Copy, scale=-1.0)
     red(vw("EV", 0, 1), vw("GM", 0, 8, 2), ALU.add)
     red(vw("EV", 1, 2), vw("GM", 1, 8, 2), ALU.add)
-    for name, src, f in (("NAM", AM, -1.0), ("NAM256", AM, -256.0), ("NID", ID, -1.0), ("NID256", ID, -256.0), ("BMB", BM, B), ("NBMB", BM, -B)):
-        act(vw(name), src, ACT.Copy, scale=f)
+    for name, f in (("NAM", -1.0), ("NAM256", -256.0)):
+        act(vw(name), AM, ACT.Copy, scale=f)
     for k in range(2):
-        act(vw("IDT", 64 * k, 64 * k + 64), vw("IDT", 128, 192), ACT.Copy, scale=vw("EV", k, k + 1))
+        act(vw("IDT", 64 * k + 64, 64 * k + 128), vw("IDT", 0, 64), ACT.Copy, scale=vw("EV", k, k + 1))
+    act(vw("IDT", 192, 256), vw("IDT", 0, 64), ACT.Copy)
 
     def first_hash():
-        bank([(vw("PR", 0, S), AM, vw("ST", 0, S))])
+        ts(vw("AM2", 0, 16), vw("PA"), vw("EV", 0, 1), None, ALU.mult)
+        act(vw("AM2", 16, 32), vw("PA"), ACT.Copy, scale=vw("EV", 1, 2))
+        for q in range(4):
+            mm(rows(vw("PR", 0, S), q), rows(vw("AM2"), q), rows(vw("ST", 0, S), q), True, True, alone=True)
         act(vw("BS"), vw("PR", 0, S), ACT.Sign, bias=nth)
         bank([(vw("SD", 0, 12), vw("W4", 12 - 4 * aa, 140 - 4 * aa), vw("BS", aa, S, 4)) for aa in range(4)])
         ts(vw("OF"), vw("SD", 0, 12), -float(PAD), None, ALU.add)
         cp(vw("CU", 0, 64), ind(vw("BI"), vw("OF", 0, 4)))
         cp(vw("CU", 64, 192), ind(vw("BI"), vw("OF", 4, 12)))
-        ts(vw("CF"), vw("CU"), -MID, None, ALU.add)
+        sel(vw("CF"), vw("CU"), [[0, 192]], ALU.is_ge, 0, 0)
 
     first_hash()
     sel(vw("BF", PAD), vw("BI"), [[0, KB]], ALU.is_ge, 0, 0)
@@ -225,20 +251,22 @@ def trace(T, send, est):
     act(vw("OC", 4, 7), vw("JR", 0, 12, 4), ACT.Identity, bias=63.0)
     ms(vw("K0", 64, 67), 2.0 ** 20); ms(vw("K1", 64, 67), 2.0 ** 20)
     act(vw("TC", 0, 3), vw("JR", 0, 3), ACT.Identity, bias=AC)
-    act(vw("TC", 3, 6), vw("TC", 0, 3), ACT.Copy, scale=128.0)
-    act(vw("OCT", 0, 3), vw("TC", 0, 3), ACT.Copy, scale=-128.0 * 64)
-    ms(vw("MK", 0, 297, 99), 0.0); ms(vw("MK", 97, 297, 99), 1.0); ms(vw("MK", 98, 297, 99), MID + PAD)
-    for b in range(3):
-        ts(vw("MK", 99 * b + 1, 99 * b + 49), vw("ORD"), vw("TC", 3 + b, 4 + b), -16.0, ALU.subtract, ALU.max)
-        act(vw("MK", 99 * b + 49, 99 * b + 97), vw("ORD"), ACT.Relu, bias=vw("OCT", b, b + 1), scale=64.0)
-    ms(vw("RC", 0, 48), -1.0)
-    act(vw("RC", 48, 50), vw("J16", 0, 2), ACT.Copy)
+    ts(vw("MK", 32, 48), vw("ORD", 51, 67), vw("TC", 0, 1), B, ALU.is_ge, ALU.mult)
+    for b, c0 in enumerate((51, 0, 0)):
+        ts(vw("MK", 99 * b + c0, 99 * b + 67 + 16 * b), vw("ORD", c0, 67 + 16 * b), vw("TC", b, b + 1), B, ALU.is_ge, ALU.mult)
+    ts(vw("MK", 48, 297, 99), vw("TC", 0, 3), -1.0, None, ALU.mult)
+    ts(vw("MK", 49, 297, 99), vw("TC", 0, 3), -1.0, MID + PAD, ALU.mult, ALU.add)
+    ms(vw("MK", 50, 297, 99), 1.0)
+    ms(vw("RC", 2, 50), -1.0)
+    act(vw("RC", 0, 2), vw("J16", 0, 2), ACT.Identity, bias=1.0, scale=-1.0)
+    act(vw("WR"), BM, ACT.Copy, scale=vw("WC", 0, 1))
+    ts(vw("RH", 0, 48), vw("ONE", 0, 48), vw("WC", 0, 1), -1.0, ALU.mult, ALU.mult)
+    act(vw("RH", 48, 49), vw("WC", 0, 1), ACT.Copy)
     ts(vw("KK"), vw("J16", 0, 32), AC, None, ALU.subtract)
     for name, w, places in (("CKA", 32, PARTS[0]), ("CKB", 16, PARTS[2])):
         for k, (f, c) in zip(places, ((B, -7.5 * B), (-B, 7.5 * B), (B, 0.0), (-B, MID), (0.0, -12.0))):
             act(vw(name, k * w, k * w + w), vw("KK", 0, w), ACT.Identity, bias=c, scale=f)
-    ms(vw("LB", 1, 97), 0.0)
-    act(vw("LB", 0, 1), vw("WC", 0, 1), ACT.Copy)
+    ms(vw("LB"), 0.0)
     ms(vw("RB", 0, 16), 0.0)
     for b in range(3):
         act(vw("SC", 64 * b, 64 * b + 16), vw("ZER"), ACT.Copy)
@@ -251,15 +279,25 @@ def trace(T, send, est):
         return vw(name, SLOT * (3 * r + b) + c0, SLOT * (3 * r + b) + c1)
 
     def recv(r, b):
+        copy(r, b)
+        vary(r, b)
+
+    def copy(r, b):
         s = state(r, b)
         if r > 0:
-            cp(s, slot("LD", r - 1, b, 0, 16))
-        bank([(vw("PR", 0, 48), ID, vw("CKS")), (vw("PR", 0, 16), ID, s), (vw("PR", 16, 32), ID, s), (vw("PR", 32, 48), vw("NID"), s)])
-        act(vw("SC", 64 * b + 16, 64 * b + 64), vw("PR", 0, 48), ACT.Copy)
+            if PLAN["gst"]:
+                sel(s, slot("LD", r - 1, b, 0, 16), [[0, 16]], ALU.is_ge, 0, 0)
+            else:
+                cp(s, slot("LD", r - 1, b, 0, 16))
+
+    def vary(r, b):
+        s = state(r, b)
+        bank([(vw("GA", 0, 48), ID, vw("CKS")), (vw("GA", 0, 16), ID, s), (vw("GA", 16, 32), ID, s), (vw("GA", 32, 48), vw("NID"), s)])
+        act(vw("SC", 64 * b + 16, 64 * b + 64), vw("GA", 0, 48), ACT.Copy)
 
     def search(r, b):
         key = vw("K%d" % ((3 * r + b) % 2), 0, 64)
-        spec, a0 = PLAN["chunks"].split()[b], 0
+        spec, a0 = PLAN.get("chunks" + str(r), PLAN["chunks"]).split()[b], 0
         for eng, n in zip(spec[0::2], map(int, spec[1::2])):
             t0 = 16 * b + a0
             src = ind(vw("NX", PAD), vw("CU", 4 * t0, 4 * (t0 + n)))
@@ -270,18 +308,24 @@ def trace(T, send, est):
             for a in range(a0, a0 + n):
                 t = 16 * b + a
                 d = vw("AB", 64 * t, 64 * t + 64)
-                act(d, vw("XG", 64 * t, 64 * t + 64), ACT.Abs, bias=vw("ST", S * r + t, S * r + t + 1), scale=-1.0)
-                mm(key, vw("ZA", 15 - a, 143 - a), d, a == 0, a == 15)
+                x, s = vw("XG", 64 * t, 64 * t + 64), vw("ST", S * r + t, S * r + t + 1)
+                if t in PLAN.get("maxv" + str(r), PLAN["maxv"]):
+                    ts(d, x, s, 2.0, ALU.max, ALU.mult)
+                    mm(key, vw("ZA", 15 - a, 143 - a), d, a == 0)
+                    mm(key, vw("NZA", 15 - a, 143 - a), x)
+                else:
+                    act(d, x, ACT.Abs, bias=s, scale=-1.0)
+                    mm(key, vw("ZA", 15 - a, 143 - a), d, a == 0)
             a0 += n
 
     def conflict_bank(b):
-        return ("GB" if b == 1 else "GA", 0)
+        return (lambda a, c: vw("GA" if b == 2 else "GB", a + 128 * (b == 0), c + 128 * (b == 0))), 0 if b else 32, 67 + 16 * b
 
     def part(r, b, k):
         if b == 2:
             c0, ub = 128 + 16 * PARTS[2][k], "K%d" % ((r + 1) % 2)
         else:
-            c0, ub = (256 + 32 * k + 16 * b, "GB") if k < 2 else (32 * (k - 2) + 16 * b, "UA")
+            c0, ub = (256 + 32 * k + 16 * b, "PR") if k < 2 else (32 * (k - 2) + 16 * b, "UA")
         return vw(ub, c0, c0 + 16)
 
     def winner(r, b):
@@ -293,40 +337,49 @@ def trace(T, send, est):
         xg = vw("XG", 1024 * b, 1024 * b + 1024)
         tt(vw("GG", 48 * b, 48 * b + 48), ind(xg, vw("OO", 8 * b, 8 * b + 3)), vw("SC", 64 * b, 64 * b + 48), ALU.max)
         m0, m1, m2 = [vw("GG", 48 * b + 16 * k, 48 * b + 16 * k + 16) for k in range(3)]
-        ge = vw("GE", 16 * b, 16 * b + 16)
-        tt(ge, ind(xg, vw("OO", 8 * b, 8 * b + 1)), vw("SC", 64 * b + 48, 64 * b + 64), ALU.is_ge)
+        ge, win = vw("GE", 16 * b, 16 * b + 16), ind(xg, vw("OO", 8 * b, 8 * b + 1))
         sv, ps = vw("SD", 0, 16), vw("PS", 0, 16)
-        bank([(sv, ID, s), (sv, ID, m0), (sv, vw("NID256"), ge)], stop=last)
-        if last:
+        if last and b in PLAN["lastv"]:
+            so, land, yy, ww = [vw(n, 16 * b, 16 * b + 16) for n in ("SOF", "SLF", "YY", "YW")]
+            tt(yy, win, s, ALU.add)
+            ts(ww, yy, 256.0, -256.0, ALU.is_ge, ALU.mult)
+            tt(so, yy, ww, ALU.add)
+        elif last:
+            tt(ge, win, vw("SC", 64 * b + 48, 64 * b + 64), ALU.is_ge)
+            bank([(sv, ID, s), (sv, ID, m0), (sv, vw("NID256"), ge)])
             so, land = vw("SOF", 16 * b, 16 * b + 16), vw("SLF", 16 * b, 16 * b + 16)
             act(so, sv, ACT.Copy)
         else:
+            tt(ge, win, vw("SC", 64 * b + 48, 64 * b + 64), ALU.is_ge)
+            bank([(sv, ID, s), (sv, ID, m0), (sv, vw("NID256"), ge)], stop=False)
             bank([(ps, AM, s), (ps, AM, m0), (ps, vw("NAM256"), ge)])
             act(vw("BS", 16 * b, 16 * b + 16), ps, ACT.Sign, bias=nth)
             bank([(vw("SD", 16, 20), vw("W4", 12 - 4 * aa, 140 - 4 * aa), vw("BS", 16 * b + aa, 16 * b + 16, 4)) for aa in range(4)], start=False)
             so, land = slot("SO", r, b, 0, 20), slot("LD", r, b, 0, 20)
-            cp(so, vw("SD", 0, 20))
+            if b in PLAN["soa"]:
+                act(so, vw("SD", 0, 20), ACT.Copy)
+            else:
+                cp(so, vw("SD", 0, 20))
         add("g", lambda q: send(q, r, b, ap(land), ap(so)), [land], [so], 300, "arr%d" % (3 * r + b),
             est["remote"] + (est["first"] if r == 0 and b < 2 else 0.0))
+
+    def proj(r, b):
+        m0, m1, m2 = [vw("GG", 48 * b + 16 * k, 48 * b + 16 * k + 16) for k in range(3)]
+        pr = vw("PR", 16 * b, 16 * b + 16)
+        bank([(pr, AM, m0), (pr, AM, m1), (pr, vw("NAM"), m2)], start=b != 1)
+
+    def bits(r, b):
+        pr = vw("PR", 16 * b, 16 * b + 16)
+        for k in range(2):
+            act(vw("LB", 48 * k + b, 48 + 48 * k, 3), pr, ACT.Sign, bias=vw("EV", 2 + k, 3 + k), scale=vw("EV", k, k + 1))
 
     def move(r, b):
         last = r == RO - 1
         m0, m1, m2 = [vw("GG", 48 * b + 16 * k, 48 * b + 16 * k + 16) for k in range(3)]
-        pr = vw("PR", 0, 16)
-        bank([(pr, AM, m0), (pr, AM, m1), (pr, vw("NAM"), m2)])
-        for k in range(2):
-            act(vw("LB", 1 + 48 * k + b, 49 + 48 * k, 3), pr, ACT.Sign, bias=vw("EV", 2 + k, 3 + k), scale=vw("EV", k, k + 1))
-        gb, g0 = conflict_bank(b)
-        if b != 1:
-            mm(vw(gb, 0, 99), ID, vw("MK", 99 * b, 99 * b + 99), True, pin=True)
+        gb, c0, c1 = conflict_bank(b)
+        mm(gb(c0, c1), ID, vw("MK", 99 * b + c0, 99 * b + c1), b != 1, pin=True)
         if b == 0:
-            mm(vw("GB", 0, 99), ID, vw("MK", 99, 198), True, pin=True)
-        for q in range(4):
-            lhs = rows(vw("LB", 1 + b, 97, 3), q)
-            mm(rows(vw(gb, g0, g0 + 49), q), lhs, rows(vw("LB", 0, 49), q))
-            mm(rows(vw(gb, g0 + 1, g0 + 49), q), lhs, rows(vw("LB", 49, 97), q))
-        if b == 0:
-            mm(vw("GB", 256, 320), ID, vw("CKA", 0, 64))
+            mm(vw("PR", 256, 320), ID, vw("CKA", 0, 64), True)
             mm(vw("UA", 0, 96), ID, vw("CKA", 64, 160), True)
         if b == 2:
             mm(vw(part(r, b, 0)[0], 128, 208), ID, vw("CKB"), True)
@@ -336,41 +389,46 @@ def trace(T, send, est):
     def name(r, b):
         oq, cs = vw("OQ", 4 * b, 4 * b + 3), vw("CS", 48 * b, 48 * b + 48)
         ts(oq, vw("UU", 68 * b + 64, 68 * b + 67), vw("R1", b, b + 1), 1.0 / 16, ALU.subtract, ALU.mult)
-        act(cs, ind(vw("CF", 64 * b, 64 * b + 64), oq), ACT.Copy)
-        tt(vw("SB", b, 144, 3), ind(vw("IDT"), vw("OO", 8 * b + 4, 8 * b + 7)), cs, ALU.mult)
-        sb = vw("SB", 96 + b, 144, 3)
-        for k, lhs in ((0, "BMB"), (1, "NBMB"), (2, "BMB"), (3, "NBMB"), (3, "BM")):
-            mm(part(r, b, k), vw(lhs), sb)
-        gb, g0 = conflict_bank(b)
-        for q in range(4):
-            mm(rows(vw(gb, g0 + 49, g0 + 99), q), rows(vw("SB", b, 96, 3), q), rows(vw("RC"), q))
-        if b < 2:
-            for u in range(b + 1):
-                mm(vw(gb, g0 + 49 + u, g0 + 97, 3), BM, vw("SB", 96 + u, 144, 3), False, u == b, pin=True)
+        if b in PLAN["csv"]:
+            ts(cs, ind(vw("CF", 64 * b, 64 * b + 64), oq), -MID, None, ALU.add)
         else:
-            mm(vw(gb, g0 + 49, g0 + 97), BM, vw("SB", 96, 144), False, True, pin=True)
+            act(cs, ind(vw("CF", 64 * b, 64 * b + 64), oq), ACT.Identity, bias=-MID)
+        t0, e0 = (0, 64) if b == 1 else (64, 48 * b)
+        tt(vw("SB", 48 * b, 48 * b + 48), ind(vw("IDT", t0, t0 + 192), vw("OO", 8 * b + 4, 8 * b + 7)), cs, ALU.mult)
+        if b:
+            sb = vw("SB", 32, 64) if b == 1 else vw("SB", 128, 144)
+            for k, lhs in ((0, "BMB"), (1, "NBMB"), (2, "BMB"), (3, "NBMB"), (3, "BM")):
+                out = part(r, b - b % 2, k)
+                mm(vw(out[0], out[1], out[1] + width(sb)), vw(lhs), sb)
+        gb, c0, c1 = conflict_bank(b)
+        for q in range(4):
+            mm(rows(gb(49, c1), q), rows(vw("SB", e0, e0 + 32), q), rows(vw("RC", 0, c1 - 49), q))
+        mm(gb(51, min(c1, 83)), BM, vw("SB", 32, min(c1, 83) - 19))
+        if b == 2:
+            mm(gb(83, 99), BM, vw("SB", 128, 144))
+
+    def meet(r, b):
+        gb, c0, c1 = conflict_bank(b)
+        for q in range(4):
+            mm(rows(gb(c0, 49), q), rows(vw("LB", b, 96, 3), q), rows(vw("RH", c0, 49), q))
+        for k in range(2):
+            mm(gb(c0, 48), vw("WR"), vw("LB", 48 * k, 48 * k + 48, 1 if b else 3), False, k == 1 and b > 0, pin=True)
 
     def stand(r, b):
-        gb, g0 = conflict_bank(b)
-        z, fo, both, tc = vw("ZZ", b, b + 1), vw("FO", b, b + 9, 8), vw(gb, g0, g0 + 99, 98), vw("TC", b, b + 1)
-        if b >= PLAN["countv"]:
-            red(z, vw(gb, g0 + 1, g0 + 98), ALU.min, True)
-            if b == 2:
-                cp(vw("HU", 0, 1), vw(gb, 0, 1))
-            ts(fo, both, z, tc, ALU.mult, ALU.max)
-        else:
-            ad = vw("AD", 96 * b, 96 * b + 96)
-            act(ad, vw(gb, g0 + 1, g0 + 97), ACT.Abs)
-            act(ad, ad, ACT.Relu, bias=2 * B, scale=-2 * B, acc=z)
-            ts(fo, both, z, tc, ALU.subtract, ALU.max)
+        gb, c0, c1 = conflict_bank(b)
+        z, tc = vw("ZZ", b, b + 1), vw("TC", b, b + 1)
+        red(z, gb(c0, c1), ALU.min, True)
+        if b == 2:
+            ts(vw("HU", 0, 1), gb(48, 49), tc, None, ALU.add)
+        ts(vw("FO", b, b + 9, 8), gb(48, 50), z, tc, ALU.mult, ALU.add)
 
     def place(r, b):
         last = r == RO - 1
         if b == 0:
             if PLAN["roundv"]:
-                ts(vw("RC2"), vw("GB", 256, 320), C16B, C16B, ALU.add, ALU.subtract)
+                ts(vw("RC2"), vw("PR", 256, 320), C16B, C16B, ALU.add, ALU.subtract)
             else:
-                act(vw("RA"), vw("GB", 256, 320), ACT.Identity, bias=C16B)
+                act(vw("RA"), vw("PR", 256, 320), ACT.Identity, bias=C16B)
                 act(vw("RC2"), vw("RA"), ACT.Identity, bias=-C16B)
             mm(vw("UA", 0, 64), vw("NID"), vw("RC2"))
             act(vw("UL", 0, 64 if last else 96), vw("UA", 0, 64 if last else 96), ACT.Copy)
@@ -395,17 +453,20 @@ def trace(T, send, est):
             cur[:] = [step + str(b), r]
             if step == "cu" and r > 0:
                 cp(vw("CU", 64 * b, 64 * b + 64), ind(vw("BF"), slot("LD", r - 1, b, 16, 20)))
-                ts(vw("CF", 64 * b, 64 * b + 64), vw("CU", 64 * b, 64 * b + 64), -MID, None, ALU.add)
+                if PLAN["gcf"]:
+                    sel(vw("CF", 64 * b, 64 * b + 64), vw("CU", 64 * b, 64 * b + 64), [[0, 64]], ALU.is_ge, 0, 0)
+                else:
+                    cp(vw("CF", 64 * b, 64 * b + 64), vw("CU", 64 * b, 64 * b + 64))
             elif step == "next" and r < RO - 1:
                 recv(r + 1, b)
-            elif step in ("recv", "search", "winner", "move", "name", "stand", "update", "place"):
-                {"recv": recv, "place": place, "search": search, "winner": winner, "move": move, "name": name, "stand": stand, "update": update}[step](r, b)
-    add("s", lambda q: q.sync.dma_start(T.yb[:], ap(vw("BF", PAD))), [], [vw("BF", PAD)], 60, "o_yb", 4500)
-    add("a", lambda q: q.scalar.dma_start(T.ys[:], ap(vw("SLF"))), [], [vw("SLF")], 60, "o_ys", 2000)
+            elif step in ("recv", "search", "winner", "move", "name", "stand", "update", "place", "copy", "vary", "proj", "bits", "meet"):
+                {"recv": recv, "meet": meet, "place": place, "proj": proj, "bits": bits, "copy": copy, "vary": vary, "search": search, "winner": winner, "move": move, "name": name, "stand": stand, "update": update}[step](r, b)
+    add("s", lambda q: q.sync.dma_start(T.yb[:], ap(vw("BF", PAD))), [], [vw("BF", PAD)], 60, "o_yb", est["yb"])
+    add("a", lambda q: q.scalar.dma_start(T.ys[:], ap(vw("SLF"))), [], [vw("SLF")], 60, "o_ys", est["ys"])
     return ops
 
 
-def edges(ops):
+def edges(ops, loads=False):
     seen, reach, bits = {}, [], {}
 
     def cols(v):
@@ -428,6 +489,8 @@ def edges(ops):
         for vs, writes in ((o["rd"], False), (o["wr"], True)):
             for v in vs:
                 seen.setdefault(v[0], []).append((i, cols(v), writes))
+        if loads and 0 < i < 5:
+            dep.add(i - 1)
         cover = 0
         for j in dep:
             cover |= reach[j]
@@ -471,13 +534,13 @@ def times(order, eng, fig, p0=0, old=None):
     return end[mi] + lat[mi], mi, why, end
 
 
-def greedy(eng, cost, pred, prio, slack, at):
+def greedy(eng, cost, pred, prio, slack):
     n = len(eng)
     left, succ = [len(p) for p in pred], [[] for i in range(n)]
     for i in range(n):
         for j, gap in pred[i]:
             succ[j].append((i, gap))
-    at, end, free = list(at), [0.0] * n, dict.fromkeys("tvags", 0.0)
+    at, end, free = [0.0] * n, [0.0] * n, dict.fromkeys("tvags", 0.0)
     ready, order = [i for i in range(n) if left[i] == 0], []
     while ready:
         first = min(ready, key=lambda i: (max(at[i], free[eng[i]]), -prio[i], i))
@@ -492,17 +555,17 @@ def greedy(eng, cost, pred, prio, slack, at):
             left[k] -= 1
             if left[k] == 0:
                 ready.append(k)
-    return order, end
+    return order
 
 
 def plan(T):
     ops = trace(T, None, EST[0])
-    reach, n, eng = edges(ops), len(ops), [o["eng"] for o in ops]
+    reach, n, eng = edges(ops, True), len(ops), [o["eng"] for o in ops]
     figs = []
     for est in EST:
         alt = trace(T, None, est)
         figs.append(([o["cost"] for o in alt], [o["lat"] for o in alt],
-                     [[(j, 0.0 if eng[j] == "t" and eng[i] == "t" else alt[j]["lat"] + est["hop"]) for j in ops[i]["near"]] for i in range(n)]))
+                     [[(j, 0.0 if eng[j] == eng[i] and (eng[i] == "t" or i < 5) else alt[j]["lat"] + est["hop"]) for j in ops[i]["near"]] for i in range(n)]))
 
     def full(o, p0=0, old=None):
         res = [times(o, eng, f, p0, old and old[k]) for k, f in enumerate(figs)]
@@ -513,29 +576,27 @@ def plan(T):
     for i, o in enumerate(ops):
         if o["eng"] in "va" and o["wr"] and o["cls"] != "setup":
             named.setdefault((o["round"], o["wr"][0][0] + o["cls"][-1]), []).append(i)
-    for e in "va":
+        elif o["eng"] == "t":
+            named.setdefault((o["round"], o["wr"][0][0][0] + o["cls"]), []).append(i)
+    made = [[i for i, o in enumerate(ops) if o["eng"] == "g" and o["wr"][0][0] == name][0] for name in PLAN["g"].split()]
+    for u, v in zip(made, made[1:]):
+        pred[v].append((u, 0.0))
+    for e in "vat":
         chain = []
         for r in range(RO):
-            for word in PLAN[e].split():
+            for word in PLAN.get(e + str(r), PLAN[e]).split():
                 name, dot, span = word.partition(".")
                 a, dash, b = span.partition("-")
                 chain += [i for i in named.get((r, name), [])[int(a or 0):int(b or a or 0) + 1] if eng[i] == e]
         for u, v in zip(chain, chain[1:]):
             pred[v].append((u, 0.0))
-    back = [[] for i in range(n)]
-    for i in range(n):
+    tail = [cost[i] + lat[i] for i in range(n)]
+    for i in reversed(greedy(eng, cost, pred, [0.0] * n, 0.0)):
         for j, gap in pred[i]:
-            back[j].append((i, gap))
-    start = [0.0 if back[i] else lat[i] for i in range(n)]
-    best = None
-    for slack in PLAN["slacks"]:
-        prio = greedy(eng, cost, back, [0.0] * n, slack, start)[1]
-        for it in range(PLAN["passes"]):
-            order, end = greedy(eng, cost, pred, prio, slack, [0.0] * n)
-            score = full(order)[0]
-            if best is None or score < best[0]:
-                best = (score, order)
-            prio = greedy(eng, cost, back, end, slack, start)[1]
+            tail[j] = max(tail[j], cost[j] + gap + tail[i])
+    first = min(i for i, o in enumerate(ops) if o["wr"] and o["wr"][0][0] == "CU")
+    tail = [tail[i] + 2000.0 * (i == first or reach[first] >> i & 1) for i in range(n)]
+    best = min((full(o)[0], o) for o in [greedy(eng, cost, pred, tail, slack) for slack in PLAN["slacks"]])
     state = [PLAN["seed"]]
 
     def rnd(k):
@@ -602,10 +663,7 @@ def engines_for(topo, cores, src, r, b):
     for k in range(1, len(cores)):
         es = topo.engines(cores[src], cores[(src + k) % len(cores)])
         common = es if common is None else [e for e in common if e in es]
-    h = len(common) // 2
-    if r == 0 and b < 2:
-        return common[h * b:h * b + h]
-    return common
+    return common[b::2] if r == 0 and b < 2 else common
 
 
 def rank_program(g, core, T, topo):
@@ -626,7 +684,6 @@ def rank_program(g, core, T, topo):
     if "order" not in PLANNED:
         PLANNED["order"], PLANNED["times"] = plan(T)
     order, end = PLANNED["order"], PLANNED["times"][0][3]
-    order = list(range(5)) + [i for i in order if i >= 5]
     ops = trace(T, send, EST[0])
     edges(ops)
     close_groups(ops, order)

import math
from concourse.mybir import AluOpType, AxisListType, ActivationFunctionType

ALU, ACT = AluOpType, ActivationFunctionType
V, KB, S, RO = 3072, 1024, 48, 3
PAD = 64
MID = 1536.0
B = 4096.0
C16B = 1.5 * 2.0 ** 39
C256 = 1.5 * 2.0 ** 31
PARTS = {0: (0, 1, 2, 3, 4), 2: (0, 1, 3, 4, 2)}
SLOT = 24

PLAN = {
    "chunks": "a2v2a3v3v3v3 a6v5v2v3 a2a4v5v2v3",
    "steps": [("recv", 0), ("cu", 0), ("search", 0), ("recv", 1), ("cu", 1), ("search", 1), ("winner", 0), ("proj", 0), ("recv", 2),
              ("cu", 2), ("search", 2), ("winner", 1), ("proj", 1), ("bits", 0), ("bits", 1), ("move", 0), ("name", 0), ("meet", 0),
              ("move", 1), ("name", 1), ("meet", 1), ("place", 0), ("stand", 0), ("stand", 1), ("update", 0), ("winner", 2), ("proj", 2),
              ("bits", 2), ("move", 2), ("name", 2), ("meet", 2), ("place", 2), ("stand", 2), ("update", 2)],
    "gst": False, "gcf": True, "soa": (), "foa": (), "csv": (0, 1), "maxv": (), "lastv": (2,), "countv": 0, "roundv": True, "joint": False,
    "v": "CU0 ST0 XG0.1 XG0.3-5 CU1 ST1 XG1.1 R10 UU0 XG1.2 OO0 XG1.3 GG0 CU2 GE0 ST2 OQ0 XG2.2 R11 UU1 XG2.3 OO1 OQ1 SO0 XG2.4 GG1 "
         "GE1 CS0 CS1 SB0 SB1 R12 UU2 OO2 OQ2 SO1 RC20 GG2 YY2 GE2 ZZ0 ZZ1 YW2 SB2 FO0 FO1 SOF2 GO0 NX0 RB2 BF0 UL2 HU2 ZZ2 SO2 GO2 FO2 "
         "BF2 NX2",
    "a": "XG0.0 XG0.2 AB0.0-15 SC0 XG1.0 AB1.6-10 AB1.0-5 AB1.11-15 XG2.0 SC1 BS0 SOF0 XG2.1 AB2.0-1 AB2.6-10 AB2.2-5 AB2.11-15 "
         "SC2 BS1 SOF1 LB1.0-1 LB0.0-1 CS2 UL0 LB2.0-1 BS2 SOF2",
    "chunks0": "a3v2a3v3v3v2 a7v4v2v3 a2a4v4v2v2v2", "maxv0": (8, 9, 10, 11),
    "v0": "XG0.1 XG0.3-5 AB0.8-11 XG1.1 R10 UU0 XG1.2 OO0 XG1.3 GE0 GG0 XG2.3 XG2.2 R11 UU1 OQ0 SO0 OO1 OQ1 CS0 GE1 GG1 XG2.4-5 CS1 "
          "SB0 SB1 SO1 R12 UU2 OO2 OQ2 RC20 GG2 ZZ0 GE2 ZZ1 SB2 FO0 FO1 GO0 NX0 RB2 BF0 UL2 ZZ2 HU2 SO2 FO2 GO2 BF2 NX2",
    "a0": "SC0 XG0.0 XG0.2 AB0.0-7 AB0.12-15 XG1.0 AB1.7-10 AB1.0-6 AB1.11-15 SC1 BS0 XG2.0-1 AB2.10-11 AB2.0-1 AB2.6-9 AB2.2-5 SC2 "
          "BS1 AB2.12-15 LB0.0-1 LB1.0-1 CS2 UL0 LB2.0-1 BS2",
    "v2": "CU0 ST0 XG0.1 XG0.3-5 CU1 ST1 XG1.1 R10 UU0 XG1.2 OO0 XG1.3 GG0 GE0 CU2 ST2 OQ0 XG2.2 R11 UU1 XG2.3 OO1 OQ1 XG2.4 GG1 CS0 "
          "CS1 GE1 SB0 SB1 R12 UU2 OO2 OQ2 YY2 GG2 RC20 YW2 ZZ0 SB2 ZZ1 SOF2 FO0 FO1 GO0 RB2 BF0 UL2 HU2 ZZ2 GO2 FO2 BF2",
    "a2": "XG0.0 XG0.2 AB0.0-15 SC0 XG1.0 AB1.6-10 AB1.0-5 AB1.11-15 SC1 XG2.0-1 SOF0 AB2.0-1 AB2.6-10 AB2.2-5 AB2.11-15 SC2 "
          "LB1.0-1 LB0.0-1 SOF1 CS2 UL0 LB2.0-1",
    "t": "Pproj2.0-2 Pwinner2.1-2 Swinner2.1-2 Kmove2.1-3 Kname2.0-4 Gname2.0-5 Gmeet2.0-5 Swinner2.3-6",
    "g": "PI J16 JG JR JP ORD CKS BF CF",
    "slacks": (0.0, 15.0, 40.0, 60.0), "moves": 70000, "heat": 8.0, "seed": 3,
}
_E = {"cyc": 0.87, "pe": 0.44, "hop": 190.0, "gather": 1.56, "scatter": 3.8, "remote": 3200.0, "first": 500.0, "nx": 6500, "bk": 3000, "short": 1500,
      "yb": 4500, "ys": 2300, "weight": 1}
EST = [dict(_E, nx=3550, bk=2400, short=1400, pe=0.47, remote=3300.0, first=700.0, weight=2),
       dict(_E, cyc=1.15, pe=0.62, gather=1.8, scatter=5.0, hop=210.0, remote=3800.0, first=1500.0, nx=3800, short=1800),
       dict(_E, hop=170.0, remote=3900.0, first=1300.0, nx=3600, short=1600)]

SCRATCH = {}
for _names, _cols, _dt in (
        ("NX", PAD + V, "bfloat16"), ("BI", KB, "int32"), ("BF", PAD + KB, "float32"), ("ST", RO * S, "bfloat16"),
        ("SO LD", (RO - 1) * 3 * SLOT, "uint16"), ("SOF SLF YY YW", S, "float32"), ("PA I16", 16, "bfloat16"), ("THR", 128, "int32"), ("THF", 128, "float32"),
        ("AC GC", 1, "float32"), ("WC EV OCT", 4, "float32"), ("XG AB", V, "bfloat16"),
        ("ONE JG JP BM ID NID NID256 AM NAM NAM256 BMB NBMB", 128, "bfloat16"), ("GM0 GM NN OC ZZ TC", 8, "float32"),
        ("W4", 140, "bfloat16"), ("AM2", 32, "bfloat16"), ("ZA NZA", 144, "bfloat16"), ("PI PJ", 1, "int32"), ("J16", 64, "float32"), ("JR", 12, "float32"),
        ("PW ZER PWM", 16, "float32"), ("TWO", 17, "float32"), ("SG", 2, "float32"), ("CKS BS GE", S, "bfloat16"),
        ("IDT", 256, "bfloat16"), ("ORD", 99, "float32"), ("RH", 49, "bfloat16"), ("WR", 128, "bfloat16"), ("DL", 67, "float32"), ("MK", 297, "float16"), ("CKA", 160, "bfloat16"), ("CKB", 80, "bfloat16"),
        ("RC", 50, "bfloat16"), ("LB", 96, "bfloat16"), ("SB GG", 144, "float16"), ("KK", 32, "float32"),
        ("OF", 12, "uint16"), ("CU", 192, "uint16"), ("CF SC", 192, "float32"), ("CS", 144, "float32"),
        ("R1", 3, "float32"), ("UU", 3 * 68, "float32"), ("OO", 24, "uint16"), ("OQ FO", 16, "uint16"), ("HU", 2, "uint16"),
        ("RA", 64, "float32"), ("RC2", 64, "bfloat16"), ("UL", 144, "float32"), ("AD", 192, "float32"), ("RB GO", S, "float32")):
    for _n in _names.split():
        SCRATCH[_n] = ("sbuf", [128, _cols], _dt)
for _n in "K0 K1 PR SD PS GA GB UA".split():
    SCRATCH[_n] = ("psum", [128, 512], "float32")
SEMAPHORES = (["e_t", "e_v", "e_a", "e_g", "sent", "l_pa", "l_th", "l_s", "l_nx", "l_bk", "o_ys", "o_yb"]
              + ["arr%d" % i for i in range(RO * 3)])


def vw(name, c0=0, c1=None, step=1):
    return (name, c0, SCRATCH[name][1][1] if c1 is None else c1, step, 0, 128)


def rows(v, q):
    return v[:4] + (32 * q, 32 * q + 32)


def width(v):
    return (v[2] - v[1] + v[3] - 1) // v[3]


def trace(T, send, est):
    ops, cur, cyc, groups = [], ["setup", 0], est["cyc"], {}

    def ap(v):
        if v[0] == "ind":
            return ap(v[1]).indirect(ap(v[2]))
        return T[v[0]][v[4]:v[5], v[1]:v[2]:v[3]] if v[3] != 1 else T[v[0]][v[4]:v[5], v[1]:v[2]]

    def sc(x):
        return ap(x) if isinstance(x, tuple) else x

    def add(eng, fn, out, ins, cost, sem=None, lat=0.0):
        rd, wr = [], []
        for v in ins:
            if isinstance(v, tuple):
                rd.extend([v[1], v[2]] if v[0] == "ind" else [v])
        for v in out:
            if v[0] == "ind":
                wr.append(v[1]); rd.append(v[2])
            else:
                wr.append(v)
        ops.append({"eng": eng, "fn": fn, "rd": rd, "wr": wr, "cost": cost, "sem": sem, "lat": lat, "cls": cur[0], "round": cur[1]})

    def ind(win, off):
        return ("ind", win, off)

    def vcost(out, a, per=None):
        if out[0] == "ind":
            return (60 + 16 * width(out[2]) * est["scatter"]) * cyc
        if a[0] == "ind":
            return (60 + 16 * width(a[2]) * est["gather"]) * cyc
        if per is None:
            per = 0.5 if all(SCRATCH[v[0]][2] in ("bfloat16", "float16", "uint16") for v in (out, a)) else 1.0
        return max(64, width(a) * per) * cyc

    def ts(out, a, s1, s2, op0, op1=None):
        if op1 is None:
            fn = lambda q: q.vector.tensor_scalar(ap(out), ap(a), sc(s1), None, op0)
        else:
            fn = lambda q: q.vector.tensor_scalar(ap(out), ap(a), sc(s1), sc(s2), op0, op1)
        add("v", fn, [out], [a, s1, s2], vcost(out, a))

    def tt(out, a, b, op):
        per = 1.0 if a[0] != "ind" and SCRATCH[a[0]][0] == "psum" else 2.0
        add("v", lambda q: q.vector.tensor_tensor(ap(out), ap(a), ap(b), op), [out], [a, b], vcost(out, a, per))

    def cp(out, a):
        add("v", lambda q: q.vector.tensor_copy(ap(out), ap(a)), [out], [a], vcost(out, a))

    def ms(out, val):
        add("v", lambda q: q.vector.memset(ap(out), val), [out], [], vcost(out, out))

    def red(out, a, op, absolute=False):
        if absolute:
            fn = lambda q: q.vector.tensor_reduce(ap(out), ap(a), AxisListType.X, op, apply_absolute_value=True)
        else:
            fn = lambda q: q.vector.tensor_reduce(ap(out), ap(a), AxisListType.X, op)
        add("v", fn, [out], [a], vcost(out, a, 1.0))

    def scan(out, d0, d1, init, op0, op1):
        add("v", lambda q: q.vector.tensor_tensor_scan(ap(out), ap(d0), ap(d1), init, op0, op1), [out], [d0, d1], vcost(out, d0, 1.0))

    def act(out, a, func, bias=0.0, scale=1.0, acc=None):
        if acc is None:
            fn = lambda q: q.scalar.activation(ap(out), ap(a), func, bias=sc(bias), scale=sc(scale))
        else:
            fn = lambda q: q.scalar.activation(ap(out), ap(a), func, bias=sc(bias), scale=sc(scale), accum_out=ap(acc))
        cost = (78 + 16 * width(a[2]) * est["gather"] if a[0] == "ind" else max(66, width(a))) * cyc
        add("a", fn, [out] + ([acc] if acc else []), [a, bias, scale], cost + (20 if acc else 0))

    def mm(out, lhs, rhs, start=False, stop=False, pin=False, alone=False):
        ends = [start, stop]
        add("t", lambda q: q.tensor.matmul(ap(out), ap(lhs), ap(rhs), ends[0], ends[1]), [out], [lhs, rhs],
            max(min(64, width(lhs)), width(rhs)) * est["pe"])
        groups[out[0]] = groups.get(out[0], 0) + start
        ops[-1].update(group=(out[0], groups[out[0]]), ends=ends, first=pin and start, last=pin and stop, wide=rhs[0][:2] in ("CK", "MK"))

    def bank(terms, start=True, stop=True):
        for i, (out, lhs, rhs) in enumerate(terms):
            mm(out, lhs, rhs, start and i == 0, stop and i == len(terms) - 1)

    def iota(out, pattern, base, mult, small=True):
        if small:
            fn = lambda q: q.iota(ap(out), pattern, base, mult, allow_small_or_imprecise_dtypes=True)
        else:
            fn = lambda q: q.iota(ap(out), pattern, base, mult)
        add("g", fn, [out], [], 160 + 2 * width(out) * cyc)

    def sel(out, a, pattern, cmp, base, mult):
        add("g", lambda q: q.affine_select(ap(out), ap(a), pattern, cmp, 0.0, base, mult), [out], [a], 210 + 2 * width(out) * cyc)

    add("s", lambda q: q.sync.dma_start(ap(vw("PA")), T.pa[:]), [vw("PA")], [], 60, "l_pa", est["short"])
    thr, thf = ("THR", 0, 128, 1, 0, 1), ("THF", 0, 128, 1, 0, 1)
    add("s", lambda q: q.sync.dma_start(ap(thr), T.th[:]), [thr], [], 60, "l_th", est["short"])
    add("s", lambda q: q.sync.dma_start(ap(vw("ST", 0, S)), T.s0[:]), [vw("ST", 0, S)], [], 60, "l_s", est["short"])
    add("s", lambda q: q.sync.dma_start(ap(vw("BI")), T.bk[:]), [vw("BI")], [], 60, "l_bk", est["bk"])
    add("s", lambda q: q.sync.dma_start(ap(vw("NX", PAD)), T.nx[:]), [vw("NX", PAD)], [], 60, "l_nx", est["nx"])

    ID, BM, AM, AC = vw("ID"), vw("BM"), vw("AM"), vw("AC")
    ms(vw("ONE"), 1.0)
    iota(vw("PI"), [[0, 1]], 0, 1, small=False)
    iota(vw("J16"), [[0, 4], [1, 16]], 0, 0)
    iota(vw("JG"), [[16, 8], [0, 16]], 0, 0)
    iota(vw("JP"), [[-1, 128]], 0, 1)
    iota(vw("JR"), [[16, 12]], 0, 0)
    iota(vw("ORD", 0, 48), [[1, 16], [16, 3]], 0, 0)
    iota(vw("ORD", 48, 99), [[1, 51]], -3, 0)
    iota(vw("CKS", 0, 32), [[-24, 2], [0, 16]], 12, 0)
    iota(vw("CKS", 32, 48), [[0, 16]], 256, 0)
    ts(vw("PJ"), vw("PI"), 15, None, ALU.bitwise_and)
    cp(AC, vw("PJ"))
    ts(vw("GC"), vw("PI"), AC, None, ALU.subtract)
    ts(vw("GM"), vw("JG", 0, 128, 16), vw("GC"), None, ALU.is_equal)
    for name, f in (("BM", 1.0), ("BMB", B), ("NBMB", -B)):
        ts(vw(name), vw("JG"), vw("GC"), f, ALU.is_equal, ALU.mult)
    for name, f in (("ID", 1.0), ("NID", -1.0), ("NID256", -256.0)):
        ts(vw(name), vw("JP"), 0.0, f, ALU.is_equal, ALU.mult)
    ts(vw("IDT", 0, 64), vw("J16"), AC, None, ALU.is_equal)
    i16 = vw("IDT", 0, 16)
    ms(vw("TWO", 0, 16), 2.0); ms(vw("ZER"), 0.0)
    scan(vw("PW"), vw("TWO", 0, 16), vw("ZER"), 0.25, ALU.mult, ALU.add)
    ms(vw("PW", 10, 11), -(512.0 + PAD)); ms(vw("PW", 11, 12), 0.5); ms(vw("PW", 12, 16), 0.0)
    tt(vw("PWM"), vw("PW"), i16, ALU.mult)
    red(vw("WC", 0, 1), vw("PWM"), ALU.add)
    ts(vw("SG"), vw("IDT", 0, 2), -2.0, 1.0, ALU.mult, ALU.add)
    ts(vw("WC", 1, 3), vw("SG"), vw("WC", 0, 1), None, ALU.mult)
    ts(vw("WC", 3, 4), vw("WC", 1, 2), vw("SG", 1, 2), None, ALU.mult)
    ms(vw("W4"), 0.0)
    for gg in range(8):
        act(vw("AM", 16 * gg, 16 * gg + 16), vw("PA"), ACT.Copy, scale=vw("GM", gg, gg + 1))
    nth = vw("NN", 1, 2)
    one, tht = ("TWO", 16, 17, 1, 0, 1), vw("PS", 0, 1)
    ms(one, 1.0)
    cp(thf, thr)
    add("t", lambda q: q.tensor.transpose(ap(tht), ap(thf), ap(one)), [tht], [thf, one], 256 * est["pe"])
    ops[-1].update(group=("PS", 0), ends=[True, True], first=False, last=False, wide=False)
    ts(nth, tht, -1.0, -0.5, ALU.mult, ALU.add)
    for k in range(4):
        if k % 2:
            act(vw("W4", 12 + k, 140, 16), vw("GM"), ACT.Copy, scale=vw("WC", k, k + 1))
        else:
            ts(vw("W4", 12 + k, 140, 16), vw("GM"), vw("WC", k, k + 1), None, ALU.mult)
    ms(vw("ZA"), 0.0)
    act(vw("ZA", 15, 143, 16), vw("GM"), ACT.Copy, scale=64.0)
    act(vw("NZA"), vw("ZA"), ACT.Copy, scale=-1.0)
    red(vw("EV", 0, 1), vw("GM", 0, 8, 2), ALU.add)
    red(vw("EV", 1, 2), vw("GM", 1, 8, 2), ALU.add)
    for name, f in (("NAM", -1.0), ("NAM256", -256.0)):
        act(vw(name), AM, ACT.Copy, scale=f)
    for k in range(2):
        act(vw("IDT", 64 * k + 64, 64 * k + 128), vw("IDT", 0, 64), ACT.Copy, scale=vw("EV", k, k + 1))
    act(vw("IDT", 192, 256), vw("IDT", 0, 64), ACT.Copy)

    def first_hash():
        ts(vw("AM2", 0, 16), vw("PA"), vw("EV", 0, 1), None, ALU.mult)
        act(vw("AM2", 16, 32), vw("PA"), ACT.Copy, scale=vw("EV", 1, 2))
        for q in range(4):
            mm(rows(vw("PR", 0, S), q), rows(vw("AM2"), q), rows(vw("ST", 0, S), q), True, True, alone=True)
        act(vw("BS"), vw("PR", 0, S), ACT.Sign, bias=nth)
        bank([(vw("SD", 0, 12), vw("W4", 12 - 4 * aa, 140 - 4 * aa), vw("BS", aa, S, 4)) for aa in range(4)])
        ts(vw("OF"), vw("SD", 0, 12), -float(PAD), None, ALU.add)
        cp(vw("CU", 0, 64), ind(vw("BI"), vw("OF", 0, 4)))
        cp(vw("CU", 64, 192), ind(vw("BI"), vw("OF", 4, 12)))
        sel(vw("CF"), vw("CU"), [[0, 192]], ALU.is_ge, 0, 0)

    first_hash()
    sel(vw("BF", PAD), vw("BI"), [[0, KB]], ALU.is_ge, 0, 0)
    bank([(vw("UA", 0, 1), AM, vw("ONE", 0, 1))])
    ts(vw("NN", 0, 1), vw("UA", 0, 1), -12.0, nth, ALU.mult, ALU.add)
    act(vw("EV", 2, 4), vw("EV", 0, 2), ACT.Copy, scale=vw("NN", 0, 1))
    ms(vw("DL", 0, 64), -1.0); ms(vw("DL", 65, 67), 0.0)
    ts(vw("DL", 64, 65), AC, 64.0, 55.5, ALU.mult, ALU.add)
    ts(vw("OC", 0, 4), vw("ONE", 0, 4), vw("DL", 64, 65), 7.5, ALU.mult, ALU.add)
    act(vw("OC", 4, 7), vw("JR", 0, 12, 4), ACT.Identity, bias=63.0)
    ms(vw("K0", 64, 67), 2.0 ** 20); ms(vw("K1", 64, 67), 2.0 ** 20)
    act(vw("TC", 0, 3), vw("JR", 0, 3), ACT.Identity, bias=AC)
    ts(vw("MK", 32, 48), vw("ORD", 51, 67), vw("TC", 0, 1), B, ALU.is_ge, ALU.mult)
    for b, c0 in enumerate((51, 0, 0)):
        ts(vw("MK", 99 * b + c0, 99 * b + 67 + 16 * b), vw("ORD", c0, 67 + 16 * b), vw("TC", b, b + 1), B, ALU.is_ge, ALU.mult)
    ts(vw("MK", 48, 297, 99), vw("TC", 0, 3), -1.0, None, ALU.mult)
    ts(vw("MK", 49, 297, 99), vw("TC", 0, 3), -1.0, MID + PAD, ALU.mult, ALU.add)
    ms(vw("MK", 50, 297, 99), 1.0)
    ms(vw("RC", 2, 50), -1.0)
    act(vw("RC", 0, 2), vw("J16", 0, 2), ACT.Identity, bias=1.0, scale=-1.0)
    act(vw("WR"), BM, ACT.Copy, scale=vw("WC", 0, 1))
    ts(vw("RH", 0, 48), vw("ONE", 0, 48), vw("WC", 0, 1), -1.0, ALU.mult, ALU.mult)
    act(vw("RH", 48, 49), vw("WC", 0, 1), ACT.Copy)
    ts(vw("KK"), vw("J16", 0, 32), AC, None, ALU.subtract)
    for name, w, places in (("CKA", 32, PARTS[0]), ("CKB", 16, PARTS[2])):
        for k, (f, c) in zip(places, ((B, -7.5 * B), (-B, 7.5 * B), (B, 0.0), (-B, MID), (0.0, -12.0))):
            act(vw(name, k * w, k * w + w), vw("KK", 0, w), ACT.Identity, bias=c, scale=f)
    ms(vw("LB"), 0.0)
    ms(vw("RB", 0, 16), 0.0)
    for b in range(3):
        act(vw("SC", 64 * b, 64 * b + 16), vw("ZER"), ACT.Copy)
    ms(vw("BF", 0, PAD), 0.0)

    def state(r, b):
        return vw("ST", S * r + 16 * b, S * r + 16 * b + 16)

    def slot(name, r, b, c0, c1):
        return vw(name, SLOT * (3 * r + b) + c0, SLOT * (3 * r + b) + c1)

    def recv(r, b):
        copy(r, b)
        vary(r, b)

    def copy(r, b):
        s = state(r, b)
        if r > 0:
            if PLAN["gst"]:
                sel(s, slot("LD", r - 1, b, 0, 16), [[0, 16]], ALU.is_ge, 0, 0)
            else:
                cp(s, slot("LD", r - 1, b, 0, 16))

    def vary(r, b):
        s = state(r, b)
        bank([(vw("GA", 0, 48), ID, vw("CKS")), (vw("GA", 0, 16), ID, s), (vw("GA", 16, 32), ID, s), (vw("GA", 32, 48), vw("NID"), s)])
        act(vw("SC", 64 * b + 16, 64 * b + 64), vw("GA", 0, 48), ACT.Copy)

    def search(r, b):
        key = vw("K%d" % ((3 * r + b) % 2), 0, 64)
        spec, a0 = PLAN.get("chunks" + str(r), PLAN["chunks"]).split()[b], 0
        for eng, n in zip(spec[0::2], map(int, spec[1::2])):
            t0 = 16 * b + a0
            src = ind(vw("NX", PAD), vw("CU", 4 * t0, 4 * (t0 + n)))
            if eng == "v":
                cp(vw("XG", 64 * t0, 64 * (t0 + n)), src)
            else:
                act(vw("XG", 64 * t0, 64 * (t0 + n)), src, ACT.Copy)
            for a in range(a0, a0 + n):
                t = 16 * b + a
                d = vw("AB", 64 * t, 64 * t + 64)
                x, s = vw("XG", 64 * t, 64 * t + 64), vw("ST", S * r + t, S * r + t + 1)
                if t in PLAN.get("maxv" + str(r), PLAN["maxv"]):
                    ts(d, x, s, 2.0, ALU.max, ALU.mult)
                    mm(key, vw("ZA", 15 - a, 143 - a), d, a == 0)
                    mm(key, vw("NZA", 15 - a, 143 - a), x)
                else:
                    act(d, x, ACT.Abs, bias=s, scale=-1.0)
                    mm(key, vw("ZA", 15 - a, 143 - a), d, a == 0)
            a0 += n

    def conflict_bank(b):
        return (lambda a, c: vw("GA" if b == 2 else "GB", a + 128 * (b == 0), c + 128 * (b == 0))), 0 if b else 32, 67 + 16 * b

    def part(r, b, k):
        if b == 2:
            c0, ub = 128 + 16 * PARTS[2][k], "K%d" % ((r + 1) % 2)
        else:
            c0, ub = (256 + 32 * k + 16 * b, "PR") if k < 2 else (32 * (k - 2) + 16 * b, "UA")
        return vw(ub, c0, c0 + 16)

    def winner(r, b):
        last, kb = r == RO - 1, "K%d" % ((3 * r + b) % 2)
        s, r1, u = state(r, b), vw("R1", b, b + 1), 68 * b
        red(r1, vw(kb, 0, 64), ALU.min)
        scan(vw("UU", u, u + 67), vw("DL"), vw(kb, 0, 67), 2.0 ** 21, ALU.add, ALU.min)
        ts(vw("OO", 8 * b, 8 * b + 7), vw("OC", 0, 7), vw("UU", u + 63, u + 64), r1, ALU.add, ALU.subtract)
        xg = vw("XG", 1024 * b, 1024 * b + 1024)
        tt(vw("GG", 48 * b, 48 * b + 48), ind(xg, vw("OO", 8 * b, 8 * b + 3)), vw("SC", 64 * b, 64 * b + 48), ALU.max)
        m0, m1, m2 = [vw("GG", 48 * b + 16 * k, 48 * b + 16 * k + 16) for k in range(3)]
        ge, win = vw("GE", 16 * b, 16 * b + 16), ind(xg, vw("OO", 8 * b, 8 * b + 1))
        sv, ps = vw("SD", 0, 16), vw("PS", 0, 16)
        if last and b in PLAN["lastv"]:
            so, land, yy, ww = [vw(n, 16 * b, 16 * b + 16) for n in ("SOF", "SLF", "YY", "YW")]
            tt(yy, win, s, ALU.add)
            ts(ww, yy, 256.0, -256.0, ALU.is_ge, ALU.mult)
            tt(so, yy, ww, ALU.add)
        elif last:
            tt(ge, win, vw("SC", 64 * b + 48, 64 * b + 64), ALU.is_ge)
            bank([(sv, ID, s), (sv, ID, m0), (sv, vw("NID256"), ge)])
            so, land = vw("SOF", 16 * b, 16 * b + 16), vw("SLF", 16 * b, 16 * b + 16)
            act(so, sv, ACT.Copy)
        else:
            tt(ge, win, vw("SC", 64 * b + 48, 64 * b + 64), ALU.is_ge)
            bank([(sv, ID, s), (sv, ID, m0), (sv, vw("NID256"), ge)], stop=False)
            bank([(ps, AM, s), (ps, AM, m0), (ps, vw("NAM256"), ge)])
            act(vw("BS", 16 * b, 16 * b + 16), ps, ACT.Sign, bias=nth)
            bank([(vw("SD", 16, 20), vw("W4", 12 - 4 * aa, 140 - 4 * aa), vw("BS", 16 * b + aa, 16 * b + 16, 4)) for aa in range(4)], start=False)
            so, land = slot("SO", r, b, 0, 20), slot("LD", r, b, 0, 20)
            if b in PLAN["soa"]:
                act(so, vw("SD", 0, 20), ACT.Copy)
            else:
                cp(so, vw("SD", 0, 20))
        add("g", lambda q: send(q, r, b, ap(land), ap(so)), [land], [so], 300, "arr%d" % (3 * r + b),
            est["remote"] + (est["first"] if r == 0 and b < 2 else 0.0))

    def proj(r, b):
        m0, m1, m2 = [vw("GG", 48 * b + 16 * k, 48 * b + 16 * k + 16) for k in range(3)]
        pr = vw("PR", 16 * b, 16 * b + 16)
        bank([(pr, AM, m0), (pr, AM, m1), (pr, vw("NAM"), m2)], start=b != 1)

    def bits(r, b):
        pr = vw("PR", 16 * b, 16 * b + 16)
        for k in range(2):
            act(vw("LB", 48 * k + b, 48 + 48 * k, 3), pr, ACT.Sign, bias=vw("EV", 2 + k, 3 + k), scale=vw("EV", k, k + 1))

    def move(r, b):
        last = r == RO - 1
        m0, m1, m2 = [vw("GG", 48 * b + 16 * k, 48 * b + 16 * k + 16) for k in range(3)]
        gb, c0, c1 = conflict_bank(b)
        mm(gb(c0, c1), ID, vw("MK", 99 * b + c0, 99 * b + c1), b != 1, pin=True)
        if b == 0:
            mm(vw("PR", 256, 320), ID, vw("CKA", 0, 64), True)
            mm(vw("UA", 0, 96), ID, vw("CKA", 64, 160), True)
        if b == 2:
            mm(vw(part(r, b, 0)[0], 128, 208), ID, vw("CKB"), True)
        if not last:
            bank([(part(r, b, 4), ID, m0), (part(r, b, 4), ID, m1), (part(r, b, 4), vw("NID"), m2)], False, False)

    def name(r, b):
        oq, cs = vw("OQ", 4 * b, 4 * b + 3), vw("CS", 48 * b, 48 * b + 48)
        ts(oq, vw("UU", 68 * b + 64, 68 * b + 67), vw("R1", b, b + 1), 1.0 / 16, ALU.subtract, ALU.mult)
        if b in PLAN["csv"]:
            ts(cs, ind(vw("CF", 64 * b, 64 * b + 64), oq), -MID, None, ALU.add)
        else:
            act(cs, ind(vw("CF", 64 * b, 64 * b + 64), oq), ACT.Identity, bias=-MID)
        t0, e0 = (0, 64) if b == 1 else (64, 48 * b)
        tt(vw("SB", 48 * b, 48 * b + 48), ind(vw("IDT", t0, t0 + 192), vw("OO", 8 * b + 4, 8 * b + 7)), cs, ALU.mult)
        if b:
            sb = vw("SB", 32, 64) if b == 1 else vw("SB", 128, 144)
            for k, lhs in ((0, "BMB"), (1, "NBMB"), (2, "BMB"), (3, "NBMB"), (3, "BM")):
                out = part(r, b - b % 2, k)
                mm(vw(out[0], out[1], out[1] + width(sb)), vw(lhs), sb)
        gb, c0, c1 = conflict_bank(b)
        for q in range(4):
            mm(rows(gb(49, c1), q), rows(vw("SB", e0, e0 + 32), q), rows(vw("RC", 0, c1 - 49), q))
        mm(gb(51, min(c1, 83)), BM, vw("SB", 32, min(c1, 83) - 19))
        if b == 2:
            mm(gb(83, 99), BM, vw("SB", 128, 144))

    def meet(r, b):
        gb, c0, c1 = conflict_bank(b)
        for q in range(4):
            mm(rows(gb(c0, 49), q), rows(vw("LB", b, 96, 3), q), rows(vw("RH", c0, 49), q))
        for k in range(2):
            mm(gb(c0, 48), vw("WR"), vw("LB", 48 * k, 48 * k + 48, 1 if b else 3), False, k == 1 and b > 0, pin=True)

    def stand(r, b):
        gb, c0, c1 = conflict_bank(b)
        z, tc = vw("ZZ", b, b + 1), vw("TC", b, b + 1)
        red(z, gb(c0, c1), ALU.min, True)
        if b == 2:
            ts(vw("HU", 0, 1), gb(48, 49), tc, None, ALU.add)
        ts(vw("FO", b, b + 9, 8), gb(48, 50), z, tc, ALU.mult, ALU.add)

    def place(r, b):
        last = r == RO - 1
        if b == 0:
            if PLAN["roundv"]:
                ts(vw("RC2"), vw("PR", 256, 320), C16B, C16B, ALU.add, ALU.subtract)
            else:
                act(vw("RA"), vw("PR", 256, 320), ACT.Identity, bias=C16B)
                act(vw("RC2"), vw("RA"), ACT.Identity, bias=-C16B)
            mm(vw("UA", 0, 64), vw("NID"), vw("RC2"))
            act(vw("UL", 0, 64 if last else 96), vw("UA", 0, 64 if last else 96), ACT.Copy)
        else:
            ub, skip = part(r, b, 0)[0], 16 if last else 0
            ts(vw("RB", 16, 48), vw(ub, 128, 160), C16B, C16B, ALU.add, ALU.subtract)
            tt(vw("UL", 96 + skip, 144), vw(ub, 160 + skip, 208), vw("RB", skip, 48), ALU.subtract)

    def update(r, b):
        n, u = (2, 0) if b == 0 else (1, 112)
        go = vw("GO", 16 * b, 16 * (b + n))
        tt(go, ind(vw("BF"), vw("HU", 0, 1) if b == 2 else vw("FO", b, b + n)), vw("UL", u, u + 16 * n), ALU.min)
        tt(ind(vw("BF"), vw("FO", b, b + n)), go, vw("UL", u + 16 * n, u + 32 * n), ALU.max)
        if r < RO - 1:
            if not PLAN["joint"]:
                cp(ind(vw("NX"), vw("FO", 8 + b, 8 + b + n)), vw("UL", 64 + 16 * b, 64 + 16 * (b + n)))
            elif b == 2:
                cp(ind(vw("NX"), vw("FO", 8, 11)), vw("UL", 64, 112))

    for r in range(RO):
        for step, b in PLAN["steps"]:
            cur[:] = [step + str(b), r]
            if step == "cu" and r > 0:
                cp(vw("CU", 64 * b, 64 * b + 64), ind(vw("BF"), slot("LD", r - 1, b, 16, 20)))
                if PLAN["gcf"]:
                    sel(vw("CF", 64 * b, 64 * b + 64), vw("CU", 64 * b, 64 * b + 64), [[0, 64]], ALU.is_ge, 0, 0)
                else:
                    cp(vw("CF", 64 * b, 64 * b + 64), vw("CU", 64 * b, 64 * b + 64))
            elif step == "next" and r < RO - 1:
                recv(r + 1, b)
            elif step in ("recv", "search", "winner", "move", "name", "stand", "update", "place", "copy", "vary", "proj", "bits", "meet"):
                {"recv": recv, "meet": meet, "place": place, "proj": proj, "bits": bits, "copy": copy, "vary": vary, "search": search, "winner": winner, "move": move, "name": name, "stand": stand, "update": update}[step](r, b)
    add("s", lambda q: q.sync.dma_start(T.yb[:], ap(vw("BF", PAD))), [], [vw("BF", PAD)], 60, "o_yb", est["yb"])
    add("a", lambda q: q.scalar.dma_start(T.ys[:], ap(vw("SLF"))), [], [vw("SLF")], 60, "o_ys", est["ys"])
    return ops


def edges(ops, loads=False):
    seen, reach, bits = {}, [], {}

    def cols(v):
        if v[1:4] not in bits:
            bits[v[1:4]] = sum(1 << c for c in range(v[1], v[2], v[3]))
        return bits[v[1:4]]

    for i, o in enumerate(ops):
        dep = set()
        for vs, writes in ((o["rd"], False), (o["wr"], True)):
            for v in vs:
                psum = SCRATCH[v[0]][0] == "psum"
                for j, u, w in seen.get(v[0], []):
                    p = ops[j]
                    if psum and p["eng"] == "t" and o["eng"] == "t":
                        if p["group"] != o["group"] or p["first"] or o["last"] or (u & cols(v) == cols(v) != u and p["wide"]):
                            dep.add(j)
                    elif (psum and p["eng"] != o["eng"]) or ((w or writes) and u & cols(v)):
                        dep.add(j)
        for vs, writes in ((o["rd"], False), (o["wr"], True)):
            for v in vs:
                seen.setdefault(v[0], []).append((i, cols(v), writes))
        if loads and 0 < i < 5:
            dep.add(i - 1)
        cover = 0
        for j in dep:
            cover |= reach[j]
        o["dep"] = sorted(dep)
        o["near"] = [j for j in o["dep"] if not cover >> j & 1]
        for j in dep:
            cover |= 1 << j
        reach.append(cover)
    return reach


def close_groups(ops, order):
    last = {}
    for i in order:
        o = ops[i]
        if o["eng"] == "t":
            o["ends"][:] = [o["group"] not in last, False]
            last[o["group"]] = o
    for o in last.values():
        o["ends"][1] = True


def times(order, eng, fig, p0=0, old=None):
    cost, lat, gp = fig
    n = len(cost)
    why, end = (old[2][:], old[3][:]) if old else ([-1] * n, [0.0] * n)
    last = dict.fromkeys("tvags", -1)
    for i in order[max(0, p0 - 300):p0]:
        last[eng[i]] = i
    free = {e: end[i] if i >= 0 else 0.0 for e, i in last.items()}
    for i in order[p0:]:
        e = eng[i]
        t, w = free[e], last[e]
        for j, gap in gp[i]:
            gap += end[j]
            if gap > t:
                t, w = gap, j
        end[i] = free[e] = t + cost[i]
        why[i], last[e] = w, i
    mi = max(n - 2, n - 1, key=lambda i: end[i] + lat[i])
    return end[mi] + lat[mi], mi, why, end


def greedy(eng, cost, pred, prio, slack):
    n = len(eng)
    left, succ = [len(p) for p in pred], [[] for i in range(n)]
    for i in range(n):
        for j, gap in pred[i]:
            succ[j].append((i, gap))
    at, end, free = [0.0] * n, [0.0] * n, dict.fromkeys("tvags", 0.0)
    ready, order = [i for i in range(n) if left[i] == 0], []
    while ready:
        first = min(ready, key=lambda i: (max(at[i], free[eng[i]]), -prio[i], i))
        e = eng[first]
        t0 = max(at[first], free[e]) + min(slack, cost[first])
        i = max((k for k in ready if eng[k] == e and at[k] <= t0), key=lambda k: (prio[k], -k))
        ready.remove(i)
        end[i] = free[e] = max(at[i], free[e]) + cost[i]
        order.append(i)
        for k, gap in succ[i]:
            at[k] = max(at[k], end[i] + gap)
            left[k] -= 1
            if left[k] == 0:
                ready.append(k)
    return order


def plan(T):
    ops = trace(T, None, EST[0])
    reach, n, eng = edges(ops, True), len(ops), [o["eng"] for o in ops]
    figs = []
    for est in EST:
        alt = trace(T, None, est)
        figs.append(([o["cost"] for o in alt], [o["lat"] for o in alt],
                     [[(j, 0.0 if eng[j] == eng[i] and (eng[i] == "t" or i < 5) else alt[j]["lat"] + est["hop"]) for j in ops[i]["near"]] for i in range(n)]))

    def full(o, p0=0, old=None):
        res = [times(o, eng, f, p0, old and old[k]) for k, f in enumerate(figs)]
        return sum(est["weight"] * x[0] for est, x in zip(EST, res)) / sum(est["weight"] for est in EST), res

    cost, lat, gp = figs[0]
    pred, named = [list(p) for p in gp], {}
    for i, o in enumerate(ops):
        if o["eng"] in "va" and o["wr"] and o["cls"] != "setup":
            named.setdefault((o["round"], o["wr"][0][0] + o["cls"][-1]), []).append(i)
        elif o["eng"] == "t":
            named.setdefault((o["round"], o["wr"][0][0][0] + o["cls"]), []).append(i)
    made = [[i for i, o in enumerate(ops) if o["eng"] == "g" and o["wr"][0][0] == name][0] for name in PLAN["g"].split()]
    for u, v in zip(made, made[1:]):
        pred[v].append((u, 0.0))
    for e in "vat":
        chain = []
        for r in range(RO):
            for word in PLAN.get(e + str(r), PLAN[e]).split():
                name, dot, span = word.partition(".")
                a, dash, b = span.partition("-")
                chain += [i for i in named.get((r, name), [])[int(a or 0):int(b or a or 0) + 1] if eng[i] == e]
        for u, v in zip(chain, chain[1:]):
            pred[v].append((u, 0.0))
    tail = [cost[i] + lat[i] for i in range(n)]
    for i in reversed(greedy(eng, cost, pred, [0.0] * n, 0.0)):
        for j, gap in pred[i]:
            tail[j] = max(tail[j], cost[j] + gap + tail[i])
    first = min(i for i, o in enumerate(ops) if o["wr"] and o["wr"][0][0] == "CU")
    tail = [tail[i] + 2000.0 * (i == first or reach[first] >> i & 1) for i in range(n)]
    best = min((full(o)[0], o) for o in [greedy(eng, cost, pred, tail, slack) for slack in PLAN["slacks"]])
    state = [PLAN["seed"]]

    def rnd(k):
        state[0] = (state[0] * 6364136223846793005 + 1442695040888963407) % (1 << 64)
        return (state[0] >> 33) % k

    order = best[1]
    now, res = full(order)
    for it in range(PLAN["moves"]):
        m, i, why, end = res[rnd(len(figs))]
        arcs = []
        while why[i] >= 0:
            j = why[i]
            if eng[j] == eng[i] and not reach[i] >> j & 1:
                arcs.append((j, i))
            i = j
        if not arcs:
            continue
        u, v = arcs[rnd(len(arcs))]
        pu, pv, far, moved, queues = order.index(u), order.index(v), rnd(4) if rnd(2) else 0, set(), set()
        if rnd(2):
            for k in range(far):
                q = pu - 1
                while q >= 0 and eng[order[q]] != eng[v]:
                    q -= 1
                if q < 0 or reach[v] >> order[q] & 1:
                    break
                pu = q
            mid, bits = order[pu:pv], reach[v]
            for x in reversed(mid):
                if bits >> x & 1 or eng[x] in queues:
                    moved.add(x); queues.add(eng[x]); bits |= reach[x]
            if eng[v] in queues:
                continue
            new = order[:pu] + [x for x in mid if x in moved] + [v] + [x for x in mid if x not in moved] + order[pv + 1:]
        else:
            for k in range(far):
                q = pv + 1
                while q < n and eng[order[q]] != eng[u]:
                    q += 1
                if q >= n or reach[order[q]] >> u & 1:
                    break
                pv = q
            mid, bits = order[pu + 1:pv + 1], 1 << u
            for x in mid:
                if reach[x] & bits or eng[x] in queues:
                    moved.add(x); queues.add(eng[x]); bits |= 1 << x
            if eng[u] in queues:
                continue
            new = order[:pu] + [x for x in mid if x not in moved] + [u] + [x for x in mid if x in moved] + order[pv + 1:]
        score, nres = full(new, pu, res)
        if score <= now or rnd(1 << 20) / (1 << 20) < math.exp((now - score) / (PLAN["heat"] * (1 - it / PLAN["moves"]) + 1)):
            order, now, res = new, score, nres
            if now < best[0]:
                best = (now, order)
    return best[1], full(best[1])[1]


PLANNED = {}


def engines_for(topo, cores, src, r, b):
    common = None
    for k in range(1, len(cores)):
        es = topo.engines(cores[src], cores[(src + k) % len(cores)])
        common = es if common is None else [e for e in common if e in es]
    return common[b::2] if r == 0 and b < 2 else common


def rank_program(g, core, T, topo):
    rank = T.rank_of(core)
    if rank is None:
        return
    cores = list(T.cores)
    nr = len(cores)
    sent = [0]

    def send(q, r, b, land, so):
        dst = cores[(rank + 1 + b) % nr]
        rid, pid = topo.addr(dst, core)
        es = engines_for(topo, cores, rank, r, b)
        sent[0] += len(es)
        q.remote_dma(land, so, T.sem["arr%d" % (3 * r + b)], T.sem.sent, pid, rid, sum(1 << e for e in es))

    if "order" not in PLANNED:
        PLANNED["order"], PLANNED["times"] = plan(T)
    order, end = PLANNED["order"], PLANNED["times"][0][3]
    ops = trace(T, send, EST[0])
    edges(ops)
    close_groups(ops, order)
    queue = {"t": g.tensor, "v": g.vector, "a": g.scalar, "g": g, "s": g.sync}
    pos, count = {}, {e: 0 for e in queue}
    for i in order:
        count[ops[i]["eng"]] += 1
        pos[i] = count[ops[i]["eng"]]
    known, after, waits = {e: {} for e in queue}, {}, {}
    for i in order:
        o = ops[i]
        kn = known[o["eng"]]
        want = {}
        for j in o["dep"]:
            if not (ops[j]["eng"] == "t" and o["eng"] == "t"):
                key = ops[j]["sem"] or ops[j]["eng"]
                if key not in want or pos[want[key]] < pos[j]:
                    want[key] = j
        mine = []
        for j in sorted(want.values(), key=lambda j: -end[j]):
            key = ops[j]["sem"] or ops[j]["eng"]
            if kn.get(key, 0) >= pos[j]:
                continue
            mine.append(j)
            kn[key] = pos[j]
            if not (ops[j]["sem"] or "").startswith("arr"):
                for k2, v2 in after[j].items():
                    kn[k2] = max(kn.get(k2, 0), v2)
        waits[i] = mine
        after[i] = dict(kn)
    raised = set(j for i in order for j in waits[i])
    value, count = {}, {e: 0 for e in queue}
    for i in order:
        o = ops[i]
        if o["sem"] is None:
            if i in raised:
                count[o["eng"]] += 1
                value[i] = count[o["eng"]]
        elif o["sem"].startswith("arr"):
            k = int(o["sem"][3:])
            value[i] = len(engines_for(topo, cores, (rank - 1 - k % 3) % nr, k // 3, k % 3))
        else:
            value[i] = 16
    for i in order:
        o = ops[i]
        for j in waits[i]:
            queue[o["eng"]].wait_ge(T.sem[ops[j]["sem"] or "e_" + ops[j]["eng"]], value[j])
        ins = o["fn"](g)
        if o["sem"] is None:
            if i in raised:
                ins.then_inc(T.sem["e_" + o["eng"]], 1)
        elif not o["sem"].startswith("arr"):
            ins.then_inc(T.sem[o["sem"]], 16)
    g.wait_ge(T.sem.sent, sent[0])
    g.sync.wait_ge(T.sem.o_yb, 16)
    g.scalar.wait_ge(T.sem.o_ys, 16)
